import numpy as np
import ml_dtypes


def mxq(x, axis, fmt="e4m3"):
    dtype, down = {"e4m3": (ml_dtypes.float8_e4m3fn, 7), "e5m2": (ml_dtypes.float8_e5m2, 14)}[fmt]
    v = np.moveaxis(np.asarray(x, np.float32).astype(ml_dtypes.bfloat16).astype(np.float64), axis, -1)
    blocks = v.reshape(v.shape[:-1] + (-1, 32))
    amax = np.abs(blocks).max(-1, keepdims=True)
    byte = np.maximum(np.where(amax > 0, np.frexp(amax)[1] - 1 + 127, 0) - down, 1)
    scale = np.exp2(byte - 127.0)
    codes = (blocks / scale).astype(np.float32).astype(dtype).astype(np.float64)
    return np.moveaxis((codes * scale).reshape(v.shape), -1, axis)


WIDE = False


def mx_kscale(k):
    if not WIDE:
        return np.ones(k)
    levels = np.array([10, -10, 5, -5, 0])
    if k % 512:
        return np.exp2(np.random.permutation(np.resize(levels, k // 32))).repeat(32)
    a = np.empty((k // 512, 16))
    for p in range(k // 512):
        a[p, :8] = np.random.permutation(np.resize(levels, 8))
        for g in range(8):
            far = levels[np.abs(levels - a[p, g]) >= 10]
            a[p, g + 8] = far[np.random.randint(len(far))]
    return np.exp2(a.ravel()).repeat(32)


BF16 = ml_dtypes.bfloat16


def bf(x):
    return np.asarray(x, np.float32).astype(BF16)


def f64(x):
    return np.asarray(x).astype(np.float64)


E2M1 = np.array([0.0, 0.5, 1.0, 1.5, 2.0, 3.0, 4.0, 6.0, -0.0, -0.5, -1.0, -1.5, -2.0, -3.0, -4.0, -6.0])


def pack_weight(w, fmt):
    k, n = w.shape
    w = f64(bf(w)).reshape(k // 32, 32, n)
    amax = np.abs(w).max(1)
    if fmt == "e4m3":
        byte = np.frexp(amax)[1] - 1 + 127 - 7
    else:
        mant, ex = np.frexp(amax / 6.0)
        byte = np.where(mant > 0.5, ex, ex - 1) + 127
    byte = np.clip(np.where(amax > 0, byte, 1), 1, 254)
    scaled = (w * np.exp2(127.0 - byte)[:, None, :]).reshape(k, n).astype(np.float32)
    by_word = np.ascontiguousarray(scaled.reshape(k // 512, 128, 4, n).transpose(0, 1, 3, 2))
    if fmt == "e4m3":
        words = by_word.astype(ml_dtypes.float8_e4m3fn).view(np.uint8)
    else:
        c = by_word.astype(ml_dtypes.float4_e2m1fn).view(np.uint8) & 0xF
        words = c[..., 0::2] | (c[..., 1::2] << 4)
    return np.ascontiguousarray(words), np.ascontiguousarray(byte.astype(np.uint8).reshape(k // 512, 16, n))


def unpack_weight(words, scales, fmt):
    g, p, n, _ = words.shape
    if fmt == "e4m3":
        vals = np.ascontiguousarray(words).view(ml_dtypes.float8_e4m3fn).astype(np.float64)
    else:
        nib = np.empty((g, p, n, 4), np.uint8)
        nib[..., 0::2] = words & 0xF
        nib[..., 1::2] = words >> 4
        vals = E2M1[nib]
    vals = vals * np.repeat(np.exp2(scales.astype(np.float64) - 127.0), 8, axis=1)[..., None]
    return vals.transpose(0, 1, 3, 2).reshape(g * 512, n)
def pack4(w):
    words, scales = pack_weight(w, "e2m1")
    return words.reshape(words.shape[0], 128, -1), scales


def unpack4(words, scales):
    return unpack_weight(words.reshape(words.shape[0], 128, -1, 2), scales, "e2m1")


def planes(Y):
    n, m = Y.shape
    b = f64(bf(Y)).reshape(n // 32, 32, m)
    amax = np.abs(b).max(1)
    byte = np.clip(np.where(amax > 0, np.frexp(amax)[1] - 1 + 127 - 7, 1), 1, 254)
    codes = (b * np.exp2(127.0 - byte)[:, None, :]).reshape(n, m).astype(np.float32).astype(ml_dtypes.float8_e4m3fn).view(np.uint8)
    words = codes.reshape(n // 512, 128, 4, m).transpose(0, 1, 3, 2)
    return np.ascontiguousarray(words), np.ascontiguousarray(byte.astype(np.uint8).reshape(n // 512, 16, m))


M, K, F, D = 1536, 1024, 2048, 512

def setup_inputs():
    s = mx_kscale(K)
    t = mx_kscale(F)
    users = np.random.randn(M, K) / s
    W1 = 1.4 * np.random.randn(K, F) / np.sqrt(K) * s[:, None] * t
    b1 = 0.3 * np.random.randn(F) * t
    W2 = np.random.randn(F, D) / np.sqrt(F) / t[:, None]
    w1_words, w1_scales = pack4(W1)
    w2_words, w2_scales = pack4(W2)
    return {
        "users": bf(users),
        "w1_words": w1_words, "w1_scales": w1_scales,
        "b1": bf(b1),
        "w2_words": w2_words, "w2_scales": w2_scales,
        "b2": bf(0.3 * np.random.randn(D)),
        "user_free": bf(0.5 * np.random.randn(M, D)),
        "dim_weight": bf(np.exp(0.7 * np.random.randn(D))),
    }

def reference(users, w1_words, w1_scales, b1, w2_words, w2_scales, b2, user_free, dim_weight):
    W1 = unpack4(w1_words, w1_scales)
    W2 = unpack4(w2_words, w2_scales)
    pre = (mxq(f64(users), 1, "e4m3") @ W1) + f64(b1)
    h = np.maximum(pre, 0.0)
    z = (mxq(h, 1, "e4m3") @ W2) + f64(b2)
    y = (z + f64(user_free)) * f64(dim_weight)
    Y = y.T
    words, scales = planes(Y)
    return y, words, scales

@@ -1,0 +1,405 @@
+from contextlib import ExitStack
+
+import concourse.mybir as mybir
+from concourse.masks import make_identity
+
+M, K, F, D = 1536, 1024, 2048, 512
+FLOPS = 2 * M * (K * F + F * D)
+
+F32 = mybir.dt.float32
+BF16 = mybir.dt.bfloat16
+I32 = mybir.dt.int32
+U32 = mybir.dt.uint32
+U8 = mybir.dt.uint8
+FP8X4 = mybir.dt.float8_e4m3fn_x4
+FP4X4 = mybir.dt.float4_e2m1fn_x4
+ALU = mybir.AluOpType
+ACT = mybir.ActivationFunctionType
+
+P = 128
+KG = K // 512
+FG = F // 512
+TILES = M // P
+CHUNKS = M // 512
+SLOTS = CHUNKS * FG
+MX_BANKS = 5
+T_BANKS = 3
+H_RING = 3
+
+USE_WARM = False
+PAIRED = ()
+SPLIT = {11: 2}
+
+
+def order():
+    L = []
+    a = L.append
+    def scales(name):
+        for q in range(4):
+            a((name, q))
+    def planes(j, n):
+        a(("Stc", j, n))
+        for q in range(4):
+            a(("Sts", j, n, q))
+    a(("ms1",)); a(("ident",)); a(("ms2",))
+    a(("Lu", 0)); a(("Lu", 1)); a(("Lw1", 0)); a(("Lb1",)); a(("Lu", 2)); a(("Lu", 3))
+    scales("Ls1a"); a(("Lw1", 1)); scales("Ls1b")
+    a(("Lw1", 2)); a(("Lu", 4)); a(("Lu", 5)); a(("Lw1", 3)); a(("Lb2",)); a(("Luf", 0)); a(("Lu", 6)); a(("Lu", 7))
+    a(("Lw2",)); scales("Ls2"); a(("Luf", 1)); a(("Ldw",))
+    for j in range(8, 12):
+        a(("Lu", j))
+    a(("Luf", 2)); a(("warm",))
+    for j in range(4):
+        a(("Tu", j)); a(("Eu", j))
+    a(("P", 0, 0)); a(("P", 0, 1)); a(("Qu", 0, 1)); a(("Ps", 0)); a(("Qu", 1, 1)); a(("P", 1, 0)); a(("Qu", 2, 1)); a(("P", 1, 1)); a(("Qu", 3, 1))
+    a(("Ps", 1)); a(("P", 2, 0)); a(("P", 2, 1)); a(("Ps", 2)); a(("P", 3, 0)); a(("P", 3, 1)); a(("Ps", 3))
+    C = {1: [0, 1], 2: [2, 3], 3: [4], 4: [5, 6], 5: [7], 6: [8], 7: [9], 8: [10], 9: [11]}
+    TU = {0: 4, 2: 6, 4: 8, 6: 10}
+    TY = {7: 0, 9: 2, 11: 4}
+    for s in range(12):
+        j = s - 4
+        if j >= 1:
+            a(("S", j - 1))
+        if s >= 1:
+            a(("I", s - 1, 0))
+        if j >= 1:
+            a(("Y", j - 1)); a(("Sty", j - 1))
+        else:
+            for x in C.get(s, []):
+                a(("C", x))
+        if s >= 1:
+            a(("Qh", s - 1, 0))
+        if s - 1 in TU:
+            a(("Qu", TU[s - 1], 2))
+        if j >= 1:
+            for x in C.get(s, []):
+                a(("C", x))
+        if s - 1 in TY:
+            a(("Qy", TY[s - 1], 2))
+            if TY[s - 1] % 4 == 2:
+                planes(TY[s - 1] - 2, 4)
+        for t in range(4):
+            a(("S1", s, t)); a(("Eh", s, t))
+        if j >= 1:
+            a(("cast", j - 1))
+        if j >= 0:
+            for g in range(4):
+                a(("S2", j, g))
+        if s in TU:
+            a(("Tu", TU[s])); a(("Tu", TU[s] + 1)); a(("Eu", TU[s])); a(("Eu", TU[s] + 1))
+        if s in TY:
+            a(("Ty", TY[s], 2)); a(("Ey", TY[s], 2))
+    a(("I", 11, 0)); a(("S", 7)); a(("Qh", 11, 0)); a(("I", 11, 1)); a(("Y", 7)); a(("Sty", 7)); a(("Qh", 11, 1)); a(("cast", 7))
+    for j in (8, 9):
+        for g in range(3):
+            a(("S2", j, g))
+    for j in (8, 9):
+        a(("S2", j, 3))
+    for g in range(4):
+        a(("S2", 10, g))
+    a(("Ty", 6, 2)); a(("Ey", 6, 2))
+    for g in range(4):
+        a(("S2", 11, g))
+    a(("Qy", 4, 2))
+    a(("S", 8)); a(("S", 9)); a(("Y", 8)); a(("Sty", 8)); a(("cast", 8)); a(("Qy", 6, 2)); planes(4, 4)
+    a(("Y", 9)); a(("Sty", 9)); a(("cast", 9)); a(("Ty", 8, 2)); a(("Ey", 8, 2))
+    a(("S", 10)); a(("S", 11)); a(("Y", 10)); a(("Sty", 10)); a(("cast", 10)); a(("Yb", 11)); a(("Qy", 8, 2)); a(("Y", 11)); a(("Sty", 11))
+    a(("Stc", 8, 2))
+    a(("Ty", 10, 1)); a(("Ey", 10, 1)); a(("Qy", 10, 1)); a(("Ty", 11, 1)); a(("Ey", 11, 1)); a(("Qy", 11, 1)); a(("Stc", 10, 2))
+    for q in range(4):
+        a(("Sts", 8, 4, q))
+    return L
+
+
+def tile_user_tower_for_scoring_h1_kernel(
+    tc, users, w1_words, w1_scales, b1, w2_words, w2_scales, b2, user_free, dim_weight, out_0, out_1, out_2
+):
+    nc = tc.nc
+    with ExitStack() as ctx:
+        sb = ctx.enter_context(tc.tile_pool(name="sb", bufs=1))
+        ps = ctx.enter_context(tc.psum_pool(name="ps", bufs=1))
+        ctx.enter_context(tc.manual_schedule())
+
+        def tiles(name, count, shape, dtype):
+            return [sb.tile(shape, dtype, name="%s%d" % (name, n), align_bytes=64) for n in range(count)]
+
+        banks = [ps.tile([P, 512], F32, name="bank%d" % n) for n in range(MX_BANKS + T_BANKS)]
+        ident = sb.tile([P, P], F32, name="ident", align_bytes=64)
+        u_raw = tiles("u_raw", TILES, [P, K], BF16)
+        w1_raw = tiles("w1_raw", FG, [P, KG, 1024], U8)
+        w1_perm = tiles("w1_perm", FG, [P, KG, 1024], U8)
+        s1_raw = sb.tile([P, KG, F], U8, name="s1_raw", align_bytes=64)
+        s1_perm = tiles("s1_perm", FG, [P, KG, 512], U8)
+        b1_raw = sb.tile([P, FG, 4], BF16, name="b1_raw", align_bytes=64)
+        b1_f32 = sb.tile([P, FG, 4], F32, name="b1_f32", align_bytes=64)
+        w2 = sb.tile([P, FG, 1024], U8, name="w2", align_bytes=64)
+        s2 = sb.tile([P, FG, D], U8, name="s2", align_bytes=64)
+        b2_all = sb.tile([P, D], BF16, name="b2_all", align_bytes=64)
+        dw_all = sb.tile([P, D], BF16, name="dw_all", align_bytes=64)
+        uf = tiles("uf", CHUNKS, [P, 4, D], BF16)
+        x_t = tiles("x_t", 2, [P, KG, 512, 4], BF16)
+        x_codes = tiles("x_codes", CHUNKS, [P, KG, 512], U32)
+        x_scales = tiles("x_scales", CHUNKS, [P, KG, 512], U8)
+        h_rows = tiles("h_rows", H_RING, [P, 4, 512], BF16)
+        h_words = tiles("h_words", H_RING, [P, 512, 4], BF16)
+        h_codes = tiles("h_codes", SLOTS, [P, 512], U32)
+        h_scales = tiles("h_scales", SLOTS, [P, 512], U8)
+        y = tiles("y", TILES, [P, D], F32)
+        y_bf = tiles("y_bf", TILES, [P, D], BF16)
+        y_t = sb.tile([P, M, 4], BF16, name="y_t", align_bytes=64)
+        y_codes = sb.tile([P, M], U32, name="y_codes", align_bytes=64)
+        y_scales = sb.tile([P, M], U8, name="y_scales", align_bytes=64)
+
+        warm_in = sb.tile([P, 2048], BF16, name="warm_in", align_bytes=64) if USE_WARM else None
+        warm_codes = sb.tile([P, 512], U32, name="warm_codes", align_bytes=64) if USE_WARM else None
+        warm_scales = sb.tile([P, 512], U8, name="warm_scales", align_bytes=64) if USE_WARM else None
+        mx_used = []
+        t_used = []
+        held = {}
+
+        def mx_bank(key):
+            held[key] = banks[len(mx_used) % MX_BANKS]
+            mx_used.append(key)
+            return held[key]
+
+        def t_bank(key):
+            held[key] = banks[MX_BANKS + len(t_used) % T_BANKS]
+            t_used.append(key)
+            return held[key]
+
+        def load_users(j):
+            nc.sync.dma_start(out=u_raw[j][:], in_=users[j * P : (j + 1) * P, :])
+
+        def load_w1(fg):
+            src = w1_words[:, :, fg * 1024 : (fg + 1) * 1024].rearrange("g p n -> p g n")
+            nc.sync.dma_start(out=w1_raw[fg][:].bitcast(I32), in_=src.bitcast(I32))
+
+        def load_scale_rows(plane, rows, cols, q):
+            src = rows[:, 4 * q : 4 * q + 4, cols].rearrange("g r n -> r g n")
+            nc.sync.dma_start(out=plane[32 * q : 32 * q + 4, :, cols].bitcast(I32), in_=src.bitcast(I32))
+
+        def load_user_free(c):
+            src = user_free[c * 512 : (c + 1) * 512, :].rearrange("(i p) d -> p i d", p=P)
+            nc.sync.dma_start(out=uf[c][:], in_=src)
+
+        def permute_w1_codes(fg, g):
+            nc.vector.tensor_copy(
+                out=w1_perm[fg][:, g, :].rearrange("p (t m b) -> p t m b", t=4, b=2),
+                in_=w1_raw[fg][:, g, :].rearrange("p (m t b) -> p t m b", t=4, b=2),
+            )
+
+        def permute_w1_scales(fg):
+            nc.vector.tensor_copy(
+                out=s1_perm[fg][:].rearrange("p g (t m) -> p g t m", t=4),
+                in_=s1_raw[:, :, fg * 512 : (fg + 1) * 512].rearrange("p g (m t) -> p g t m", t=4),
+            )
+
+        def transpose_users(j):
+            bank = t_bank(("u", j))
+            words = u_raw[j][:].bitcast(F32)
+            for g in range(KG):
+                for u in range(2):
+                    col = (2 * g + u) * P
+                    nc.tensor.transpose(bank[:, col : col + P], words[:, 256 * g + u : 256 * (g + 1) : 2], ident[:])
+
+        def evacuate_users(j):
+            c, i = divmod(j, 4)
+            nc.scalar.copy(
+                out=x_t[c % 2][:, :, i * P : (i + 1) * P, :].bitcast(F32),
+                in_=held[("u", j)][:].rearrange("p (g u m) -> p g m u", g=KG, u=2),
+            )
+
+        def quantize_users(j, count):
+            c, i = divmod(j, 4)
+            cols = slice(i * P, (i + count) * P)
+            for g in range(KG):
+                nc.vector.quantize_mx(
+                    out=x_codes[c][:, g, cols].bitcast(FP8X4),
+                    scales=x_scales[c][:, g, cols],
+                    in_=x_t[c % 2][:, g, cols, :].rearrange("p m t -> p (m t)"),
+                )
+
+        def hidden_matmul(s, t):
+            c, fg = divmod(s, FG)
+            bank = mx_bank(("h", s, t))
+            for g in range(KG):
+                nc.tensor.matmul_mx(
+                    out=bank[:],
+                    lhsT=w1_perm[fg][:, g, t * 256 : (t + 1) * 256].bitcast(FP4X4),
+                    lhsT_scale=s1_perm[fg][:, g, t * P : (t + 1) * P],
+                    rhs=x_codes[c][:, g, :].bitcast(FP8X4),
+                    rhs_scale=x_scales[c][:, g, :],
+                    start=(g == 0),
+                    stop=(g == KG - 1),
+                )
+
+        def evacuate_hidden(s, t):
+            fg = s % FG
+            rows = h_rows[s % H_RING]
+            if s in PAIRED:
+                dst = rows[:].rearrange("p t m -> p (t m)").rearrange("p (u m e) -> p u m e", u=2, e=2)[:, t // 2, :, t % 2]
+            else:
+                dst = rows[:, t, :]
+            nc.scalar.activation(out=dst, in_=held[("h", s, t)][:], func=ACT.Relu, bias=b1_f32[:, fg, t : t + 1])
+
+        def part_cols(s, h):
+            width = 512 // SPLIT.get(s, 1)
+            return slice(h * width, (h + 1) * width)
+
+        def interleave_hidden(s, h, copy):
+            cols = part_cols(s, h)
+            if s in PAIRED:
+                src = h_rows[s % H_RING][:].rearrange("p t m -> p (t m)").bitcast(F32).rearrange("p (u m) -> p m u", u=2)
+                copy(out=h_words[s % H_RING][:, cols, :].bitcast(F32), in_=src[:, cols, :])
+            else:
+                copy(
+                    out=h_words[s % H_RING][:, cols, :].rearrange("p (c i) t -> p c t i", i=4),
+                    in_=h_rows[s % H_RING][:, :, cols].rearrange("p t (c i) -> p c t i", i=4),
+                )
+
+        def quantize_hidden(s, h):
+            cols = part_cols(s, h)
+            nc.vector.quantize_mx(
+                out=h_codes[s][:, cols].bitcast(FP8X4),
+                scales=h_scales[s][:, cols],
+                in_=h_words[s % H_RING][:, cols, :].rearrange("p m t -> p (m t)"),
+            )
+
+        def output_pass(j, fg):
+            c, i = divmod(j, 4)
+            bank = mx_bank(("z", j)) if fg == 0 else held[("z", j)]
+            s = c * FG + fg
+            nc.tensor.matmul_mx(
+                out=bank[:],
+                lhsT=h_codes[s][:, i * P : (i + 1) * P].bitcast(FP8X4),
+                lhsT_scale=h_scales[s][:, i * P : (i + 1) * P],
+                rhs=w2[:, fg, :].bitcast(FP4X4),
+                rhs_scale=s2[:, fg, :],
+                start=(fg == 0),
+                stop=(fg == FG - 1),
+            )
+
+        def add_free_and_bias(j):
+            c, i = divmod(j, 4)
+            nc.vector.tensor_tensor(out=y[j][:], in0=uf[c][:, i, :], in1=b2_all[:], op=ALU.add)
+
+        def add_product(j):
+            nc.vector.tensor_tensor(out=y[j][:], in0=held[("z", j)][:], in1=y[j][:], op=ALU.add)
+
+        def weight(j):
+            nc.vector.tensor_tensor(out=y[j][:], in0=y[j][:], in1=dw_all[:], op=ALU.mult)
+
+        def weight_rounded(j):
+            nc.vector.tensor_tensor(
+                out=y_bf[j][:].rearrange("p (u q e) -> p u q e", u=2, e=2),
+                in0=y[j][:].rearrange("p (q u e) -> p u q e", u=2, e=2),
+                in1=dw_all[:].rearrange("p (q u e) -> p u q e", u=2, e=2),
+                op=ALU.mult,
+            )
+
+        def store_output(j):
+            nc.sync.dma_start(out=out_0[j * P : (j + 1) * P, :], in_=y[j][:])
+
+        def round_output(j):
+            nc.scalar.copy(
+                out=y_bf[j][:].rearrange("p (u q e) -> p u q e", u=2, e=2),
+                in_=y[j][:].rearrange("p (q u e) -> p u q e", u=2, e=2),
+            )
+
+        def transpose_output(j, count):
+            bank = t_bank(("y", j))
+            for x in range(count):
+                words = y_bf[j + x][:].bitcast(F32)
+                for u in range(2):
+                    col = (2 * x + u) * P
+                    nc.tensor.transpose(bank[:, col : col + P], words[:, u * P : (u + 1) * P], ident[:])
+
+        def evacuate_output(j, count):
+            nc.scalar.copy(
+                out=y_t[:, j * P : (j + count) * P, :].bitcast(F32).rearrange("p (x m) u -> p x m u", x=count),
+                in_=held[("y", j)][:, : count * 256].rearrange("p (x u m) -> p x m u", x=count, u=2),
+            )
+
+        def quantize_output(j, count):
+            cols = slice(j * P, (j + count) * P)
+            nc.vector.quantize_mx(
+                out=y_codes[:, cols].bitcast(FP8X4),
+                scales=y_scales[:, cols],
+                in_=y_t[:, cols, :].rearrange("p m t -> p (m t)"),
+            )
+
+        def store_codes(j, count):
+            cols = slice(j * P, (j + count) * P)
+            dst = out_1[0].rearrange("p m t -> p (m t)")[:, 4 * j * P : 4 * (j + count) * P]
+            nc.sync.dma_start(out=dst.bitcast(I32), in_=y_codes[:, cols].bitcast(I32))
+
+        def store_scales(j, count, q):
+            cols = slice(j * P, (j + count) * P)
+            queue = nc.scalar if (j >= 8 and q % 2 == 1) else nc.sync
+            queue.dma_start(
+                out=out_2[0][4 * q : 4 * q + 4, cols].bitcast(I32),
+                in_=y_scales[32 * q : 32 * q + 4, cols].bitcast(I32),
+            )
+
+        def warm_source():
+            nc.vector.memset(warm_in[:], 1.0)
+
+        def warm_quantize():
+            nc.vector.quantize_mx(out=warm_codes[:].bitcast(FP8X4), scales=warm_scales[:], in_=warm_in[:])
+
+        def warm_pass(n):
+            nc.tensor.matmul_mx(
+                out=banks[MX_BANKS - 1][:],
+                lhsT=warm_codes[:, :64].bitcast(FP4X4),
+                lhsT_scale=warm_scales[:, :P],
+                rhs=warm_codes[:].bitcast(FP8X4),
+                rhs_scale=warm_scales[:],
+                start=True,
+                stop=True,
+            )
+
+        steps = {
+            "ms1": lambda: nc.vector.memset(s1_raw[:].bitcast(I32), 0),
+            "ident": lambda: make_identity(nc, ident[:]),
+            "ms2": lambda: nc.gpsimd.memset(s2[:].bitcast(I32), 0),
+            "Lu": load_users,
+            "Lw1": load_w1,
+            "Lb1": lambda: nc.sync.dma_start(out=b1_raw[:], in_=b1.rearrange("(g p t) -> p g t", p=P, t=4)),
+            "Ls1a": lambda q: load_scale_rows(s1_raw, w1_scales, slice(0, 512), q),
+            "Ls1b": lambda q: load_scale_rows(s1_raw, w1_scales, slice(512, F), q),
+            "Ls2": lambda q: load_scale_rows(s2, w2_scales, slice(0, D), q),
+            "Lw2": lambda: nc.sync.dma_start(
+                out=w2[:].bitcast(I32), in_=w2_words.rearrange("g p n -> p g n").bitcast(I32)
+            ),
+            "Lb2": lambda: nc.sync.dma_start(out=b2_all[:], in_=b2.partition_broadcast(P)),
+            "Ldw": lambda: nc.sync.dma_start(out=dw_all[:], in_=dim_weight.partition_broadcast(P)),
+            "Luf": load_user_free,
+            "warm": lambda: nc.scalar.activation(out=b1_f32[:], in_=b1_raw[:], func=ACT.Identity),
+            "Tu": transpose_users,
+            "Eu": evacuate_users,
+            "Qu": quantize_users,
+            "P": permute_w1_codes,
+            "Ps": permute_w1_scales,
+            "S1": hidden_matmul,
+            "Eh": evacuate_hidden,
+            "I": lambda s, h: interleave_hidden(s, h, nc.vector.tensor_copy),
+            "IA": lambda s, h: interleave_hidden(s, h, nc.scalar.copy),
+            "Qh": quantize_hidden,
+            "S2": output_pass,
+            "C": add_free_and_bias,
+            "S": add_product,
+            "Y": weight,
+            "Yb": weight_rounded,
+            "Sty": store_output,
+            "cast": round_output,
+            "Ty": transpose_output,
+            "Ey": evacuate_output,
+            "Qy": quantize_output,
+            "Stc": store_codes,
+            "Sts": store_scales,
+            "Wm": warm_source,
+            "Wq": warm_quantize,
+            "W": warm_pass,
+        }
+        for step in order():
+            steps[step[0]](*step[1:])

@@ -24,11 +24,13 @@ CHUNKS = M // 512
 SLOTS = CHUNKS * FG
 MX_BANKS = 5
 T_BANKS = 3
-H_RING = 3
+H_RING = 4
 
-USE_WARM = False
-PAIRED = ()
+USE_WARM = True
+PAIRED = (3, 4, 6, 8)
 SPLIT = {11: 2}
+WARM_FIRST = 14
+WARM_AFTER = [0, 8, 0, 10]
 
 
 def order():
@@ -41,37 +43,47 @@ def order():
         a(("Stc", j, n))
         for q in range(4):
             a(("Sts", j, n, q))
-    a(("ms1",)); a(("ident",)); a(("ms2",))
-    a(("Lu", 0)); a(("Lu", 1)); a(("Lw1", 0)); a(("Lb1",)); a(("Lu", 2)); a(("Lu", 3))
-    scales("Ls1a"); a(("Lw1", 1)); scales("Ls1b")
-    a(("Lw1", 2)); a(("Lu", 4)); a(("Lu", 5)); a(("Lw1", 3)); a(("Lb2",)); a(("Luf", 0)); a(("Lu", 6)); a(("Lu", 7))
-    a(("Lw2",)); scales("Ls2"); a(("Luf", 1)); a(("Ldw",))
+    a(("Wm",)); a(("warm",)); a(("ms1",)); a(("Wq",)); a(("ident",)); a(("ms2",))
+    a(("Lu", 0)); a(("Lw1h", 0)); a(("Lu", 1)); a(("Lw1h", 1)); a(("Lu", 2)); a(("Lu", 3))
+    scales("Ls1a"); a(("Lw1", 1)); a(("Lb1",)); scales("Ls1b")
+    a(("Lw1", 2)); a(("Lb2",)); a(("Ldw",)); a(("Lu", 4)); a(("Lu", 5)); a(("Lw1", 3)); a(("Lu", 6)); a(("Lu", 7))
+    a(("Lw2",)); scales("Ls2"); a(("Luf", 0))
     for j in range(8, 12):
         a(("Lu", j))
-    a(("Luf", 2)); a(("warm",))
+    a(("Luf", 1)); a(("Luf", 2))
+    a(("W", 0, WARM_FIRST))
     for j in range(4):
         a(("Tu", j)); a(("Eu", j))
-    a(("P", 0, 0)); a(("P", 0, 1)); a(("Qu", 0, 1)); a(("Ps", 0)); a(("Qu", 1, 1)); a(("P", 1, 0)); a(("Qu", 2, 1)); a(("P", 1, 1)); a(("Qu", 3, 1))
-    a(("Ps", 1)); a(("P", 2, 0)); a(("P", 2, 1)); a(("Ps", 2)); a(("P", 3, 0)); a(("P", 3, 1)); a(("Ps", 3))
-    C = {1: [0, 1], 2: [2, 3], 3: [4], 4: [5, 6], 5: [7], 6: [8], 7: [9], 8: [10], 9: [11]}
-    TU = {0: 4, 2: 6, 4: 8, 6: 10}
-    TY = {7: 0, 9: 2, 11: 4}
+        if WARM_AFTER[j]:
+            a(("W", j + 1, WARM_AFTER[j]))
+    a(("P", 0, 0)); a(("P", 0, 1)); a(("Qu", 0, 1)); a(("Qu", 1, 1)); a(("Ps", 0)); a(("Qu", 2, 1)); a(("Qu", 3, 1))
+    a(("P", 1, 0)); a(("P", 1, 1)); a(("Ps", 1)); a(("P", 2, 0)); a(("P", 2, 1)); a(("Ps", 2))
+    C = {3: [0], 4: [1, 2], 5: [3, 4], 6: [5, 6], 7: [7, 8], 8: [9], 9: [10], 10: [11]}
+    TU = {0: 4, 1: 6, 4: 8, 5: 10}
+    TY = {8: 0, 10: 2, 11: 4}
+    Z = {4: [0], 5: [1], 6: [2], 7: [3], 8: [4], 9: [5], 10: [6], 11: [7]}
     for s in range(12):
-        j = s - 4
-        if j >= 1:
-            a(("S", j - 1))
+        done = Z.get(s - 1, [])
+        for j in done:
+            a(("S", j))
+        if s == 1:
+            a(("P", 3, 0)); a(("P", 3, 1)); a(("Ps", 3))
+        if s == 2:
+            a(("Qu", 4, 2))
         if s >= 1:
             a(("I", s - 1, 0))
-        if j >= 1:
-            a(("Y", j - 1)); a(("Sty", j - 1))
-        else:
+        for j in done:
+            a(("Y", j)); a(("Sty", j))
+        if s == 2:
+            a(("Qu", 6, 2))
+        if not done:
             for x in C.get(s, []):
                 a(("C", x))
         if s >= 1:
             a(("Qh", s - 1, 0))
-        if s - 1 in TU:
+        if s - 1 in TU and s > 2:
             a(("Qu", TU[s - 1], 2))
-        if j >= 1:
+        if done:
             for x in C.get(s, []):
                 a(("C", x))
         if s - 1 in TY:
@@ -80,16 +92,23 @@ def order():
                 planes(TY[s - 1] - 2, 4)
         for t in range(4):
             a(("S1", s, t)); a(("Eh", s, t))
-        if j >= 1:
-            a(("cast", j - 1))
-        if j >= 0:
+        for j in done:
+            a(("cast", j))
+        if s in TU:
+            a(("Tu", TU[s])); a(("Tu", TU[s] + 1))
+            if s == 0:
+                a(("Tv",))
+            a(("Eu", TU[s])); a(("Eu", TU[s] + 1))
+            if s == 0:
+                a(("Ev",))
+        if s in TY:
+            a(("Ty", TY[s], 2))
+            if s < 11:
+                a(("Ey", TY[s], 2))
+        for j in Z.get(s, []):
             for g in range(4):
                 a(("S2", j, g))
-        if s in TU:
-            a(("Tu", TU[s])); a(("Tu", TU[s] + 1)); a(("Eu", TU[s])); a(("Eu", TU[s] + 1))
-        if s in TY:
-            a(("Ty", TY[s], 2)); a(("Ey", TY[s], 2))
-    a(("I", 11, 0)); a(("S", 7)); a(("Qh", 11, 0)); a(("I", 11, 1)); a(("Y", 7)); a(("Sty", 7)); a(("Qh", 11, 1)); a(("cast", 7))
+    a(("I", 11, 0)); a(("Ey", 4, 2)); a(("IA", 11, 1)); a(("S", 7)); a(("Qh", 11, 0)); a(("Y", 7)); a(("Sty", 7)); a(("Qy", 4, 2)); a(("Qh", 11, 1)); a(("cast", 7))
     for j in (8, 9):
         for g in range(3):
             a(("S2", j, g))
@@ -100,10 +119,10 @@ def order():
     a(("Ty", 6, 2)); a(("Ey", 6, 2))
     for g in range(4):
         a(("S2", 11, g))
-    a(("Qy", 4, 2))
-    a(("S", 8)); a(("S", 9)); a(("Y", 8)); a(("Sty", 8)); a(("cast", 8)); a(("Qy", 6, 2)); planes(4, 4)
-    a(("Y", 9)); a(("Sty", 9)); a(("cast", 9)); a(("Ty", 8, 2)); a(("Ey", 8, 2))
-    a(("S", 10)); a(("S", 11)); a(("Y", 10)); a(("Sty", 10)); a(("cast", 10)); a(("Yb", 11)); a(("Qy", 8, 2)); a(("Y", 11)); a(("Sty", 11))
+    a(("S", 8)); a(("S", 9)); a(("Y", 8)); a(("Sty", 8)); a(("cast", 8)); a(("Y", 9)); a(("Sty", 9)); a(("cast", 9))
+    a(("Qy", 6, 2)); planes(4, 4)
+    a(("Ty", 8, 2))
+    a(("S", 10)); a(("S", 11)); a(("Y", 10)); a(("Sty", 10)); a(("Ey", 8, 2)); a(("cast", 10)); a(("Yb", 11)); a(("Qy", 8, 2)); a(("Y", 11)); a(("Sty", 11))
     a(("Stc", 8, 2))
     a(("Ty", 10, 1)); a(("Ey", 10, 1)); a(("Qy", 10, 1)); a(("Ty", 11, 1)); a(("Ey", 11, 1)); a(("Qy", 11, 1)); a(("Stc", 10, 2))
     for q in range(4):
@@ -131,11 +150,14 @@ def tile_user_tower_for_scoring_h1_kernel(
         s1_raw = sb.tile([P, KG, F], U8, name="s1_raw", align_bytes=64)
         s1_perm = tiles("s1_perm", FG, [P, KG, 512], U8)
         b1_raw = sb.tile([P, FG, 4], BF16, name="b1_raw", align_bytes=64)
-        b1_f32 = sb.tile([P, FG, 4], F32, name="b1_f32", align_bytes=64)
+        act_warm = sb.tile([P, 1], F32, name="act_warm", align_bytes=64)
         w2 = sb.tile([P, FG, 1024], U8, name="w2", align_bytes=64)
         s2 = sb.tile([P, FG, D], U8, name="s2", align_bytes=64)
-        b2_all = sb.tile([P, D], BF16, name="b2_all", align_bytes=64)
-        dw_all = sb.tile([P, D], BF16, name="dw_all", align_bytes=64)
+        b2_col = sb.tile([P, 4], BF16, name="b2_col", align_bytes=64)
+        dw_col = sb.tile([P, 4], BF16, name="dw_col", align_bytes=64)
+        vec_all = sb.tile([P, 2, D], BF16, name="vec_all", align_bytes=64)
+        b2_all = vec_all[:, 0, :]
+        dw_all = vec_all[:, 1, :]
         uf = tiles("uf", CHUNKS, [P, 4, D], BF16)
         x_t = tiles("x_t", 2, [P, KG, 512, 4], BF16)
         x_codes = tiles("x_codes", CHUNKS, [P, KG, 512], U32)
@@ -150,9 +172,9 @@ def tile_user_tower_for_scoring_h1_kernel(
         y_codes = sb.tile([P, M], U32, name="y_codes", align_bytes=64)
         y_scales = sb.tile([P, M], U8, name="y_scales", align_bytes=64)
 
-        warm_in = sb.tile([P, 2048], BF16, name="warm_in", align_bytes=64) if USE_WARM else None
-        warm_codes = sb.tile([P, 512], U32, name="warm_codes", align_bytes=64) if USE_WARM else None
-        warm_scales = sb.tile([P, 512], U8, name="warm_scales", align_bytes=64) if USE_WARM else None
+        warm_in = sb.tile([P, 512], BF16, name="warm_in", align_bytes=64) if USE_WARM else None
+        warm_codes = sb.tile([P, P], U32, name="warm_codes", align_bytes=64) if USE_WARM else None
+        warm_scales = sb.tile([P, P], U8, name="warm_scales", align_bytes=64) if USE_WARM else None
         mx_used = []
         t_used = []
         held = {}
@@ -240,7 +262,7 @@ def tile_user_tower_for_scoring_h1_kernel(
                 dst = rows[:].rearrange("p t m -> p (t m)").rearrange("p (u m e) -> p u m e", u=2, e=2)[:, t // 2, :, t % 2]
             else:
                 dst = rows[:, t, :]
-            nc.scalar.activation(out=dst, in_=held[("h", s, t)][:], func=ACT.Relu, bias=b1_f32[:, fg, t : t + 1])
+            nc.scalar.activation(out=dst, in_=held[("h", s, t)][:], func=ACT.Relu, bias=b1_raw[:, fg, t : t + 1])
 
         def part_cols(s, h):
             width = 512 // SPLIT.get(s, 1)
@@ -281,19 +303,19 @@ def tile_user_tower_for_scoring_h1_kernel(
 
         def add_free_and_bias(j):
             c, i = divmod(j, 4)
-            nc.vector.tensor_tensor(out=y[j][:], in0=uf[c][:, i, :], in1=b2_all[:], op=ALU.add)
+            nc.vector.tensor_tensor(out=y[j][:], in0=uf[c][:, i, :], in1=b2_all, op=ALU.add)
 
         def add_product(j):
             nc.vector.tensor_tensor(out=y[j][:], in0=held[("z", j)][:], in1=y[j][:], op=ALU.add)
 
         def weight(j):
-            nc.vector.tensor_tensor(out=y[j][:], in0=y[j][:], in1=dw_all[:], op=ALU.mult)
+            nc.vector.tensor_tensor(out=y[j][:], in0=y[j][:], in1=dw_all, op=ALU.mult)
 
         def weight_rounded(j):
             nc.vector.tensor_tensor(
                 out=y_bf[j][:].rearrange("p (u q e) -> p u q e", u=2, e=2),
                 in0=y[j][:].rearrange("p (q u e) -> p u q e", u=2, e=2),
-                in1=dw_all[:].rearrange("p (q u e) -> p u q e", u=2, e=2),
+                in1=dw_all.rearrange("p (q u e) -> p u q e", u=2, e=2),
                 op=ALU.mult,
             )
 
@@ -342,26 +364,44 @@ def tile_user_tower_for_scoring_h1_kernel(
             )
 
         def warm_source():
-            nc.vector.memset(warm_in[:], 1.0)
+            nc.vector.memset(warm_in[:], 0.0)
 
         def warm_quantize():
             nc.vector.quantize_mx(out=warm_codes[:].bitcast(FP8X4), scales=warm_scales[:], in_=warm_in[:])
 
-        def warm_pass(n):
-            nc.tensor.matmul_mx(
-                out=banks[MX_BANKS - 1][:],
-                lhsT=warm_codes[:, :64].bitcast(FP4X4),
-                lhsT_scale=warm_scales[:, :P],
-                rhs=warm_codes[:].bitcast(FP8X4),
-                rhs_scale=warm_scales[:],
-                start=True,
-                stop=True,
+        def warm_pass(n, count):
+            for x in range(count):
+                nc.tensor.matmul_mx(
+                    out=banks[MX_BANKS - 1][:, :P],
+                    lhsT=warm_codes[:, :64].bitcast(FP4X4),
+                    lhsT_scale=warm_scales[:],
+                    rhs=warm_codes[:].bitcast(FP8X4),
+                    rhs_scale=warm_scales[:],
+                    start=True,
+                    stop=True,
+                )
+
+        def load_w1_half(g):
+            nc.sync.dma_start(out=w1_raw[0][:, g, :].bitcast(I32), in_=w1_words[g, :, 0:1024].bitcast(I32))
+
+        def transpose_vectors():
+            bank = t_bank(("v",))
+            for v, col in enumerate((b2_col, dw_col)):
+                words = col[:].bitcast(F32)
+                for u in range(2):
+                    at = (2 * v + u) * P
+                    nc.tensor.transpose(bank[:, at : at + P], words[:, u : u + 1].to_broadcast([P, P]), ident[:])
+
+        def evacuate_vectors():
+            nc.scalar.copy(
+                out=vec_all[:].bitcast(F32).rearrange("m v (q u) -> m v q u", u=2),
+                in_=held[("v",)][:].rearrange("m (v u q) -> m v q u", v=2, u=2),
             )
 
         steps = {
             "ms1": lambda: nc.vector.memset(s1_raw[:].bitcast(I32), 0),
             "ident": lambda: make_identity(nc, ident[:]),
-            "ms2": lambda: nc.gpsimd.memset(s2[:].bitcast(I32), 0),
+            "ms2": lambda: nc.vector.memset(s2[:].bitcast(I32), 0),
             "Lu": load_users,
             "Lw1": load_w1,
             "Lb1": lambda: nc.sync.dma_start(out=b1_raw[:], in_=b1.rearrange("(g p t) -> p g t", p=P, t=4)),
@@ -371,10 +411,10 @@ def tile_user_tower_for_scoring_h1_kernel(
             "Lw2": lambda: nc.sync.dma_start(
                 out=w2[:].bitcast(I32), in_=w2_words.rearrange("g p n -> p g n").bitcast(I32)
             ),
-            "Lb2": lambda: nc.sync.dma_start(out=b2_all[:], in_=b2.partition_broadcast(P)),
-            "Ldw": lambda: nc.sync.dma_start(out=dw_all[:], in_=dim_weight.partition_broadcast(P)),
+            "Lb2": lambda: nc.sync.dma_start(out=b2_col[:], in_=b2.rearrange("(p t) -> p t", t=4)),
+            "Ldw": lambda: nc.sync.dma_start(out=dw_col[:], in_=dim_weight.rearrange("(p t) -> p t", t=4)),
             "Luf": load_user_free,
-            "warm": lambda: nc.scalar.activation(out=b1_f32[:], in_=b1_raw[:], func=ACT.Identity),
+            "warm": lambda: nc.scalar.activation(out=act_warm[:], in_=warm_in[:, 0:1], func=ACT.Relu),
             "Tu": transpose_users,
             "Eu": evacuate_users,
             "Qu": quantize_users,
@@ -400,6 +440,9 @@ def tile_user_tower_for_scoring_h1_kernel(
             "Wm": warm_source,
             "Wq": warm_quantize,
             "W": warm_pass,
+            "Lw1h": load_w1_half,
+            "Tv": transpose_vectors,
+            "Ev": evacuate_vectors,
         }
         for step in order():
             steps[step[0]](*step[1:])

@@ -27,10 +27,10 @@ T_BANKS = 3
 H_RING = 4
 
 USE_WARM = True
-PAIRED = (3, 4, 6, 8)
+PAIRED = (4, 6, 8, 9)
 SPLIT = {11: 2}
-WARM_FIRST = 14
-WARM_AFTER = [0, 8, 0, 10]
+WARM_FIRST = 13
+WARM_AFTER = [0, 7, 0, 9]
 
 
 def order():
@@ -43,9 +43,9 @@ def order():
         a(("Stc", j, n))
         for q in range(4):
             a(("Sts", j, n, q))
-    a(("Wm",)); a(("warm",)); a(("ms1",)); a(("Wq",)); a(("ident",)); a(("ms2",))
-    a(("Lu", 0)); a(("Lw1h", 0)); a(("Lu", 1)); a(("Lw1h", 1)); a(("Lu", 2)); a(("Lu", 3))
-    scales("Ls1a"); a(("Lw1", 1)); a(("Lb1",)); scales("Ls1b")
+    a(("ident",)); a(("Wm",)); a(("ms1a",)); a(("Wq",)); a(("warm",)); a(("ms1",)); a(("ms2",))
+    a(("Lu", 0)); a(("Lu", 1)); scales("Ls1a"); a(("Lw1h", 0)); a(("Lu", 2)); a(("Lu", 3)); a(("Lw1h", 1))
+    a(("Lw1", 1)); a(("Lb1",)); scales("Ls1b")
     a(("Lw1", 2)); a(("Lb2",)); a(("Ldw",)); a(("Lu", 4)); a(("Lu", 5)); a(("Lw1", 3)); a(("Lu", 6)); a(("Lu", 7))
     a(("Lw2",)); scales("Ls2"); a(("Luf", 0))
     for j in range(8, 12):
@@ -56,11 +56,11 @@ def order():
         a(("Tu", j)); a(("Eu", j))
         if WARM_AFTER[j]:
             a(("W", j + 1, WARM_AFTER[j]))
-    a(("P", 0, 0)); a(("P", 0, 1)); a(("Qu", 0, 1)); a(("Qu", 1, 1)); a(("Ps", 0)); a(("Qu", 2, 1)); a(("Qu", 3, 1))
+    a(("Ps", 0)); a(("P", 0, 0)); a(("Qu", 0, 1)); a(("Qu", 1, 1)); a(("P", 0, 1)); a(("Qu", 2, 1)); a(("Qu", 3, 1))
     a(("P", 1, 0)); a(("P", 1, 1)); a(("Ps", 1)); a(("P", 2, 0)); a(("P", 2, 1)); a(("Ps", 2))
     C = {3: [0], 4: [1, 2], 5: [3, 4], 6: [5, 6], 7: [7, 8], 8: [9], 9: [10], 10: [11]}
     TU = {0: 4, 1: 6, 4: 8, 5: 10}
-    TY = {8: 0, 10: 2, 11: 4}
+    TY = {8: 0, 9: 2}
     Z = {4: [0], 5: [1], 6: [2], 7: [3], 8: [4], 9: [5], 10: [6], 11: [7]}
     for s in range(12):
         done = Z.get(s - 1, [])
@@ -93,7 +93,8 @@ def order():
         for t in range(4):
             a(("S1", s, t)); a(("Eh", s, t))
         for j in done:
-            a(("cast", j))
+            if s < 11:
+                a(("cast", j))
         if s in TU:
             a(("Tu", TU[s])); a(("Tu", TU[s] + 1))
             if s == 0:
@@ -102,31 +103,24 @@ def order():
             if s == 0:
                 a(("Ev",))
         if s in TY:
-            a(("Ty", TY[s], 2))
-            if s < 11:
-                a(("Ey", TY[s], 2))
+            a(("Ty", TY[s], 2)); a(("Ey", TY[s], 2))
         for j in Z.get(s, []):
             for g in range(4):
                 a(("S2", j, g))
-    a(("I", 11, 0)); a(("Ey", 4, 2)); a(("IA", 11, 1)); a(("S", 7)); a(("Qh", 11, 0)); a(("Y", 7)); a(("Sty", 7)); a(("Qy", 4, 2)); a(("Qh", 11, 1)); a(("cast", 7))
-    for j in (8, 9):
-        for g in range(3):
+    def z(j, first=0, last=4):
+        for g in range(first, last):
             a(("S2", j, g))
-    for j in (8, 9):
-        a(("S2", j, 3))
-    for g in range(4):
-        a(("S2", 10, g))
-    a(("Ty", 6, 2)); a(("Ey", 6, 2))
-    for g in range(4):
-        a(("S2", 11, g))
-    a(("S", 8)); a(("S", 9)); a(("Y", 8)); a(("Sty", 8)); a(("cast", 8)); a(("Y", 9)); a(("Sty", 9)); a(("cast", 9))
-    a(("Qy", 6, 2)); planes(4, 4)
+    a(("I", 11, 0)); a(("IA", 11, 1)); a(("cast", 6)); a(("S", 7)); a(("Qh", 11, 0)); a(("Y", 7)); a(("Sty", 7)); a(("Qh", 11, 1)); a(("cast", 7))
+    z(8, 0, 3); z(9, 0, 3); z(8, 3); z(9, 3); z(10); z(11)
+    a(("Ty", 4, 2)); a(("Ty", 6, 2))
+    a(("S", 8)); a(("S", 9)); a(("Y", 8)); a(("Sty", 8)); a(("cast", 8)); a(("Y", 9)); a(("Sty", 9)); a(("cast", 9)); a(("Ey", 4, 2)); a(("Ey", 6, 2))
     a(("Ty", 8, 2))
-    a(("S", 10)); a(("S", 11)); a(("Y", 10)); a(("Sty", 10)); a(("Ey", 8, 2)); a(("cast", 10)); a(("Yb", 11)); a(("Qy", 8, 2)); a(("Y", 11)); a(("Sty", 11))
-    a(("Stc", 8, 2))
-    a(("Ty", 10, 1)); a(("Ey", 10, 1)); a(("Qy", 10, 1)); a(("Ty", 11, 1)); a(("Ey", 11, 1)); a(("Qy", 11, 1)); a(("Stc", 10, 2))
+    a(("S", 10)); a(("S", 11)); a(("Y", 10)); a(("Sty", 10)); a(("cast", 10)); a(("Ey", 8, 2))
+    a(("Yb", 11)); a(("Qy", 4, 4)); a(("Stc", 4, 4)); a(("Y", 11)); a(("Sty", 11))
+    a(("Qy", 8, 2)); a(("Stc", 8, 2))
+    a(("Ty", 10, 2)); a(("Ey", 10, 2)); a(("Qy", 10, 2)); a(("Stc", 10, 2))
     for q in range(4):
-        a(("Sts", 8, 4, q))
+        a(("Sts", 4, 8, q))
     return L
 
 
@@ -139,20 +133,20 @@ def tile_user_tower_for_scoring_h1_kernel(
         ps = ctx.enter_context(tc.psum_pool(name="ps", bufs=1))
         ctx.enter_context(tc.manual_schedule())
 
-        def tiles(name, count, shape, dtype):
-            return [sb.tile(shape, dtype, name="%s%d" % (name, n), align_bytes=64) for n in range(count)]
+        def tiles(name, count, shape, dtype, align=64):
+            return [sb.tile(shape, dtype, name="%s%d" % (name, n), align_bytes=align) for n in range(count)]
 
         banks = [ps.tile([P, 512], F32, name="bank%d" % n) for n in range(MX_BANKS + T_BANKS)]
         ident = sb.tile([P, P], F32, name="ident", align_bytes=64)
         u_raw = tiles("u_raw", TILES, [P, K], BF16)
         w1_raw = tiles("w1_raw", FG, [P, KG, 1024], U8)
-        w1_perm = tiles("w1_perm", FG, [P, KG, 1024], U8)
+        w1_perm = tiles("w1_perm", FG, [P, KG, 1024], U8, 256)
         s1_raw = sb.tile([P, KG, F], U8, name="s1_raw", align_bytes=64)
-        s1_perm = tiles("s1_perm", FG, [P, KG, 512], U8)
+        s1_perm = tiles("s1_perm", FG, [P, KG, 512], U8, 256)
         b1_raw = sb.tile([P, FG, 4], BF16, name="b1_raw", align_bytes=64)
         act_warm = sb.tile([P, 1], F32, name="act_warm", align_bytes=64)
-        w2 = sb.tile([P, FG, 1024], U8, name="w2", align_bytes=64)
-        s2 = sb.tile([P, FG, D], U8, name="s2", align_bytes=64)
+        w2 = sb.tile([P, FG, 1024], U8, name="w2", align_bytes=256)
+        s2 = sb.tile([P, FG, D], U8, name="s2", align_bytes=256)
         b2_col = sb.tile([P, 4], BF16, name="b2_col", align_bytes=64)
         dw_col = sb.tile([P, 4], BF16, name="dw_col", align_bytes=64)
         vec_all = sb.tile([P, 2, D], BF16, name="vec_all", align_bytes=64)
@@ -160,12 +154,12 @@ def tile_user_tower_for_scoring_h1_kernel(
         dw_all = vec_all[:, 1, :]
         uf = tiles("uf", CHUNKS, [P, 4, D], BF16)
         x_t = tiles("x_t", 2, [P, KG, 512, 4], BF16)
-        x_codes = tiles("x_codes", CHUNKS, [P, KG, 512], U32)
-        x_scales = tiles("x_scales", CHUNKS, [P, KG, 512], U8)
+        x_codes = tiles("x_codes", CHUNKS, [P, KG, 512], U32, 256)
+        x_scales = tiles("x_scales", CHUNKS, [P, KG, 512], U8, 256)
         h_rows = tiles("h_rows", H_RING, [P, 4, 512], BF16)
         h_words = tiles("h_words", H_RING, [P, 512, 4], BF16)
-        h_codes = tiles("h_codes", SLOTS, [P, 512], U32)
-        h_scales = tiles("h_scales", SLOTS, [P, 512], U8)
+        h_codes = tiles("h_codes", SLOTS, [P, 512], U32, 256)
+        h_scales = tiles("h_scales", SLOTS, [P, 512], U8, 256)
         y = tiles("y", TILES, [P, D], F32)
         y_bf = tiles("y_bf", TILES, [P, D], BF16)
         y_t = sb.tile([P, M, 4], BF16, name="y_t", align_bytes=64)
@@ -197,8 +191,8 @@ def tile_user_tower_for_scoring_h1_kernel(
             nc.sync.dma_start(out=w1_raw[fg][:].bitcast(I32), in_=src.bitcast(I32))
 
         def load_scale_rows(plane, rows, cols, q):
-            src = rows[:, 4 * q : 4 * q + 4, cols].rearrange("g r n -> r g n")
-            nc.sync.dma_start(out=plane[32 * q : 32 * q + 4, :, cols].bitcast(I32), in_=src.bitcast(I32))
+            src = rows[:, q:16:4, cols].rearrange("g r n -> r g n")
+            nc.sync.dma_start(out=plane[q:P:32, :, cols].bitcast(I32), in_=src.bitcast(I32))
 
         def load_user_free(c):
             src = user_free[c * 512 : (c + 1) * 512, :].rearrange("(i p) d -> p i d", p=P)
@@ -357,10 +351,10 @@ def tile_user_tower_for_scoring_h1_kernel(
 
         def store_scales(j, count, q):
             cols = slice(j * P, (j + count) * P)
-            queue = nc.scalar if (j >= 8 and q % 2 == 1) else nc.sync
+            queue = nc.scalar if (j >= 4 and q % 2 == 1) else nc.sync
             queue.dma_start(
-                out=out_2[0][4 * q : 4 * q + 4, cols].bitcast(I32),
-                in_=y_scales[32 * q : 32 * q + 4, cols].bitcast(I32),
+                out=out_2[0][q:16:4, cols].bitcast(I32),
+                in_=y_scales[q:P:32, cols].bitcast(I32),
             )
 
         def warm_source():
@@ -399,7 +393,8 @@ def tile_user_tower_for_scoring_h1_kernel(
             )
 
         steps = {
-            "ms1": lambda: nc.vector.memset(s1_raw[:].bitcast(I32), 0),
+            "ms1a": lambda: nc.vector.memset(s1_raw[:, :, 0:512].bitcast(I32), 0),
+            "ms1": lambda: nc.vector.memset(s1_raw[:, :, 512:F].bitcast(I32), 0),
             "ident": lambda: make_identity(nc, ident[:]),
             "ms2": lambda: nc.vector.memset(s2[:].bitcast(I32), 0),
             "Lu": load_users,

@@ -27,10 +27,23 @@ T_BANKS = 3
 H_RING = 4
 
 USE_WARM = True
-PAIRED = (4, 6, 8, 9)
+PAIRED = (4, 6, 9, 10)
 SPLIT = {11: 2}
-WARM_FIRST = 13
-WARM_AFTER = [0, 7, 0, 9]
+LOADS = [("Lw1", 1), ("Lb1",), ("Ls1b",), ("Lu", 4), ("Lu", 5), ("Lb2",), ("Ldw",), ("Lw1", 2), ("Lu", 6), ("Lw1", 3), ("Lu", 7), ("Lw2",), ("Ls2",), ("Luf", 0), ("Lu", 8), ("Lu", 9), ("Lu", 10), ("Lu", 11), ("Luf", 1), ("Luf", 2)]
+Z = {4: [0], 5: [1], 6: [2], 7: [3], 8: [4], 9: [5], 10: [6], 11: [7]}
+C = {4: [0, 1], 5: [2, 3], 6: [4, 5], 7: [6], 8: [7, 8], 9: [9, 10], 10: [11]}
+TU = {0: [4, 5], 1: [6, 7], 4: [8, 9], 5: [10, 11]}
+QU_FIRST = {2: [4]}
+QU_MID = {2: [6]}
+QU_LAST = {5: [8], 6: [10]}
+PRE = {}
+TY = {8: [0], 9: [2]}
+QY = {9: [0], 10: [2]}
+VECTORS_AFTER = 0
+CAST = {5: [0], 6: [1], 7: [2], 8: [3], 12: [4, 5, 6]}
+HALVES = True
+HEAD_LOADS = [("Lug", 0, 0), ("Lug", 0, 1), ("Lw1h", 0), ("Ls1a",), ("Lug", 1, 0), ("Lug", 1, 1), ("Lw1h", 1)]
+HEAD = [("W", 0, 13), ("Tug", 0, 0), ("Eug", 0, 0), ("Tug", 0, 1), ("Eug", 0, 1), ("W", 1, 7), ("Tug", 1, 0), ("Eug", 1, 0), ("Tug", 1, 1), ("Eug", 1, 1), ("W", 2, 3), ("P", 0, 0), ("Qug", 0, 0), ("Ps", 0), ("Qug", 0, 1), ("S1a", 0), ("S1a", 1), ("S1a", 2), ("S1a", 3), ("P", 0, 1), ("Qug", 1, 0), ("Qug", 1, 1)]
 
 
 def order():
@@ -44,73 +57,73 @@ def order():
         for q in range(4):
             a(("Sts", j, n, q))
     a(("ident",)); a(("Wm",)); a(("ms1a",)); a(("Wq",)); a(("warm",)); a(("ms1",)); a(("ms2",))
-    a(("Lu", 0)); a(("Lu", 1)); scales("Ls1a"); a(("Lw1h", 0)); a(("Lu", 2)); a(("Lu", 3)); a(("Lw1h", 1))
-    a(("Lw1", 1)); a(("Lb1",)); scales("Ls1b")
-    a(("Lw1", 2)); a(("Lb2",)); a(("Ldw",)); a(("Lu", 4)); a(("Lu", 5)); a(("Lw1", 3)); a(("Lu", 6)); a(("Lu", 7))
-    a(("Lw2",)); scales("Ls2"); a(("Luf", 0))
-    for j in range(8, 12):
-        a(("Lu", j))
-    a(("Luf", 1)); a(("Luf", 2))
-    a(("W", 0, WARM_FIRST))
-    for j in range(4):
-        a(("Tu", j)); a(("Eu", j))
-        if WARM_AFTER[j]:
-            a(("W", j + 1, WARM_AFTER[j]))
-    a(("Ps", 0)); a(("P", 0, 0)); a(("Qu", 0, 1)); a(("Qu", 1, 1)); a(("P", 0, 1)); a(("Qu", 2, 1)); a(("Qu", 3, 1))
+    for step in HEAD_LOADS:
+        if step[0] == "Ls1a":
+            scales(step[0])
+        else:
+            a(step)
+    for step in LOADS:
+        if step[0] in ("Ls1b", "Ls2"):
+            scales(step[0])
+        else:
+            a(step)
+    for step in HEAD:
+        a(step)
     a(("P", 1, 0)); a(("P", 1, 1)); a(("Ps", 1)); a(("P", 2, 0)); a(("P", 2, 1)); a(("Ps", 2))
-    C = {3: [0], 4: [1, 2], 5: [3, 4], 6: [5, 6], 7: [7, 8], 8: [9], 9: [10], 10: [11]}
-    TU = {0: 4, 1: 6, 4: 8, 5: 10}
-    TY = {8: 0, 9: 2}
-    Z = {4: [0], 5: [1], 6: [2], 7: [3], 8: [4], 9: [5], 10: [6], 11: [7]}
     for s in range(12):
         done = Z.get(s - 1, [])
-        for j in done:
-            a(("S", j))
         if s == 1:
-            a(("P", 3, 0)); a(("P", 3, 1)); a(("Ps", 3))
-        if s == 2:
-            a(("Qu", 4, 2))
+            a(("P", 3, 0)); a(("P", 3, 1))
+        for x in QU_FIRST.get(s, []):
+            a(("Qu", x, 2))
         if s >= 1:
             a(("I", s - 1, 0))
         for j in done:
-            a(("Y", j)); a(("Sty", j))
-        if s == 2:
-            a(("Qu", 6, 2))
-        if not done:
-            for x in C.get(s, []):
-                a(("C", x))
+            a(("S", j))
+        for x in QU_MID.get(s, []):
+            a(("Qu", x, 2))
+        for x in PRE.get(s, []):
+            a(("pre", x))
+        if s == 1:
+            a(("Ps", 3))
         if s >= 1:
             a(("Qh", s - 1, 0))
-        if s - 1 in TU and s > 2:
-            a(("Qu", TU[s - 1], 2))
-        if done:
-            for x in C.get(s, []):
-                a(("C", x))
-        if s - 1 in TY:
-            a(("Qy", TY[s - 1], 2))
-            if TY[s - 1] % 4 == 2:
-                planes(TY[s - 1] - 2, 4)
-        for t in range(4):
-            a(("S1", s, t)); a(("Eh", s, t))
         for j in done:
-            if s < 11:
-                a(("cast", j))
-        if s in TU:
-            a(("Tu", TU[s])); a(("Tu", TU[s] + 1))
-            if s == 0:
-                a(("Tv",))
-            a(("Eu", TU[s])); a(("Eu", TU[s] + 1))
-            if s == 0:
-                a(("Ev",))
-        if s in TY:
-            a(("Ty", TY[s], 2)); a(("Ey", TY[s], 2))
+            a(("Y", j)); a(("Sty", j))
+        for x in QU_LAST.get(s, []):
+            a(("Qu", x, 2))
+        for x in C.get(s, []):
+            a(("C", x))
+        for x in QY.get(s, []):
+            a(("Qy", x, 2))
+            if x == 2:
+                planes(0, 4)
+        for t in range(4):
+            a(("S1b", t) if (s == 0 and HALVES) else ("S1", s, t)); a(("Eh", s, t))
+        for x in TU.get(s, []):
+            a(("Tu", x))
+        if s == VECTORS_AFTER:
+            a(("Tv",))
+        for x in TY.get(s, []):
+            a(("Ty", x, 2))
+        for x in TU.get(s, []):
+            a(("Eu", x))
+        if s == VECTORS_AFTER:
+            a(("Ev",))
+        for j in CAST.get(s, []):
+            a(("cast", j))
+        for x in TY.get(s, []):
+            a(("Ey", x, 2))
         for j in Z.get(s, []):
             for g in range(4):
                 a(("S2", j, g))
     def z(j, first=0, last=4):
         for g in range(first, last):
             a(("S2", j, g))
-    a(("I", 11, 0)); a(("IA", 11, 1)); a(("cast", 6)); a(("S", 7)); a(("Qh", 11, 0)); a(("Y", 7)); a(("Sty", 7)); a(("Qh", 11, 1)); a(("cast", 7))
+    a(("I", 11, 0)); a(("IA", 11, 1))
+    for j in CAST.get(12, []):
+        a(("cast", j))
+    a(("S", 7)); a(("Qh", 11, 0)); a(("Y", 7)); a(("Sty", 7)); a(("Qh", 11, 1)); a(("cast", 7))
     z(8, 0, 3); z(9, 0, 3); z(8, 3); z(9, 3); z(10); z(11)
     a(("Ty", 4, 2)); a(("Ty", 6, 2))
     a(("S", 8)); a(("S", 9)); a(("Y", 8)); a(("Sty", 8)); a(("cast", 8)); a(("Y", 9)); a(("Sty", 9)); a(("cast", 9)); a(("Ey", 4, 2)); a(("Ey", 6, 2))
@@ -118,7 +131,7 @@ def order():
     a(("S", 10)); a(("S", 11)); a(("Y", 10)); a(("Sty", 10)); a(("cast", 10)); a(("Ey", 8, 2))
     a(("Yb", 11)); a(("Qy", 4, 4)); a(("Stc", 4, 4)); a(("Y", 11)); a(("Sty", 11))
     a(("Qy", 8, 2)); a(("Stc", 8, 2))
-    a(("Ty", 10, 2)); a(("Ey", 10, 2)); a(("Qy", 10, 2)); a(("Stc", 10, 2))
+    a(("Ty", 10, 1)); a(("Ey", 10, 1)); a(("Qy", 10, 1)); a(("Ty", 11, 1)); a(("Ey", 11, 1)); a(("Qy", 11, 1)); a(("Stc", 10, 2))
     for q in range(4):
         a(("Sts", 4, 8, q))
     return L
@@ -138,7 +151,8 @@ def tile_user_tower_for_scoring_h1_kernel(
 
         banks = [ps.tile([P, 512], F32, name="bank%d" % n) for n in range(MX_BANKS + T_BANKS)]
         ident = sb.tile([P, P], F32, name="ident", align_bytes=64)
-        u_raw = tiles("u_raw", TILES, [P, K], BF16)
+        u_raw = [None] * 4 + tiles("u_raw", TILES - 4, [P, K], BF16)
+        u_head = tiles("u_head", 4, [P, 2, 512], BF16)
         w1_raw = tiles("w1_raw", FG, [P, KG, 1024], U8)
         w1_perm = tiles("w1_perm", FG, [P, KG, 1024], U8, 256)
         s1_raw = sb.tile([P, KG, F], U8, name="s1_raw", align_bytes=64)
@@ -375,6 +389,44 @@ def tile_user_tower_for_scoring_h1_kernel(
                     stop=True,
                 )
 
+        def load_users_half(g, pair):
+            src = users[pair * 256 : (pair + 1) * 256, g * 512 : (g + 1) * 512].rearrange("(i p) k -> p i k", p=P)
+            nc.sync.dma_start(out=u_head[2 * g + pair][:], in_=src)
+
+        def transpose_users_half(g, pair):
+            bank = t_bank(("uh", g, pair))
+            words = u_head[2 * g + pair][:].bitcast(F32)
+            for i in range(2):
+                for u in range(2):
+                    col = (2 * i + u) * P
+                    nc.tensor.transpose(bank[:, col : col + P], words[:, i, u:256:2], ident[:])
+
+        def evacuate_users_half(g, pair):
+            nc.scalar.copy(
+                out=x_t[0][:, g, pair * 256 : (pair + 1) * 256, :].bitcast(F32).rearrange("p (i m) u -> p i m u", i=2),
+                in_=held[("uh", g, pair)][:].rearrange("p (i u m) -> p i m u", i=2, u=2),
+            )
+
+        def quantize_users_half(g, pair):
+            cols = slice(pair * 256, (pair + 1) * 256)
+            nc.vector.quantize_mx(
+                out=x_codes[0][:, g, cols].bitcast(FP8X4),
+                scales=x_scales[0][:, g, cols],
+                in_=x_t[0][:, g, cols, :].rearrange("p m t -> p (m t)"),
+            )
+
+        def hidden_first_pass(t, g):
+            bank = mx_bank(("h", 0, t)) if g == 0 else held[("h", 0, t)]
+            nc.tensor.matmul_mx(
+                out=bank[:],
+                lhsT=w1_perm[0][:, g, t * 256 : (t + 1) * 256].bitcast(FP4X4),
+                lhsT_scale=s1_perm[0][:, g, t * P : (t + 1) * P],
+                rhs=x_codes[0][:, g, :].bitcast(FP8X4),
+                rhs_scale=x_scales[0][:, g, :],
+                start=(g == 0),
+                stop=(g == KG - 1),
+            )
+
         def load_w1_half(g):
             nc.sync.dma_start(out=w1_raw[0][:, g, :].bitcast(I32), in_=w1_words[g, :, 0:1024].bitcast(I32))
 
@@ -436,6 +488,12 @@ def tile_user_tower_for_scoring_h1_kernel(
             "Wq": warm_quantize,
             "W": warm_pass,
             "Lw1h": load_w1_half,
+            "Lug": load_users_half,
+            "Tug": transpose_users_half,
+            "Eug": evacuate_users_half,
+            "Qug": quantize_users_half,
+            "S1a": lambda t: hidden_first_pass(t, 0),
+            "S1b": lambda t: hidden_first_pass(t, 1),
             "Tv": transpose_vectors,
             "Ev": evacuate_vectors,
         }

@@ -10,6 +10,7 @@ F32 = mybir.dt.float32
 BF16 = mybir.dt.bfloat16
 I32 = mybir.dt.int32
 U32 = mybir.dt.uint32
+U16 = mybir.dt.uint16
 U8 = mybir.dt.uint8
 FP8X4 = mybir.dt.float8_e4m3fn_x4
 FP4X4 = mybir.dt.float4_e2m1fn_x4
@@ -20,121 +21,33 @@ P = 128
 KG = K // 512
 FG = F // 512
 TILES = M // P
+PAIRS = TILES // 2
 CHUNKS = M // 512
-SLOTS = CHUNKS * FG
-MX_BANKS = 5
-T_BANKS = 3
+BANKS = 8
 H_RING = 4
+X_RING = 6
 
-USE_WARM = True
-PAIRED = (4, 6, 9, 10)
-SPLIT = {11: 2}
-LOADS = [("Lw1", 1), ("Lb1",), ("Ls1b",), ("Lu", 4), ("Lu", 5), ("Lb2",), ("Ldw",), ("Lw1", 2), ("Lu", 6), ("Lw1", 3), ("Lu", 7), ("Lw2",), ("Ls2",), ("Luf", 0), ("Lu", 8), ("Lu", 9), ("Lu", 10), ("Lu", 11), ("Luf", 1), ("Luf", 2)]
-Z = {4: [0], 5: [1], 6: [2], 7: [3], 8: [4], 9: [5], 10: [6], 11: [7]}
-C = {4: [0, 1], 5: [2, 3], 6: [4, 5], 7: [6], 8: [7, 8], 9: [9, 10], 10: [11]}
-TU = {0: [4, 5], 1: [6, 7], 4: [8, 9], 5: [10, 11]}
-QU_FIRST = {2: [4]}
-QU_MID = {2: [6]}
-QU_LAST = {5: [8], 6: [10]}
-PRE = {}
-TY = {8: [0], 9: [2]}
-QY = {9: [0], 10: [2]}
-VECTORS_AFTER = 0
-CAST = {5: [0], 6: [1], 7: [2], 8: [3], 12: [4, 5, 6]}
-HALVES = True
-HEAD_LOADS = [("Lug", 0, 0), ("Lug", 0, 1), ("Lw1h", 0), ("Ls1a",), ("Lug", 1, 0), ("Lug", 1, 1), ("Lw1h", 1)]
-HEAD = [("W", 0, 13), ("Tug", 0, 0), ("Eug", 0, 0), ("Tug", 0, 1), ("Eug", 0, 1), ("W", 1, 7), ("Tug", 1, 0), ("Eug", 1, 0), ("Tug", 1, 1), ("Eug", 1, 1), ("W", 2, 3), ("P", 0, 0), ("Qug", 0, 0), ("Ps", 0), ("Qug", 0, 1), ("S1a", 0), ("S1a", 1), ("S1a", 2), ("S1a", 3), ("P", 0, 1), ("Qug", 1, 0), ("Qug", 1, 1)]
-
-
-def order():
-    L = []
-    a = L.append
-    def scales(name):
-        for q in range(4):
-            a((name, q))
-    def planes(j, n):
-        a(("Stc", j, n))
-        for q in range(4):
-            a(("Sts", j, n, q))
-    a(("ident",)); a(("Wm",)); a(("ms1a",)); a(("Wq",)); a(("warm",)); a(("ms1",)); a(("ms2",))
-    for step in HEAD_LOADS:
-        if step[0] == "Ls1a":
-            scales(step[0])
-        else:
-            a(step)
-    for step in LOADS:
-        if step[0] in ("Ls1b", "Ls2"):
-            scales(step[0])
-        else:
-            a(step)
-    for step in HEAD:
-        a(step)
-    a(("P", 1, 0)); a(("P", 1, 1)); a(("Ps", 1)); a(("P", 2, 0)); a(("P", 2, 1)); a(("Ps", 2))
-    for s in range(12):
-        done = Z.get(s - 1, [])
-        if s == 1:
-            a(("P", 3, 0)); a(("P", 3, 1))
-        for x in QU_FIRST.get(s, []):
-            a(("Qu", x, 2))
-        if s >= 1:
-            a(("I", s - 1, 0))
-        for j in done:
-            a(("S", j))
-        for x in QU_MID.get(s, []):
-            a(("Qu", x, 2))
-        for x in PRE.get(s, []):
-            a(("pre", x))
-        if s == 1:
-            a(("Ps", 3))
-        if s >= 1:
-            a(("Qh", s - 1, 0))
-        for j in done:
-            a(("Y", j)); a(("Sty", j))
-        for x in QU_LAST.get(s, []):
-            a(("Qu", x, 2))
-        for x in C.get(s, []):
-            a(("C", x))
-        for x in QY.get(s, []):
-            a(("Qy", x, 2))
-            if x == 2:
-                planes(0, 4)
-        for t in range(4):
-            a(("S1b", t) if (s == 0 and HALVES) else ("S1", s, t)); a(("Eh", s, t))
-        for x in TU.get(s, []):
-            a(("Tu", x))
-        if s == VECTORS_AFTER:
-            a(("Tv",))
-        for x in TY.get(s, []):
-            a(("Ty", x, 2))
-        for x in TU.get(s, []):
-            a(("Eu", x))
-        if s == VECTORS_AFTER:
-            a(("Ev",))
-        for j in CAST.get(s, []):
-            a(("cast", j))
-        for x in TY.get(s, []):
-            a(("Ey", x, 2))
-        for j in Z.get(s, []):
-            for g in range(4):
-                a(("S2", j, g))
-    def z(j, first=0, last=4):
-        for g in range(first, last):
-            a(("S2", j, g))
-    a(("I", 11, 0)); a(("IA", 11, 1))
-    for j in CAST.get(12, []):
-        a(("cast", j))
-    a(("S", 7)); a(("Qh", 11, 0)); a(("Y", 7)); a(("Sty", 7)); a(("Qh", 11, 1)); a(("cast", 7))
-    z(8, 0, 3); z(9, 0, 3); z(8, 3); z(9, 3); z(10); z(11)
-    a(("Ty", 4, 2)); a(("Ty", 6, 2))
-    a(("S", 8)); a(("S", 9)); a(("Y", 8)); a(("Sty", 8)); a(("cast", 8)); a(("Y", 9)); a(("Sty", 9)); a(("cast", 9)); a(("Ey", 4, 2)); a(("Ey", 6, 2))
-    a(("Ty", 8, 2))
-    a(("S", 10)); a(("S", 11)); a(("Y", 10)); a(("Sty", 10)); a(("cast", 10)); a(("Ey", 8, 2))
-    a(("Yb", 11)); a(("Qy", 4, 4)); a(("Stc", 4, 4)); a(("Y", 11)); a(("Sty", 11))
-    a(("Qy", 8, 2)); a(("Stc", 8, 2))
-    a(("Ty", 10, 1)); a(("Ey", 10, 1)); a(("Qy", 10, 1)); a(("Ty", 11, 1)); a(("Ey", 11, 1)); a(("Qy", 11, 1)); a(("Stc", 10, 2))
-    for q in range(4):
-        a(("Sts", 4, 8, q))
-    return L
+SLOTS = [(4 * c, 4, fg) for c in range(CHUNKS) for fg in range(FG)][:10] + [(8, 2, 2), (8, 2, 3), (10, 2, 2), (10, 2, 3)]
+PAIRED = (5, 7, 9)
+HEAD_EXTRA = []
+TU_AFTER = {1: [(2, 0), (2, 1), (3, 0), (3, 1)], 5: [(4, 0), (4, 1), (5, 0), (5, 1)]}
+EU_ACT = TU_AFTER
+Z_AFTER = {5: [0], 6: [1], 7: [2, 3], 8: [4], 9: [5], 10: [6], 11: [7], 12: [8]}
+PRE = {0: [("P", 1), ("P", 2), ("O", 3, 0), ("O", 3, 1)], 6: [("S", 0), ("C", 5)], 7: [("S", 1), ("Q", 5, 0), ("Q", 5, 1), ("W", 1), ("C", 6)],
+       8: [("S", 2), ("C", 7), ("W", 2), ("S", 3)], 10: [("S", 5), ("C", 11)]}
+MID = {1: [("P", 3)], 2: [("Q", 2, 0), ("Q", 2, 1)], 3: [("C", 2)], 4: [("C", 3)], 5: [("C", 4)], 6: [("W", 0)], 7: [("C", 8)], 8: [("W", 3)], 9: [("S", 4)], 10: [("W", 5)],
+       11: [("S", 6)], 12: [("S", 7)], 13: [("S", 8)]}
+END = {2: [("Q", 3, 0), ("Q", 3, 1), ("O", 4, 0), ("O", 4, 1), ("C", 0), ("O", 5, 0), ("O", 5, 1), ("C", 1)], 6: [("Q", 4, 0), ("Q", 4, 1)],
+       8: [("C", 9)], 9: [("W", 4), ("C", 10)], 11: [("W", 6)], 12: [("W", 7), ("Y", 0)], 13: [("W", 8), ("Y", 2)]}
+TAIL0 = []
+TAIL1 = [("S", 9)]
+TAIL2 = [("W", 9), ("Y", 4)]
+TY_AFTER = {11: [0, 2, 4]}
+EY_AFTER = {11: [0, 2], 12: [4]}
+CAST_AFTER = {6: [0], 7: [1], 8: [2, 3], 9: [4], 10: [5]}
+CAST_LATE = {11: [6], 12: [7]}
+SORT_ACT = {-1: [(2, 0), (2, 1)]}
+VEC_AFTER = 1
 
 
 def tile_user_tower_for_scoring_h1_kernel(
@@ -149,16 +62,16 @@ def tile_user_tower_for_scoring_h1_kernel(
         def tiles(name, count, shape, dtype, align=64):
             return [sb.tile(shape, dtype, name="%s%d" % (name, n), align_bytes=align) for n in range(count)]
 
-        banks = [ps.tile([P, 512], F32, name="bank%d" % n) for n in range(MX_BANKS + T_BANKS)]
+        banks = [ps.tile([P, 512], F32, name="bank%d" % n) for n in range(BANKS)]
         ident = sb.tile([P, P], F32, name="ident", align_bytes=64)
-        u_raw = [None] * 4 + tiles("u_raw", TILES - 4, [P, K], BF16)
-        u_head = tiles("u_head", 4, [P, 2, 512], BF16)
-        w1_raw = tiles("w1_raw", FG, [P, KG, 1024], U8)
-        w1_perm = tiles("w1_perm", FG, [P, KG, 1024], U8, 256)
-        s1_raw = sb.tile([P, KG, F], U8, name="s1_raw", align_bytes=64)
+        u_raw = tiles("u_raw", PAIRS * KG, [P, 2, 512], BF16)
+        u_sorted = tiles("u_sorted", 4, [P, 2, 2, P], F32)
+        w1_raw = tiles("w1_raw", FG * KG, [P, 1024], U8)
+        w1_perm = tiles("w1_perm", FG * KG, [P, 1024], U8, 256)
+        s1_first = sb.tile([P, KG, 512], U8, name="s1_first", align_bytes=64)
+        s1_rest = sb.tile([P, KG, F - 512], U8, name="s1_rest", align_bytes=64)
         s1_perm = tiles("s1_perm", FG, [P, KG, 512], U8, 256)
-        b1_raw = sb.tile([P, FG, 4], BF16, name="b1_raw", align_bytes=64)
-        act_warm = sb.tile([P, 1], F32, name="act_warm", align_bytes=64)
+        b1_col = sb.tile([P, FG, 4], BF16, name="b1_col", align_bytes=64)
         w2 = sb.tile([P, FG, 1024], U8, name="w2", align_bytes=256)
         s2 = sb.tile([P, FG, D], U8, name="s2", align_bytes=256)
         b2_col = sb.tile([P, 4], BF16, name="b2_col", align_bytes=64)
@@ -167,46 +80,41 @@ def tile_user_tower_for_scoring_h1_kernel(
         b2_all = vec_all[:, 0, :]
         dw_all = vec_all[:, 1, :]
         uf = tiles("uf", CHUNKS, [P, 4, D], BF16)
-        x_t = tiles("x_t", 2, [P, KG, 512, 4], BF16)
-        x_codes = tiles("x_codes", CHUNKS, [P, KG, 512], U32, 256)
-        x_scales = tiles("x_scales", CHUNKS, [P, KG, 512], U8, 256)
-        h_rows = tiles("h_rows", H_RING, [P, 4, 512], BF16)
-        h_words = tiles("h_words", H_RING, [P, 512, 4], BF16)
-        h_codes = tiles("h_codes", SLOTS, [P, 512], U32, 256)
-        h_scales = tiles("h_scales", SLOTS, [P, 512], U8, 256)
+        x_t = tiles("x_t", X_RING, [P, 1024], BF16)
+        x_codes = tiles("x_codes", CHUNKS * KG, [P, 512], U32, 256)
+        x_scales = tiles("x_scales", CHUNKS * KG, [P, 512], U8, 256)
+        h_rows = tiles("h_rows", H_RING, [P, 2048], BF16)
+        h_words = tiles("h_words", H_RING, [P, 2048], BF16)
+        h_codes = tiles("h_codes", CHUNKS * FG, [P, 512], U32, 256)
+        h_scales = tiles("h_scales", CHUNKS * FG, [P, 512], U8, 256)
         y = tiles("y", TILES, [P, D], F32)
         y_bf = tiles("y_bf", TILES, [P, D], BF16)
-        y_t = sb.tile([P, M, 4], BF16, name="y_t", align_bytes=64)
+        y_t = sb.tile([P, TILES * 512], BF16, name="y_t", align_bytes=64)
         y_codes = sb.tile([P, M], U32, name="y_codes", align_bytes=64)
         y_scales = sb.tile([P, M], U8, name="y_scales", align_bytes=64)
 
-        warm_in = sb.tile([P, 512], BF16, name="warm_in", align_bytes=64) if USE_WARM else None
-        warm_codes = sb.tile([P, P], U32, name="warm_codes", align_bytes=64) if USE_WARM else None
-        warm_scales = sb.tile([P, P], U8, name="warm_scales", align_bytes=64) if USE_WARM else None
-        mx_used = []
-        t_used = []
+        taken = []
         held = {}
+        x_home = {}
+        sorted_home = {}
 
-        def mx_bank(key):
-            held[key] = banks[len(mx_used) % MX_BANKS]
-            mx_used.append(key)
+        def next_bank(key):
+            held[key] = banks[len(taken) % BANKS]
+            taken.append(key)
             return held[key]
 
-        def t_bank(key):
-            held[key] = banks[MX_BANKS + len(t_used) % T_BANKS]
-            t_used.append(key)
-            return held[key]
+        def load_users(pair, g):
+            src = users[pair * 256 : (pair + 1) * 256, g * 512 : (g + 1) * 512].rearrange("(i p) k -> p i k", p=P)
+            nc.sync.dma_start(out=u_raw[pair * KG + g][:], in_=src)
 
-        def load_users(j):
-            nc.sync.dma_start(out=u_raw[j][:], in_=users[j * P : (j + 1) * P, :])
+        def load_w1(fg, g):
+            src = w1_words[g, :, fg * 1024 : (fg + 1) * 1024]
+            nc.sync.dma_start(out=w1_raw[fg * KG + g][:].bitcast(I32), in_=src.bitcast(I32))
 
-        def load_w1(fg):
-            src = w1_words[:, :, fg * 1024 : (fg + 1) * 1024].rearrange("g p n -> p g n")
-            nc.sync.dma_start(out=w1_raw[fg][:].bitcast(I32), in_=src.bitcast(I32))
-
-        def load_scale_rows(plane, rows, cols, q):
-            src = rows[:, q:16:4, cols].rearrange("g r n -> r g n")
-            nc.sync.dma_start(out=plane[q:P:32, :, cols].bitcast(I32), in_=src.bitcast(I32))
+        def load_scale_rows(plane, rows):
+            for q in range(4):
+                src = rows[:, q:16:4, :].rearrange("g r n -> r g n")
+                nc.sync.dma_start(out=plane[q:P:32, :, :].bitcast(I32), in_=src.bitcast(I32))
 
         def load_user_free(c):
             src = user_free[c * 512 : (c + 1) * 512, :].rearrange("(i p) d -> p i d", p=P)
@@ -214,100 +122,112 @@ def tile_user_tower_for_scoring_h1_kernel(
 
         def permute_w1_codes(fg, g):
             nc.vector.tensor_copy(
-                out=w1_perm[fg][:, g, :].rearrange("p (t m b) -> p t m b", t=4, b=2),
-                in_=w1_raw[fg][:, g, :].rearrange("p (m t b) -> p t m b", t=4, b=2),
+                out=w1_perm[fg * KG + g][:].bitcast(U16).rearrange("p (t m) -> p t m", t=4),
+                in_=w1_raw[fg * KG + g][:].bitcast(U16).rearrange("p (m t) -> p t m", t=4),
             )
 
         def permute_w1_scales(fg):
+            src = s1_first[:] if fg == 0 else s1_rest[:, :, (fg - 1) * 512 : fg * 512]
             nc.vector.tensor_copy(
                 out=s1_perm[fg][:].rearrange("p g (t m) -> p g t m", t=4),
-                in_=s1_raw[:, :, fg * 512 : (fg + 1) * 512].rearrange("p g (m t) -> p g t m", t=4),
+                in_=src.rearrange("p g (m t) -> p g t m", t=4),
             )
 
-        def transpose_users(j):
-            bank = t_bank(("u", j))
-            words = u_raw[j][:].bitcast(F32)
-            for g in range(KG):
+        def sort_users(pair, g, copy=nc.vector.tensor_copy):
+            sorted_home[(pair, g)] = u_sorted[len(sorted_home) % 4]
+            copy(
+                out=sorted_home[(pair, g)][:],
+                in_=u_raw[pair * KG + g][:].bitcast(F32).rearrange("p i (q u) -> p i u q", u=2),
+            )
+
+        def transpose_users(pair, g):
+            bank = next_bank(("u", pair, g))
+            words = u_raw[pair * KG + g][:].bitcast(F32)
+            for i in range(2):
                 for u in range(2):
-                    col = (2 * g + u) * P
-                    nc.tensor.transpose(bank[:, col : col + P], words[:, 256 * g + u : 256 * (g + 1) : 2], ident[:])
+                    col = (2 * i + u) * P
+                    src = sorted_home[(pair, g)][:, i, u, :] if (pair, g) in sorted_home else words[:, i, u:256:2]
+                    nc.tensor.transpose(bank[:, col : col + P], src, ident[:])
 
-        def evacuate_users(j):
-            c, i = divmod(j, 4)
-            nc.scalar.copy(
-                out=x_t[c % 2][:, :, i * P : (i + 1) * P, :].bitcast(F32),
-                in_=held[("u", j)][:].rearrange("p (g u m) -> p g m u", g=KG, u=2),
+        def evacuate_users(pair, g, copy=nc.scalar.copy):
+            x_home[(pair, g)] = x_t[len(x_home) % X_RING]
+            copy(
+                out=x_home[(pair, g)][:].bitcast(F32).rearrange("p (i m u) -> p i m u", i=2, u=2),
+                in_=held[("u", pair, g)][:].rearrange("p (i u m) -> p i m u", i=2, u=2),
             )
 
-        def quantize_users(j, count):
-            c, i = divmod(j, 4)
-            cols = slice(i * P, (i + count) * P)
-            for g in range(KG):
-                nc.vector.quantize_mx(
-                    out=x_codes[c][:, g, cols].bitcast(FP8X4),
-                    scales=x_scales[c][:, g, cols],
-                    in_=x_t[c % 2][:, g, cols, :].rearrange("p m t -> p (m t)"),
-                )
+        def quantize_users(pair, g):
+            c, half = divmod(pair, 2)
+            cols = slice(half * 256, (half + 1) * 256)
+            nc.vector.quantize_mx(
+                out=x_codes[c * KG + g][:, cols].bitcast(FP8X4),
+                scales=x_scales[c * KG + g][:, cols],
+                in_=x_home[(pair, g)][:],
+            )
 
-        def hidden_matmul(s, t):
-            c, fg = divmod(s, FG)
-            bank = mx_bank(("h", s, t))
-            for g in range(KG):
-                nc.tensor.matmul_mx(
-                    out=bank[:],
-                    lhsT=w1_perm[fg][:, g, t * 256 : (t + 1) * 256].bitcast(FP4X4),
-                    lhsT_scale=s1_perm[fg][:, g, t * P : (t + 1) * P],
-                    rhs=x_codes[c][:, g, :].bitcast(FP8X4),
-                    rhs_scale=x_scales[c][:, g, :],
-                    start=(g == 0),
-                    stop=(g == KG - 1),
-                )
+        def slot_cols(s):
+            first, count, fg = SLOTS[s]
+            return slice(first % 4 * P, (first % 4 + count) * P)
+
+        def hidden_pass(s, t, g):
+            first, count, fg = SLOTS[s]
+            bank = next_bank(("h", s, t)) if g == 0 else held[("h", s, t)]
+            nc.tensor.matmul_mx(
+                out=bank[:, : count * P],
+                lhsT=w1_perm[fg * KG + g][:, t * 256 : (t + 1) * 256].bitcast(FP4X4),
+                lhsT_scale=s1_perm[fg][:, g, t * P : (t + 1) * P],
+                rhs=x_codes[first // 4 * KG + g][:, slot_cols(s)].bitcast(FP8X4),
+                rhs_scale=x_scales[first // 4 * KG + g][:, slot_cols(s)],
+                start=(g == 0),
+                stop=(g == KG - 1),
+            )
 
         def evacuate_hidden(s, t):
-            fg = s % FG
-            rows = h_rows[s % H_RING]
+            first, count, fg = SLOTS[s]
+            n = count * P
+            rows = h_rows[s % H_RING][:, : 4 * n]
             if s in PAIRED:
-                dst = rows[:].rearrange("p t m -> p (t m)").rearrange("p (u m e) -> p u m e", u=2, e=2)[:, t // 2, :, t % 2]
+                dst = rows.rearrange("p (u m e) -> p u m e", u=2, e=2)[:, t // 2, :, t % 2]
             else:
-                dst = rows[:, t, :]
-            nc.scalar.activation(out=dst, in_=held[("h", s, t)][:], func=ACT.Relu, bias=b1_raw[:, fg, t : t + 1])
+                dst = rows[:, t * n : (t + 1) * n]
+            nc.scalar.activation(out=dst, in_=held[("h", s, t)][:, :n], func=ACT.Relu, bias=b1_col[:, fg, t : t + 1])
 
-        def part_cols(s, h):
-            width = 512 // SPLIT.get(s, 1)
-            return slice(h * width, (h + 1) * width)
-
-        def interleave_hidden(s, h, copy):
-            cols = part_cols(s, h)
+        def interleave_hidden(s):
+            n = SLOTS[s][1] * P
+            rows = h_rows[s % H_RING][:, : 4 * n]
+            words = h_words[s % H_RING][:, : 4 * n]
             if s in PAIRED:
-                src = h_rows[s % H_RING][:].rearrange("p t m -> p (t m)").bitcast(F32).rearrange("p (u m) -> p m u", u=2)
-                copy(out=h_words[s % H_RING][:, cols, :].bitcast(F32), in_=src[:, cols, :])
+                nc.vector.tensor_copy(
+                    out=words.bitcast(F32).rearrange("p (m u) -> p m u", u=2),
+                    in_=rows.bitcast(F32).rearrange("p (u m) -> p m u", u=2),
+                )
             else:
-                copy(
-                    out=h_words[s % H_RING][:, cols, :].rearrange("p (c i) t -> p c t i", i=4),
-                    in_=h_rows[s % H_RING][:, :, cols].rearrange("p t (c i) -> p c t i", i=4),
+                nc.vector.tensor_copy(
+                    out=words.rearrange("p (c i t) -> p c t i", i=4, t=4),
+                    in_=rows.rearrange("p (t c i) -> p c t i", i=4, t=4),
                 )
 
-        def quantize_hidden(s, h):
-            cols = part_cols(s, h)
+        def quantize_hidden(s):
+            first, count, fg = SLOTS[s]
             nc.vector.quantize_mx(
-                out=h_codes[s][:, cols].bitcast(FP8X4),
-                scales=h_scales[s][:, cols],
-                in_=h_words[s % H_RING][:, cols, :].rearrange("p m t -> p (m t)"),
+                out=h_codes[first // 4 * FG + fg][:, slot_cols(s)].bitcast(FP8X4),
+                scales=h_scales[first // 4 * FG + fg][:, slot_cols(s)],
+                in_=h_words[s % H_RING][:, : 4 * count * P],
             )
 
-        def output_pass(j, fg):
+        def output_passes(j, first=0, last=FG):
             c, i = divmod(j, 4)
-            bank = mx_bank(("z", j)) if fg == 0 else held[("z", j)]
-            s = c * FG + fg
-            nc.tensor.matmul_mx(
-                out=bank[:],
-                lhsT=h_codes[s][:, i * P : (i + 1) * P].bitcast(FP8X4),
-                lhsT_scale=h_scales[s][:, i * P : (i + 1) * P],
-                rhs=w2[:, fg, :].bitcast(FP4X4),
-                rhs_scale=s2[:, fg, :],
-                start=(fg == 0),
-                stop=(fg == FG - 1),
-            )
+            for fg in range(first, last):
+                bank = next_bank(("z", j)) if fg == 0 else held[("z", j)]
+                nc.tensor.matmul_mx(
+                    out=bank[:],
+                    lhsT=h_codes[c * FG + fg][:, i * P : (i + 1) * P].bitcast(FP8X4),
+                    lhsT_scale=h_scales[c * FG + fg][:, i * P : (i + 1) * P],
+                    rhs=w2[:, fg, :].bitcast(FP4X4),
+                    rhs_scale=s2[:, fg, :],
+                    start=(fg == 0),
+                    stop=(fg == FG - 1),
+                )
 
         def add_free_and_bias(j):
             c, i = divmod(j, 4)
@@ -316,8 +236,9 @@ def tile_user_tower_for_scoring_h1_kernel(
         def add_product(j):
             nc.vector.tensor_tensor(out=y[j][:], in0=held[("z", j)][:], in1=y[j][:], op=ALU.add)
 
-        def weight(j):
+        def weight_and_store(j):
             nc.vector.tensor_tensor(out=y[j][:], in0=y[j][:], in1=dw_all, op=ALU.mult)
+            nc.sync.dma_start(out=out_0[j * P : (j + 1) * P, :], in_=y[j][:])
 
         def weight_rounded(j):
             nc.vector.tensor_tensor(
@@ -327,9 +248,6 @@ def tile_user_tower_for_scoring_h1_kernel(
                 op=ALU.mult,
             )
 
-        def store_output(j):
-            nc.sync.dma_start(out=out_0[j * P : (j + 1) * P, :], in_=y[j][:])
-
         def round_output(j):
             nc.scalar.copy(
                 out=y_bf[j][:].rearrange("p (u q e) -> p u q e", u=2, e=2),
@@ -337,101 +255,39 @@ def tile_user_tower_for_scoring_h1_kernel(
             )
 
         def transpose_output(j, count):
-            bank = t_bank(("y", j))
+            bank = next_bank(("y", j))
             for x in range(count):
                 words = y_bf[j + x][:].bitcast(F32)
                 for u in range(2):
                     col = (2 * x + u) * P
                     nc.tensor.transpose(bank[:, col : col + P], words[:, u * P : (u + 1) * P], ident[:])
 
+        def turned(j, count):
+            return y_t[:, j * 512 : (j + count) * 512]
+
         def evacuate_output(j, count):
             nc.scalar.copy(
-                out=y_t[:, j * P : (j + count) * P, :].bitcast(F32).rearrange("p (x m) u -> p x m u", x=count),
+                out=turned(j, count).bitcast(F32).rearrange("p (x m u) -> p x m u", x=count, u=2),
                 in_=held[("y", j)][:, : count * 256].rearrange("p (x u m) -> p x m u", x=count, u=2),
             )
 
         def quantize_output(j, count):
             cols = slice(j * P, (j + count) * P)
-            nc.vector.quantize_mx(
-                out=y_codes[:, cols].bitcast(FP8X4),
-                scales=y_scales[:, cols],
-                in_=y_t[:, cols, :].rearrange("p m t -> p (m t)"),
-            )
+            nc.vector.quantize_mx(out=y_codes[:, cols].bitcast(FP8X4), scales=y_scales[:, cols], in_=turned(j, count))
 
         def store_codes(j, count):
-            cols = slice(j * P, (j + count) * P)
             dst = out_1[0].rearrange("p m t -> p (m t)")[:, 4 * j * P : 4 * (j + count) * P]
-            nc.sync.dma_start(out=dst.bitcast(I32), in_=y_codes[:, cols].bitcast(I32))
+            nc.sync.dma_start(out=dst.bitcast(I32), in_=y_codes[:, j * P : (j + count) * P].bitcast(I32))
 
-        def store_scales(j, count, q):
+        def store_scales(j, count, queues):
             cols = slice(j * P, (j + count) * P)
-            queue = nc.scalar if (j >= 4 and q % 2 == 1) else nc.sync
-            queue.dma_start(
-                out=out_2[0][q:16:4, cols].bitcast(I32),
-                in_=y_scales[q:P:32, cols].bitcast(I32),
-            )
-
-        def warm_source():
-            nc.vector.memset(warm_in[:], 0.0)
-
-        def warm_quantize():
-            nc.vector.quantize_mx(out=warm_codes[:].bitcast(FP8X4), scales=warm_scales[:], in_=warm_in[:])
-
-        def warm_pass(n, count):
-            for x in range(count):
-                nc.tensor.matmul_mx(
-                    out=banks[MX_BANKS - 1][:, :P],
-                    lhsT=warm_codes[:, :64].bitcast(FP4X4),
-                    lhsT_scale=warm_scales[:],
-                    rhs=warm_codes[:].bitcast(FP8X4),
-                    rhs_scale=warm_scales[:],
-                    start=True,
-                    stop=True,
+            for q in range(4):
+                queues[q % len(queues)].dma_start(
+                    out=out_2[0][q:16:4, cols].bitcast(I32), in_=y_scales[q:P:32, cols].bitcast(I32)
                 )
 
-        def load_users_half(g, pair):
-            src = users[pair * 256 : (pair + 1) * 256, g * 512 : (g + 1) * 512].rearrange("(i p) k -> p i k", p=P)
-            nc.sync.dma_start(out=u_head[2 * g + pair][:], in_=src)
-
-        def transpose_users_half(g, pair):
-            bank = t_bank(("uh", g, pair))
-            words = u_head[2 * g + pair][:].bitcast(F32)
-            for i in range(2):
-                for u in range(2):
-                    col = (2 * i + u) * P
-                    nc.tensor.transpose(bank[:, col : col + P], words[:, i, u:256:2], ident[:])
-
-        def evacuate_users_half(g, pair):
-            nc.scalar.copy(
-                out=x_t[0][:, g, pair * 256 : (pair + 1) * 256, :].bitcast(F32).rearrange("p (i m) u -> p i m u", i=2),
-                in_=held[("uh", g, pair)][:].rearrange("p (i u m) -> p i m u", i=2, u=2),
-            )
-
-        def quantize_users_half(g, pair):
-            cols = slice(pair * 256, (pair + 1) * 256)
-            nc.vector.quantize_mx(
-                out=x_codes[0][:, g, cols].bitcast(FP8X4),
-                scales=x_scales[0][:, g, cols],
-                in_=x_t[0][:, g, cols, :].rearrange("p m t -> p (m t)"),
-            )
-
-        def hidden_first_pass(t, g):
-            bank = mx_bank(("h", 0, t)) if g == 0 else held[("h", 0, t)]
-            nc.tensor.matmul_mx(
-                out=bank[:],
-                lhsT=w1_perm[0][:, g, t * 256 : (t + 1) * 256].bitcast(FP4X4),
-                lhsT_scale=s1_perm[0][:, g, t * P : (t + 1) * P],
-                rhs=x_codes[0][:, g, :].bitcast(FP8X4),
-                rhs_scale=x_scales[0][:, g, :],
-                start=(g == 0),
-                stop=(g == KG - 1),
-            )
-
-        def load_w1_half(g):
-            nc.sync.dma_start(out=w1_raw[0][:, g, :].bitcast(I32), in_=w1_words[g, :, 0:1024].bitcast(I32))
-
         def transpose_vectors():
-            bank = t_bank(("v",))
+            bank = next_bank(("v",))
             for v, col in enumerate((b2_col, dw_col)):
                 words = col[:].bitcast(F32)
                 for u in range(2):
@@ -444,58 +300,141 @@ def tile_user_tower_for_scoring_h1_kernel(
                 in_=held[("v",)][:].rearrange("m (v u q) -> m v q u", v=2, u=2),
             )
 
-        steps = {
-            "ms1a": lambda: nc.vector.memset(s1_raw[:, :, 0:512].bitcast(I32), 0),
-            "ms1": lambda: nc.vector.memset(s1_raw[:, :, 512:F].bitcast(I32), 0),
-            "ident": lambda: make_identity(nc, ident[:]),
-            "ms2": lambda: nc.vector.memset(s2[:].bitcast(I32), 0),
-            "Lu": load_users,
-            "Lw1": load_w1,
-            "Lb1": lambda: nc.sync.dma_start(out=b1_raw[:], in_=b1.rearrange("(g p t) -> p g t", p=P, t=4)),
-            "Ls1a": lambda q: load_scale_rows(s1_raw, w1_scales, slice(0, 512), q),
-            "Ls1b": lambda q: load_scale_rows(s1_raw, w1_scales, slice(512, F), q),
-            "Ls2": lambda q: load_scale_rows(s2, w2_scales, slice(0, D), q),
-            "Lw2": lambda: nc.sync.dma_start(
-                out=w2[:].bitcast(I32), in_=w2_words.rearrange("g p n -> p g n").bitcast(I32)
-            ),
-            "Lb2": lambda: nc.sync.dma_start(out=b2_col[:], in_=b2.rearrange("(p t) -> p t", t=4)),
-            "Ldw": lambda: nc.sync.dma_start(out=dw_col[:], in_=dim_weight.rearrange("(p t) -> p t", t=4)),
-            "Luf": load_user_free,
-            "warm": lambda: nc.scalar.activation(out=act_warm[:], in_=warm_in[:, 0:1], func=ACT.Relu),
-            "Tu": transpose_users,
-            "Eu": evacuate_users,
-            "Qu": quantize_users,
-            "P": permute_w1_codes,
-            "Ps": permute_w1_scales,
-            "S1": hidden_matmul,
-            "Eh": evacuate_hidden,
-            "I": lambda s, h: interleave_hidden(s, h, nc.vector.tensor_copy),
-            "IA": lambda s, h: interleave_hidden(s, h, nc.scalar.copy),
-            "Qh": quantize_hidden,
-            "S2": output_pass,
-            "C": add_free_and_bias,
-            "S": add_product,
-            "Y": weight,
-            "Yb": weight_rounded,
-            "Sty": store_output,
-            "cast": round_output,
-            "Ty": transpose_output,
-            "Ey": evacuate_output,
-            "Qy": quantize_output,
-            "Stc": store_codes,
-            "Sts": store_scales,
-            "Wm": warm_source,
-            "Wq": warm_quantize,
-            "W": warm_pass,
-            "Lw1h": load_w1_half,
-            "Lug": load_users_half,
-            "Tug": transpose_users_half,
-            "Eug": evacuate_users_half,
-            "Qug": quantize_users_half,
-            "S1a": lambda t: hidden_first_pass(t, 0),
-            "S1b": lambda t: hidden_first_pass(t, 1),
-            "Tv": transpose_vectors,
-            "Ev": evacuate_vectors,
-        }
-        for step in order():
-            steps[step[0]](*step[1:])
+        make_identity(nc, ident[:])
+        nc.vector.memset(s1_first[:].bitcast(I32), 0)
+        nc.vector.memset(s1_rest[:].bitcast(I32), 0)
+        nc.vector.memset(s2[:].bitcast(I32), 0)
+
+        load_users(0, 0)
+        load_users(1, 0)
+        load_w1(0, 0)
+        load_scale_rows(s1_first, w1_scales[:, :, :512])
+        load_users(0, 1)
+        load_users(1, 1)
+        load_w1(0, 1)
+        nc.sync.dma_start(out=b1_col[:], in_=b1.rearrange("(g p t) -> p g t", p=P, t=4))
+        nc.sync.dma_start(out=b2_col[:], in_=b2.rearrange("(p t) -> p t", t=4))
+        nc.sync.dma_start(out=dw_col[:], in_=dim_weight.rearrange("(p t) -> p t", t=4))
+        load_users(2, 0)
+        load_users(2, 1)
+        load_w1(1, 0)
+        load_w1(1, 1)
+        load_scale_rows(s1_rest, w1_scales[:, :, 512:])
+        load_w1(2, 0)
+        load_w1(2, 1)
+        load_users(3, 0)
+        load_users(3, 1)
+        load_user_free(0)
+        load_w1(3, 0)
+        load_w1(3, 1)
+        load_user_free(1)
+        nc.sync.dma_start(out=w2[:].bitcast(I32), in_=w2_words.rearrange("g p n -> p g n").bitcast(I32))
+        load_scale_rows(s2, w2_scales)
+        for pair in (4, 5):
+            for g in range(KG):
+                load_users(pair, g)
+        load_user_free(2)
+
+        for g in range(KG):
+            for pair in range(2):
+                transpose_users(pair, g)
+                evacuate_users(pair, g)
+        permute_w1_codes(0, 0)
+        quantize_users(0, 0)
+        permute_w1_scales(0)
+        quantize_users(1, 0)
+        for t in range(4):
+            hidden_pass(0, t, 0)
+        quantize_users(0, 1)
+        permute_w1_codes(0, 1)
+        quantize_users(1, 1)
+        if VEC_AFTER < 0:
+            transpose_vectors()
+            evacuate_vectors()
+        for unit in SORT_ACT.get(-1, []):
+            sort_users(*unit, nc.scalar.copy)
+        for unit in HEAD_EXTRA:
+            transpose_users(*unit)
+            evacuate_users(*unit)
+
+        def permute_w1(fg):
+            for g in range(KG):
+                permute_w1_codes(fg, g)
+            permute_w1_scales(fg)
+
+        def planes(x):
+            quantize_output(x, 2)
+            if x == 2:
+                store_codes(0, 4)
+                store_scales(0, 4, [nc.sync])
+
+        extra = {"P": permute_w1, "Q": quantize_users, "C": add_free_and_bias, "Y": planes, "O": sort_users,
+                 "S": add_product, "W": weight_and_store,
+                 "E": lambda pair, g: evacuate_users(pair, g, nc.vector.tensor_copy)}
+
+        def extras(steps):
+            for step in steps:
+                extra[step[0]](*step[1:])
+
+        for s in range(len(SLOTS)):
+            extras(PRE.get(s, []))
+            if s >= 1:
+                interleave_hidden(s - 1)
+            extras(MID.get(s, []))
+            if s >= 1:
+                quantize_hidden(s - 1)
+            extras(END.get(s, []))
+            for t in range(4):
+                for g in range(KG):
+                    if s > 0 or g > 0:
+                        hidden_pass(s, t, g)
+                evacuate_hidden(s, t)
+            for x in CAST_AFTER.get(s, []):
+                round_output(x)
+            for unit in TU_AFTER.get(s, []):
+                transpose_users(*unit)
+            if s == VEC_AFTER:
+                transpose_vectors()
+                evacuate_vectors()
+            for x in TY_AFTER.get(s, []):
+                transpose_output(x, 2)
+            for unit in EU_ACT.get(s, []):
+                evacuate_users(*unit)
+            for x in EY_AFTER.get(s, []):
+                evacuate_output(x, 2)
+            for x in CAST_LATE.get(s, []):
+                round_output(x)
+            for j in Z_AFTER.get(s, []):
+                output_passes(j)
+
+        last = len(SLOTS) - 1
+        extras(TAIL0)
+        interleave_hidden(last)
+        output_passes(9)
+        extras(TAIL1)
+        quantize_hidden(last)
+        extras(TAIL2)
+        round_output(8)
+        output_passes(10, 0, 3)
+        output_passes(11, 0, 3)
+        output_passes(10, 3)
+        output_passes(11, 3)
+        round_output(9)
+        transpose_output(6, 2)
+        transpose_output(8, 2)
+        evacuate_output(6, 2)
+        evacuate_output(8, 2)
+        add_product(10)
+        add_product(11)
+        weight_rounded(10)
+        weight_rounded(11)
+        for j in (10, 11):
+            transpose_output(j, 1)
+            evacuate_output(j, 1)
+        weight_and_store(10)
+        quantize_output(6, 4)
+        store_codes(4, 6)
+        weight_and_store(11)
+        quantize_output(10, 2)
+        store_codes(10, 2)
+        store_scales(4, 8, [nc.sync, nc.scalar])

@@ -23,31 +23,37 @@ FG = F // 512
 TILES = M // P
 PAIRS = TILES // 2
 CHUNKS = M // 512
-BANKS = 8
+BANKS = 7
 H_RING = 4
-X_RING = 6
+X_RING = 4
 
 SLOTS = [(4 * c, 4, fg) for c in range(CHUNKS) for fg in range(FG)][:10] + [(8, 2, 2), (8, 2, 3), (10, 2, 2), (10, 2, 3)]
-PAIRED = (5, 7, 9)
+PAIRED = ()
+POOL_COLS = 512
 HEAD_EXTRA = []
-TU_AFTER = {1: [(2, 0), (2, 1), (3, 0), (3, 1)], 5: [(4, 0), (4, 1), (5, 0), (5, 1)]}
+TU_AFTER = {0: [(2, 0), (3, 0)], 1: [(2, 1), (3, 1)], 4: [(4, 0), (5, 0)], 5: [(4, 1), (5, 1)]}
 EU_ACT = TU_AFTER
-Z_AFTER = {5: [0], 6: [1], 7: [2, 3], 8: [4], 9: [5], 10: [6], 11: [7], 12: [8]}
-PRE = {0: [("P", 1), ("P", 2), ("O", 3, 0), ("O", 3, 1)], 6: [("S", 0), ("C", 5)], 7: [("S", 1), ("Q", 5, 0), ("Q", 5, 1), ("W", 1), ("C", 6)],
-       8: [("S", 2), ("C", 7), ("W", 2), ("S", 3)], 10: [("S", 5), ("C", 11)]}
-MID = {1: [("P", 3)], 2: [("Q", 2, 0), ("Q", 2, 1)], 3: [("C", 2)], 4: [("C", 3)], 5: [("C", 4)], 6: [("W", 0)], 7: [("C", 8)], 8: [("W", 3)], 9: [("S", 4)], 10: [("W", 5)],
-       11: [("S", 6)], 12: [("S", 7)], 13: [("S", 8)]}
-END = {2: [("Q", 3, 0), ("Q", 3, 1), ("O", 4, 0), ("O", 4, 1), ("C", 0), ("O", 5, 0), ("O", 5, 1), ("C", 1)], 6: [("Q", 4, 0), ("Q", 4, 1)],
-       8: [("C", 9)], 9: [("W", 4), ("C", 10)], 11: [("W", 6)], 12: [("W", 7), ("Y", 0)], 13: [("W", 8), ("Y", 2)]}
+Z_AFTER = {s: [s - 4] for s in range(4, 13)}
+VEC = {s: [("I", s - 1), ("G", s - 4, s - 1), ("S", s - 5), ("W", s - 6), ("H", s - 1)] for s in range(6, 14)}
+VEC[0] = [("P", 1), ("P", 2), ("P", 3)]
+VEC[1] = [("I", 0), ("QC", 1, 0), ("H", 0), ("C", 0)]
+VEC[2] = [("I", 1), ("QC", 1, 1), ("H", 1), ("C", 4)]
+VEC[3] = [("I", 2), ("C", 8), ("H", 2)]
+VEC[4] = [("I", 3), ("H", 3), ("C", 10)]
+VEC[5] = [("I", 4), ("G", 1, 4), ("S", 0), ("C", 11), ("H", 4), ("QC", 2, 0)]
+VEC[6] = VEC[6] + [("QC", 2, 1)]
+VEC[8] = [("I", 7), ("S", 3), ("H", 7), ("W", 2)]
+VEC[12] = [("I", 11), ("S", 7), ("H", 11), ("W", 6), ("Y", 0, 4)]
+VEC[13] = [("W", 7), ("I", 12), ("G", 9, 12), ("S", 8), ("W", 8), ("H", 12)]
 TAIL0 = []
 TAIL1 = [("S", 9)]
-TAIL2 = [("W", 9), ("Y", 4)]
-TY_AFTER = {11: [0, 2, 4]}
+TAIL2 = [("W", 9), ("Y", 4, 2)]
+TY_AFTER = {11: [0, 2], 12: [4]}
 EY_AFTER = {11: [0, 2], 12: [4]}
-CAST_AFTER = {6: [0], 7: [1], 8: [2, 3], 9: [4], 10: [5]}
-CAST_LATE = {11: [6], 12: [7]}
-SORT_ACT = {-1: [(2, 0), (2, 1)]}
-VEC_AFTER = 1
+CAST_AFTER = {6: [0], 7: [1], 8: [2], 9: [3], 10: [4]}
+CAST_LATE = {11: [5], 12: [6], 13: [7]}
+SORT_ACT = {}
+VEC_AFTER = 0
 
 
 def tile_user_tower_for_scoring_h1_kernel(
@@ -66,8 +72,9 @@ def tile_user_tower_for_scoring_h1_kernel(
         ident = sb.tile([P, P], F32, name="ident", align_bytes=64)
         u_raw = tiles("u_raw", PAIRS * KG, [P, 2, 512], BF16)
         u_sorted = tiles("u_sorted", 4, [P, 2, 2, P], F32)
-        w1_raw = tiles("w1_raw", FG * KG, [P, 1024], U8)
-        w1_perm = tiles("w1_perm", FG * KG, [P, 1024], U8, 256)
+        w1_first = tiles("w1_first", KG, [P, 1024], U8)
+        w1_raw = [None] + tiles("w1_raw", FG - 1, [P, KG, 1024], U8)
+        w1_perm = tiles("w1_perm", FG, [P, KG, 1024], U8, 256)
         s1_first = sb.tile([P, KG, 512], U8, name="s1_first", align_bytes=64)
         s1_rest = sb.tile([P, KG, F - 512], U8, name="s1_rest", align_bytes=64)
         s1_perm = tiles("s1_perm", FG, [P, KG, 512], U8, 256)
@@ -76,11 +83,12 @@ def tile_user_tower_for_scoring_h1_kernel(
         s2 = sb.tile([P, FG, D], U8, name="s2", align_bytes=256)
         b2_col = sb.tile([P, 4], BF16, name="b2_col", align_bytes=64)
         dw_col = sb.tile([P, 4], BF16, name="dw_col", align_bytes=64)
-        vec_all = sb.tile([P, 2, D], BF16, name="vec_all", align_bytes=64)
-        b2_all = vec_all[:, 0, :]
-        dw_all = vec_all[:, 1, :]
+        b2_all = sb.tile([P, D], BF16, name="b2_all", align_bytes=64)
+        vec_bank = ps.tile([P, 512], F32, name="vec_bank")
+        b2_psum = vec_bank[:].bitcast(BF16)[:, :D]
+        dw_all = vec_bank[:].bitcast(BF16)[:, D:]
         uf = tiles("uf", CHUNKS, [P, 4, D], BF16)
-        x_t = tiles("x_t", X_RING, [P, 1024], BF16)
+        x_t = tiles("x_t", X_RING, [P, 2048], BF16)
         x_codes = tiles("x_codes", CHUNKS * KG, [P, 512], U32, 256)
         x_scales = tiles("x_scales", CHUNKS * KG, [P, 512], U8, 256)
         h_rows = tiles("h_rows", H_RING, [P, 2048], BF16)
@@ -96,6 +104,7 @@ def tile_user_tower_for_scoring_h1_kernel(
         taken = []
         held = {}
         x_home = {}
+        addend = {}
         sorted_home = {}
 
         def next_bank(key):
@@ -107,9 +116,12 @@ def tile_user_tower_for_scoring_h1_kernel(
             src = users[pair * 256 : (pair + 1) * 256, g * 512 : (g + 1) * 512].rearrange("(i p) k -> p i k", p=P)
             nc.sync.dma_start(out=u_raw[pair * KG + g][:], in_=src)
 
-        def load_w1(fg, g):
-            src = w1_words[g, :, fg * 1024 : (fg + 1) * 1024]
-            nc.sync.dma_start(out=w1_raw[fg * KG + g][:].bitcast(I32), in_=src.bitcast(I32))
+        def load_w1_first(g):
+            nc.sync.dma_start(out=w1_first[g][:].bitcast(I32), in_=w1_words[g, :, :1024].bitcast(I32))
+
+        def load_w1(fg):
+            src = w1_words[:, :, fg * 1024 : (fg + 1) * 1024].rearrange("g p n -> p g n")
+            nc.sync.dma_start(out=w1_raw[fg][:].bitcast(I32), in_=src.bitcast(I32))
 
         def load_scale_rows(plane, rows):
             for q in range(4):
@@ -120,10 +132,16 @@ def tile_user_tower_for_scoring_h1_kernel(
             src = user_free[c * 512 : (c + 1) * 512, :].rearrange("(i p) d -> p i d", p=P)
             nc.sync.dma_start(out=uf[c][:], in_=src)
 
-        def permute_w1_codes(fg, g):
+        def permute_w1_first(g):
             nc.vector.tensor_copy(
-                out=w1_perm[fg * KG + g][:].bitcast(U16).rearrange("p (t m) -> p t m", t=4),
-                in_=w1_raw[fg * KG + g][:].bitcast(U16).rearrange("p (m t) -> p t m", t=4),
+                out=w1_perm[0][:, g, :].bitcast(U16).rearrange("p (t m) -> p t m", t=4),
+                in_=w1_first[g][:].bitcast(U16).rearrange("p (m t) -> p t m", t=4),
+            )
+
+        def permute_w1_codes(fg):
+            nc.vector.tensor_copy(
+                out=w1_perm[fg][:].bitcast(U16).rearrange("p g (t m) -> p g t m", t=4),
+                in_=w1_raw[fg][:].bitcast(U16).rearrange("p g (m t) -> p g t m", t=4),
             )
 
         def permute_w1_scales(fg):
@@ -150,9 +168,9 @@ def tile_user_tower_for_scoring_h1_kernel(
                     nc.tensor.transpose(bank[:, col : col + P], src, ident[:])
 
         def evacuate_users(pair, g, copy=nc.scalar.copy):
-            x_home[(pair, g)] = x_t[len(x_home) % X_RING]
+            x_home[(pair, g)] = x_t[(pair // 2 * KG + g) % X_RING][:, pair % 2 * 1024 : (pair % 2 + 1) * 1024]
             copy(
-                out=x_home[(pair, g)][:].bitcast(F32).rearrange("p (i m u) -> p i m u", i=2, u=2),
+                out=x_home[(pair, g)].bitcast(F32).rearrange("p (i m u) -> p i m u", i=2, u=2),
                 in_=held[("u", pair, g)][:].rearrange("p (i u m) -> p i m u", i=2, u=2),
             )
 
@@ -162,7 +180,12 @@ def tile_user_tower_for_scoring_h1_kernel(
             nc.vector.quantize_mx(
                 out=x_codes[c * KG + g][:, cols].bitcast(FP8X4),
                 scales=x_scales[c * KG + g][:, cols],
-                in_=x_home[(pair, g)][:],
+                in_=x_home[(pair, g)],
+            )
+
+        def quantize_chunk(c, g):
+            nc.vector.quantize_mx(
+                out=x_codes[c * KG + g][:].bitcast(FP8X4), scales=x_scales[c * KG + g][:], in_=x_t[(c * KG + g) % X_RING][:]
             )
 
         def slot_cols(s):
@@ -174,7 +197,7 @@ def tile_user_tower_for_scoring_h1_kernel(
             bank = next_bank(("h", s, t)) if g == 0 else held[("h", s, t)]
             nc.tensor.matmul_mx(
                 out=bank[:, : count * P],
-                lhsT=w1_perm[fg * KG + g][:, t * 256 : (t + 1) * 256].bitcast(FP4X4),
+                lhsT=w1_perm[fg][:, g, t * 256 : (t + 1) * 256].bitcast(FP4X4),
                 lhsT_scale=s1_perm[fg][:, g, t * P : (t + 1) * P],
                 rhs=x_codes[first // 4 * KG + g][:, slot_cols(s)].bitcast(FP8X4),
                 rhs_scale=x_scales[first // 4 * KG + g][:, slot_cols(s)],
@@ -231,10 +254,25 @@ def tile_user_tower_for_scoring_h1_kernel(
 
         def add_free_and_bias(j):
             c, i = divmod(j, 4)
-            nc.vector.tensor_tensor(out=y[j][:], in0=uf[c][:, i, :], in1=b2_all, op=ALU.add)
+            addend[j] = y[j][:]
+            nc.vector.tensor_tensor(out=addend[j], in0=uf[c][:, i, :], in1=b2_psum, op=ALU.add)
+
+        def add_on_gpsimd(j, s):
+            c, i = divmod(j, 4)
+            addend[j] = h_rows[s % H_RING][:].bitcast(F32)[:, :D]
+            nc.gpsimd.tensor_tensor(
+                out=addend[j][:, :POOL_COLS], in0=uf[c][:, i, :POOL_COLS], in1=b2_all[:, :POOL_COLS], op=ALU.add
+            )
+
+        def add_rest(j):
+            c, i = divmod(j, 4)
+            if POOL_COLS < D:
+                nc.vector.tensor_tensor(
+                    out=addend[j][:, POOL_COLS:], in0=uf[c][:, i, POOL_COLS:], in1=b2_psum[:, POOL_COLS:], op=ALU.add
+                )
 
         def add_product(j):
-            nc.vector.tensor_tensor(out=y[j][:], in0=held[("z", j)][:], in1=y[j][:], op=ALU.add)
+            nc.vector.tensor_tensor(out=y[j][:], in0=held[("z", j)][:], in1=addend[j], op=ALU.add)
 
         def weight_and_store(j):
             nc.vector.tensor_tensor(out=y[j][:], in0=y[j][:], in1=dw_all, op=ALU.mult)
@@ -287,18 +325,15 @@ def tile_user_tower_for_scoring_h1_kernel(
                 )
 
         def transpose_vectors():
-            bank = next_bank(("v",))
             for v, col in enumerate((b2_col, dw_col)):
                 words = col[:].bitcast(F32)
                 for u in range(2):
-                    at = (2 * v + u) * P
-                    nc.tensor.transpose(bank[:, at : at + P], words[:, u : u + 1].to_broadcast([P, P]), ident[:])
+                    nc.tensor.transpose(
+                        vec_bank[:, v * 256 + u : (v + 1) * 256 : 2], words[:, u : u + 1].to_broadcast([P, P]), ident[:]
+                    )
 
         def evacuate_vectors():
-            nc.scalar.copy(
-                out=vec_all[:].bitcast(F32).rearrange("m v (q u) -> m v q u", u=2),
-                in_=held[("v",)][:].rearrange("m (v u q) -> m v q u", v=2, u=2),
-            )
+            nc.scalar.copy(out=b2_all[:].bitcast(F32), in_=vec_bank[:, :256])
 
         make_identity(nc, ident[:])
         nc.vector.memset(s1_first[:].bitcast(I32), 0)
@@ -307,46 +342,42 @@ def tile_user_tower_for_scoring_h1_kernel(
 
         load_users(0, 0)
         load_users(1, 0)
-        load_w1(0, 0)
+        load_w1_first(0)
         load_scale_rows(s1_first, w1_scales[:, :, :512])
         load_users(0, 1)
         load_users(1, 1)
-        load_w1(0, 1)
+        load_w1_first(1)
         nc.sync.dma_start(out=b1_col[:], in_=b1.rearrange("(g p t) -> p g t", p=P, t=4))
         nc.sync.dma_start(out=b2_col[:], in_=b2.rearrange("(p t) -> p t", t=4))
         nc.sync.dma_start(out=dw_col[:], in_=dim_weight.rearrange("(p t) -> p t", t=4))
         load_users(2, 0)
-        load_users(2, 1)
-        load_w1(1, 0)
-        load_w1(1, 1)
-        load_scale_rows(s1_rest, w1_scales[:, :, 512:])
-        load_w1(2, 0)
-        load_w1(2, 1)
         load_users(3, 0)
+        load_w1(1)
+        load_scale_rows(s1_rest, w1_scales[:, :, 512:])
+        load_w1(2)
+        load_w1(3)
+        load_users(2, 1)
         load_users(3, 1)
-        load_user_free(0)
-        load_w1(3, 0)
-        load_w1(3, 1)
-        load_user_free(1)
+        for c in range(CHUNKS):
+            load_user_free(c)
         nc.sync.dma_start(out=w2[:].bitcast(I32), in_=w2_words.rearrange("g p n -> p g n").bitcast(I32))
         load_scale_rows(s2, w2_scales)
-        for pair in (4, 5):
-            for g in range(KG):
+        for g in range(KG):
+            for pair in (4, 5):
                 load_users(pair, g)
-        load_user_free(2)
 
         for g in range(KG):
             for pair in range(2):
                 transpose_users(pair, g)
                 evacuate_users(pair, g)
-        permute_w1_codes(0, 0)
+        permute_w1_first(0)
         quantize_users(0, 0)
         permute_w1_scales(0)
         quantize_users(1, 0)
         for t in range(4):
             hidden_pass(0, t, 0)
         quantize_users(0, 1)
-        permute_w1_codes(0, 1)
+        permute_w1_first(1)
         quantize_users(1, 1)
         if VEC_AFTER < 0:
             transpose_vectors()
@@ -358,18 +389,17 @@ def tile_user_tower_for_scoring_h1_kernel(
             evacuate_users(*unit)
 
         def permute_w1(fg):
-            for g in range(KG):
-                permute_w1_codes(fg, g)
+            permute_w1_codes(fg)
             permute_w1_scales(fg)
 
-        def planes(x):
-            quantize_output(x, 2)
-            if x == 2:
+        def planes(x, count):
+            quantize_output(x, count)
+            if x == 0:
                 store_codes(0, 4)
                 store_scales(0, 4, [nc.sync])
 
         extra = {"P": permute_w1, "Q": quantize_users, "C": add_free_and_bias, "Y": planes, "O": sort_users,
-                 "S": add_product, "W": weight_and_store,
+                 "S": add_product, "I": interleave_hidden, "H": quantize_hidden, "QC": quantize_chunk, "G": add_on_gpsimd, "R": add_rest, "A": round_output, "W": weight_and_store,
                  "E": lambda pair, g: evacuate_users(pair, g, nc.vector.tensor_copy)}
 
         def extras(steps):
@@ -377,13 +407,7 @@ def tile_user_tower_for_scoring_h1_kernel(
                 extra[step[0]](*step[1:])
 
         for s in range(len(SLOTS)):
-            extras(PRE.get(s, []))
-            if s >= 1:
-                interleave_hidden(s - 1)
-            extras(MID.get(s, []))
-            if s >= 1:
-                quantize_hidden(s - 1)
-            extras(END.get(s, []))
+            extras(VEC.get(s, []))
             for t in range(4):
                 for g in range(KG):
                     if s > 0 or g > 0:

@@ -29,29 +29,32 @@ X_RING = 4
 
 SLOTS = [(4 * c, 4, fg) for c in range(CHUNKS) for fg in range(FG)][:10] + [(8, 2, 2), (8, 2, 3), (10, 2, 2), (10, 2, 3)]
 PAIRED = ()
-POOL_COLS = 512
+POOL_COLS = 320
 HEAD_EXTRA = []
-TU_AFTER = {0: [(2, 0), (3, 0)], 1: [(2, 1), (3, 1)], 4: [(4, 0), (5, 0)], 5: [(4, 1), (5, 1)]}
+U1 = [(2, 0), (3, 0), (2, 1), (3, 1)]
+U2 = [(4, 0), (5, 0), (4, 1), (5, 1)]
+TU_AFTER = {0: U1[:2], 1: U1[2:], 4: U2}
 EU_ACT = TU_AFTER
 Z_AFTER = {s: [s - 4] for s in range(4, 13)}
-VEC = {s: [("I", s - 1), ("G", s - 4, s - 1), ("S", s - 5), ("W", s - 6), ("H", s - 1)] for s in range(6, 14)}
+VEC = {s: [("I", s - 1), ("G", s - 4, s - 1), ("S", s - 5), ("R", s - 4), ("W", s - 6 if s < 9 else s - 5), ("H", s - 1)] for s in range(6, 14)}
 VEC[0] = [("P", 1), ("P", 2), ("P", 3)]
 VEC[1] = [("I", 0), ("QC", 1, 0), ("H", 0), ("C", 0)]
-VEC[2] = [("I", 1), ("QC", 1, 1), ("H", 1), ("C", 4)]
-VEC[3] = [("I", 2), ("C", 8), ("H", 2)]
+VEC[2] = [("I", 1), ("QC", 1, 1), ("H", 1), ("C", 4), ("O", 4, 0), ("O", 5, 0)]
+VEC[3] = [("I", 2), ("C", 8), ("H", 2), ("O", 4, 1), ("O", 5, 1)]
 VEC[4] = [("I", 3), ("H", 3), ("C", 10)]
-VEC[5] = [("I", 4), ("G", 1, 4), ("S", 0), ("C", 11), ("H", 4), ("QC", 2, 0)]
+VEC[5] = [("I", 4), ("G", 1, 4), ("S", 0), ("R", 1), ("C", 11), ("H", 4), ("QC", 2, 0)]
 VEC[6] = VEC[6] + [("QC", 2, 1)]
 VEC[8] = [("I", 7), ("S", 3), ("H", 7), ("W", 2)]
-VEC[12] = [("I", 11), ("S", 7), ("H", 11), ("W", 6), ("Y", 0, 4)]
-VEC[13] = [("W", 7), ("I", 12), ("G", 9, 12), ("S", 8), ("W", 8), ("H", 12)]
-TAIL0 = []
-TAIL1 = [("S", 9)]
-TAIL2 = [("W", 9), ("Y", 4, 2)]
-TY_AFTER = {11: [0, 2], 12: [4]}
-EY_AFTER = {11: [0, 2], 12: [4]}
-CAST_AFTER = {6: [0], 7: [1], 8: [2], 9: [3], 10: [4]}
-CAST_LATE = {11: [5], 12: [6], 13: [7]}
+VEC[9] = [("W", 3)] + VEC[9]
+VEC[12] = [("I", 11), ("S", 7), ("H", 11), ("W", 7), ("Y", 0, 4), ("SS", 0, 4)]
+TAIL = [("I", 13), ("Z", 9), ("T", 4, 2), ("T", 6, 2), ("Z", 10, 0, 3), ("EY", 4, 2), ("EY", 6, 2), ("S", 9), ("H", 13), ("W", 9), ("A", 9),
+        ("Z", 11, 0, 1), ("Z", 10, 3), ("Z", 11, 1), ("T", 8, 2), ("EY", 8, 2),
+        ("S", 10), ("S", 11), ("W", 10), ("A", 10), ("B", 11), ("T", 11, 1), ("EY", 11, 1), ("T", 10, 1), ("EY", 10, 1),
+        ("W", 11), ("Y", 4, 4), ("Y", 8, 2), ("Y", 10, 2), ("SS", 4, 8)]
+TY_AFTER = {11: [0, 2]}
+EY_AFTER = {11: [0, 2]}
+CAST_AFTER = {6: [0], 7: [1], 8: [2], 9: [3, 4], 10: [5]}
+CAST_LATE = {11: [6], 12: [7], 13: [8]}
 SORT_ACT = {}
 VEC_AFTER = 0
 
@@ -303,8 +306,8 @@ def tile_user_tower_for_scoring_h1_kernel(
         def turned(j, count):
             return y_t[:, j * 512 : (j + count) * 512]
 
-        def evacuate_output(j, count):
-            nc.scalar.copy(
+        def evacuate_output(j, count, copy=nc.scalar.copy):
+            copy(
                 out=turned(j, count).bitcast(F32).rearrange("p (x m u) -> p x m u", x=count, u=2),
                 in_=held[("y", j)][:, : count * 256].rearrange("p (x u m) -> p x m u", x=count, u=2),
             )
@@ -394,12 +397,12 @@ def tile_user_tower_for_scoring_h1_kernel(
 
         def planes(x, count):
             quantize_output(x, count)
-            if x == 0:
-                store_codes(0, 4)
-                store_scales(0, 4, [nc.sync])
+            store_codes(x, count)
 
         extra = {"P": permute_w1, "Q": quantize_users, "C": add_free_and_bias, "Y": planes, "O": sort_users,
-                 "S": add_product, "I": interleave_hidden, "H": quantize_hidden, "QC": quantize_chunk, "G": add_on_gpsimd, "R": add_rest, "A": round_output, "W": weight_and_store,
+                 "S": add_product, "Z": output_passes, "T": transpose_output, "EY": evacuate_output, "B": weight_rounded,
+                 "SS": lambda x, n: store_scales(x, n, [nc.sync, nc.scalar] if x + n == TILES else [nc.sync]),
+                 "EV": lambda j, n: evacuate_output(j, n, nc.vector.tensor_copy), "I": interleave_hidden, "H": quantize_hidden, "QC": quantize_chunk, "G": add_on_gpsimd, "R": add_rest, "A": round_output, "W": weight_and_store,
                  "E": lambda pair, g: evacuate_users(pair, g, nc.vector.tensor_copy)}
 
         def extras(steps):
@@ -431,34 +434,4 @@ def tile_user_tower_for_scoring_h1_kernel(
             for j in Z_AFTER.get(s, []):
                 output_passes(j)
 
-        last = len(SLOTS) - 1
-        extras(TAIL0)
-        interleave_hidden(last)
-        output_passes(9)
-        extras(TAIL1)
-        quantize_hidden(last)
-        extras(TAIL2)
-        round_output(8)
-        output_passes(10, 0, 3)
-        output_passes(11, 0, 3)
-        output_passes(10, 3)
-        output_passes(11, 3)
-        round_output(9)
-        transpose_output(6, 2)
-        transpose_output(8, 2)
-        evacuate_output(6, 2)
-        evacuate_output(8, 2)
-        add_product(10)
-        add_product(11)
-        weight_rounded(10)
-        weight_rounded(11)
-        for j in (10, 11):
-            transpose_output(j, 1)
-            evacuate_output(j, 1)
-        weight_and_store(10)
-        quantize_output(6, 4)
-        store_codes(4, 6)
-        weight_and_store(11)
-        quantize_output(10, 2)
-        store_codes(10, 2)
-        store_scales(4, 8, [nc.sync, nc.scalar])
+        extras(TAIL)

@@ -23,37 +23,36 @@ FG = F // 512
 TILES = M // P
 PAIRS = TILES // 2
 CHUNKS = M // 512
-BANKS = 7
+BANKS = 8
 H_RING = 4
 X_RING = 4
 
 SLOTS = [(4 * c, 4, fg) for c in range(CHUNKS) for fg in range(FG)][:10] + [(8, 2, 2), (8, 2, 3), (10, 2, 2), (10, 2, 3)]
-PAIRED = ()
-POOL_COLS = 320
+PAIRED = (5, 7, 9)
 HEAD_EXTRA = []
 U1 = [(2, 0), (3, 0), (2, 1), (3, 1)]
 U2 = [(4, 0), (5, 0), (4, 1), (5, 1)]
-TU_AFTER = {0: U1[:2], 1: U1[2:], 4: U2}
+TU_AFTER = {0: U1[:2], 1: U1[2:], 4: U2[:2], 5: U2[2:]}
 EU_ACT = TU_AFTER
 Z_AFTER = {s: [s - 4] for s in range(4, 13)}
-VEC = {s: [("I", s - 1), ("G", s - 4, s - 1), ("S", s - 5), ("R", s - 4), ("W", s - 6 if s < 9 else s - 5), ("H", s - 1)] for s in range(6, 14)}
+VEC = {s: [("I", s - 1), ("S", s - 5), ("H", s - 1), ("W", s - 5)] for s in range(5, 14)}
 VEC[0] = [("P", 1), ("P", 2), ("P", 3)]
 VEC[1] = [("I", 0), ("QC", 1, 0), ("H", 0), ("C", 0)]
-VEC[2] = [("I", 1), ("QC", 1, 1), ("H", 1), ("C", 4), ("O", 4, 0), ("O", 5, 0)]
-VEC[3] = [("I", 2), ("C", 8), ("H", 2), ("O", 4, 1), ("O", 5, 1)]
-VEC[4] = [("I", 3), ("H", 3), ("C", 10)]
-VEC[5] = [("I", 4), ("G", 1, 4), ("S", 0), ("R", 1), ("C", 11), ("H", 4), ("QC", 2, 0)]
-VEC[6] = VEC[6] + [("QC", 2, 1)]
-VEC[8] = [("I", 7), ("S", 3), ("H", 7), ("W", 2)]
-VEC[9] = [("W", 3)] + VEC[9]
-VEC[12] = [("I", 11), ("S", 7), ("H", 11), ("W", 7), ("Y", 0, 4), ("SS", 0, 4)]
+VEC[2] = [("I", 1), ("QC", 1, 1), ("H", 1)]
+VEC[3] = [("I", 2), ("H", 2)]
+VEC[4] = [("I", 3), ("H", 3), ("C", 1)]
+VEC[5] = VEC[5] + [("C", 2), ("QC", 2, 0)]
+VEC[6] = VEC[6] + [("QC", 2, 1), ("C", 3)]
+VEC[7] = VEC[7] + [("C", 4)]
+VEC[8] = VEC[8] + [("C", 5)]
+VEC[12] = VEC[12] + [("Y", 0, 4), ("SS", 0, 4)]
 TAIL = [("I", 13), ("Z", 9), ("T", 4, 2), ("T", 6, 2), ("Z", 10, 0, 3), ("EY", 4, 2), ("EY", 6, 2), ("S", 9), ("H", 13), ("W", 9), ("A", 9),
         ("Z", 11, 0, 1), ("Z", 10, 3), ("Z", 11, 1), ("T", 8, 2), ("EY", 8, 2),
         ("S", 10), ("S", 11), ("W", 10), ("A", 10), ("B", 11), ("T", 11, 1), ("EY", 11, 1), ("T", 10, 1), ("EY", 10, 1),
         ("W", 11), ("Y", 4, 4), ("Y", 8, 2), ("Y", 10, 2), ("SS", 4, 8)]
 TY_AFTER = {11: [0, 2]}
 EY_AFTER = {11: [0, 2]}
-CAST_AFTER = {6: [0], 7: [1], 8: [2], 9: [3, 4], 10: [5]}
+CAST_AFTER = {5: [0], 6: [1], 7: [2], 8: [3], 9: [4], 10: [5]}
 CAST_LATE = {11: [6], 12: [7], 13: [8]}
 SORT_ACT = {}
 VEC_AFTER = 0
@@ -86,10 +85,9 @@ def tile_user_tower_for_scoring_h1_kernel(
         s2 = sb.tile([P, FG, D], U8, name="s2", align_bytes=256)
         b2_col = sb.tile([P, 4], BF16, name="b2_col", align_bytes=64)
         dw_col = sb.tile([P, 4], BF16, name="dw_col", align_bytes=64)
-        b2_all = sb.tile([P, D], BF16, name="b2_all", align_bytes=64)
-        vec_bank = ps.tile([P, 512], F32, name="vec_bank")
-        b2_psum = vec_bank[:].bitcast(BF16)[:, :D]
-        dw_all = vec_bank[:].bitcast(BF16)[:, D:]
+        vec_all = sb.tile([P, 2, D], BF16, name="vec_all", align_bytes=64)
+        b2_all = vec_all[:, 0:1, :]
+        dw_all = vec_all[:, 1, :]
         uf = tiles("uf", CHUNKS, [P, 4, D], BF16)
         x_t = tiles("x_t", X_RING, [P, 2048], BF16)
         x_codes = tiles("x_codes", CHUNKS * KG, [P, 512], U32, 256)
@@ -98,7 +96,8 @@ def tile_user_tower_for_scoring_h1_kernel(
         h_words = tiles("h_words", H_RING, [P, 2048], BF16)
         h_codes = tiles("h_codes", CHUNKS * FG, [P, 512], U32, 256)
         h_scales = tiles("h_scales", CHUNKS * FG, [P, 512], U8, 256)
-        y = tiles("y", TILES, [P, D], F32)
+        y_pair = tiles("y", PAIRS, [P, 2, D], F32)
+        y = [y_pair[j // 2][:, j % 2, :] for j in range(TILES)]
         y_bf = tiles("y_bf", TILES, [P, D], BF16)
         y_t = sb.tile([P, TILES * 512], BF16, name="y_t", align_bytes=64)
         y_codes = sb.tile([P, M], U32, name="y_codes", align_bytes=64)
@@ -107,7 +106,6 @@ def tile_user_tower_for_scoring_h1_kernel(
         taken = []
         held = {}
         x_home = {}
-        addend = {}
         sorted_home = {}
 
         def next_bank(key):
@@ -255,36 +253,23 @@ def tile_user_tower_for_scoring_h1_kernel(
                     stop=(fg == FG - 1),
                 )
 
-        def add_free_and_bias(j):
-            c, i = divmod(j, 4)
-            addend[j] = y[j][:]
-            nc.vector.tensor_tensor(out=addend[j], in0=uf[c][:, i, :], in1=b2_psum, op=ALU.add)
-
-        def add_on_gpsimd(j, s):
-            c, i = divmod(j, 4)
-            addend[j] = h_rows[s % H_RING][:].bitcast(F32)[:, :D]
-            nc.gpsimd.tensor_tensor(
-                out=addend[j][:, :POOL_COLS], in0=uf[c][:, i, :POOL_COLS], in1=b2_all[:, :POOL_COLS], op=ALU.add
+        def add_free_and_bias(pair):
+            c, half = divmod(pair, 2)
+            nc.vector.tensor_tensor(
+                out=y_pair[pair][:], in0=uf[c][:, 2 * half : 2 * half + 2, :], in1=b2_all.to_broadcast([P, 2, D]), op=ALU.add
             )
 
-        def add_rest(j):
-            c, i = divmod(j, 4)
-            if POOL_COLS < D:
-                nc.vector.tensor_tensor(
-                    out=addend[j][:, POOL_COLS:], in0=uf[c][:, i, POOL_COLS:], in1=b2_psum[:, POOL_COLS:], op=ALU.add
-                )
-
         def add_product(j):
-            nc.vector.tensor_tensor(out=y[j][:], in0=held[("z", j)][:], in1=addend[j], op=ALU.add)
+            nc.vector.tensor_tensor(out=y[j], in0=held[("z", j)][:], in1=y[j], op=ALU.add)
 
         def weight_and_store(j):
-            nc.vector.tensor_tensor(out=y[j][:], in0=y[j][:], in1=dw_all, op=ALU.mult)
-            nc.sync.dma_start(out=out_0[j * P : (j + 1) * P, :], in_=y[j][:])
+            nc.vector.tensor_tensor(out=y[j], in0=y[j], in1=dw_all, op=ALU.mult)
+            nc.sync.dma_start(out=out_0[j * P : (j + 1) * P, :], in_=y[j])
 
         def weight_rounded(j):
             nc.vector.tensor_tensor(
                 out=y_bf[j][:].rearrange("p (u q e) -> p u q e", u=2, e=2),
-                in0=y[j][:].rearrange("p (q u e) -> p u q e", u=2, e=2),
+                in0=y[j].rearrange("p (q u e) -> p u q e", u=2, e=2),
                 in1=dw_all.rearrange("p (q u e) -> p u q e", u=2, e=2),
                 op=ALU.mult,
             )
@@ -292,7 +277,7 @@ def tile_user_tower_for_scoring_h1_kernel(
         def round_output(j):
             nc.scalar.copy(
                 out=y_bf[j][:].rearrange("p (u q e) -> p u q e", u=2, e=2),
-                in_=y[j][:].rearrange("p (q u e) -> p u q e", u=2, e=2),
+                in_=y[j].rearrange("p (q u e) -> p u q e", u=2, e=2),
             )
 
         def transpose_output(j, count):
@@ -328,15 +313,18 @@ def tile_user_tower_for_scoring_h1_kernel(
                 )
 
         def transpose_vectors():
+            bank = next_bank(("v",))
             for v, col in enumerate((b2_col, dw_col)):
                 words = col[:].bitcast(F32)
                 for u in range(2):
-                    nc.tensor.transpose(
-                        vec_bank[:, v * 256 + u : (v + 1) * 256 : 2], words[:, u : u + 1].to_broadcast([P, P]), ident[:]
-                    )
+                    at = (2 * v + u) * P
+                    nc.tensor.transpose(bank[:, at : at + P], words[:, u : u + 1].to_broadcast([P, P]), ident[:])
 
         def evacuate_vectors():
-            nc.scalar.copy(out=b2_all[:].bitcast(F32), in_=vec_bank[:, :256])
+            nc.scalar.copy(
+                out=vec_all[:].bitcast(F32).rearrange("m v (q u) -> m v q u", u=2),
+                in_=held[("v",)][:].rearrange("m (v u q) -> m v q u", v=2, u=2),
+            )
 
         make_identity(nc, ident[:])
         nc.vector.memset(s1_first[:].bitcast(I32), 0)
@@ -402,7 +390,7 @@ def tile_user_tower_for_scoring_h1_kernel(
         extra = {"P": permute_w1, "Q": quantize_users, "C": add_free_and_bias, "Y": planes, "O": sort_users,
                  "S": add_product, "Z": output_passes, "T": transpose_output, "EY": evacuate_output, "B": weight_rounded,
                  "SS": lambda x, n: store_scales(x, n, [nc.sync, nc.scalar] if x + n == TILES else [nc.sync]),
-                 "EV": lambda j, n: evacuate_output(j, n, nc.vector.tensor_copy), "I": interleave_hidden, "H": quantize_hidden, "QC": quantize_chunk, "G": add_on_gpsimd, "R": add_rest, "A": round_output, "W": weight_and_store,
+                 "EV": lambda j, n: evacuate_output(j, n, nc.vector.tensor_copy), "I": interleave_hidden, "H": quantize_hidden, "QC": quantize_chunk, "A": round_output, "W": weight_and_store,
                  "E": lambda pair, g: evacuate_users(pair, g, nc.vector.tensor_copy)}
 
         def extras(steps):

@@ -27,34 +27,35 @@ BANKS = 8
 H_RING = 4
 X_RING = 4
 
-SLOTS = [(4 * c, 4, fg) for c in range(CHUNKS) for fg in range(FG)][:10] + [(8, 2, 2), (8, 2, 3), (10, 2, 2), (10, 2, 3)]
+SLOTS = [(4 * c, 4, fg) for c in range(CHUNKS) for fg in range(FG)]
 PAIRED = (5, 7, 9)
 HEAD_EXTRA = []
 U1 = [(2, 0), (3, 0), (2, 1), (3, 1)]
 U2 = [(4, 0), (5, 0), (4, 1), (5, 1)]
-TU_AFTER = {0: U1[:2], 1: U1[2:], 4: U2[:2], 5: U2[2:]}
+TU_AFTER = {0: U1[:2], 1: U1[2:], 4: U2}
 EU_ACT = TU_AFTER
-Z_AFTER = {s: [s - 4] for s in range(4, 13)}
-VEC = {s: [("I", s - 1), ("S", s - 5), ("H", s - 1), ("W", s - 5)] for s in range(5, 14)}
+Z_AFTER = {s: [s - 4] for s in range(4, 12)}
+VEC = {s: [("I", s - 1), ("S", s - 5), ("H", s - 1), ("W", s - 5)] for s in range(5, 12)}
 VEC[0] = [("P", 1), ("P", 2), ("P", 3)]
 VEC[1] = [("I", 0), ("QC", 1, 0), ("H", 0), ("C", 0)]
-VEC[2] = [("I", 1), ("QC", 1, 1), ("H", 1)]
-VEC[3] = [("I", 2), ("H", 2)]
+VEC[2] = [("I", 1), ("QC", 1, 1), ("H", 1), ("O", 4, 0), ("O", 5, 0), ("O", 4, 1)]
+VEC[3] = [("I", 2), ("O", 5, 1), ("H", 2)]
 VEC[4] = [("I", 3), ("H", 3), ("C", 1)]
 VEC[5] = VEC[5] + [("C", 2), ("QC", 2, 0)]
 VEC[6] = VEC[6] + [("QC", 2, 1), ("C", 3)]
-VEC[7] = VEC[7] + [("C", 4)]
-VEC[8] = VEC[8] + [("C", 5)]
-VEC[12] = VEC[12] + [("Y", 0, 4), ("SS", 0, 4)]
-TAIL = [("I", 13), ("Z", 9), ("T", 4, 2), ("T", 6, 2), ("Z", 10, 0, 3), ("EY", 4, 2), ("EY", 6, 2), ("S", 9), ("H", 13), ("W", 9), ("A", 9),
-        ("Z", 11, 0, 1), ("Z", 10, 3), ("Z", 11, 1), ("T", 8, 2), ("EY", 8, 2),
-        ("S", 10), ("S", 11), ("W", 10), ("A", 10), ("B", 11), ("T", 11, 1), ("EY", 11, 1), ("T", 10, 1), ("EY", 10, 1),
-        ("W", 11), ("Y", 4, 4), ("Y", 8, 2), ("Y", 10, 2), ("SS", 4, 8)]
-TY_AFTER = {11: [0, 2]}
-EY_AFTER = {11: [0, 2]}
-CAST_AFTER = {5: [0], 6: [1], 7: [2], 8: [3], 9: [4], 10: [5]}
-CAST_LATE = {11: [6], 12: [7], 13: [8]}
-SORT_ACT = {}
+VEC[8] = VEC[8] + [("C", 4)]
+VEC[10] = VEC[10] + [("C", 5)]
+VEC[11] = VEC[11] + [("Y", 0, 4), ("SS", 0, 4)]
+TAIL = [("IH", 11, 0), ("IA", 11, 1), ("A", 6), ("S", 7), ("HH", 11, 0), ("W", 7), ("HH", 11, 1), ("A", 7),
+        ("Z", 8, 0, 3), ("Z", 9, 0, 3), ("Z", 8, 3), ("Z", 9, 3), ("Z", 10), ("Z", 11),
+        ("T", 4, 2), ("T", 6, 2), ("S", 8), ("S", 9), ("W", 8), ("A", 8), ("W", 9), ("A", 9), ("EY", 4, 2), ("EY", 6, 2),
+        ("T", 8, 2), ("S", 10), ("S", 11), ("W", 10), ("A", 10), ("EY", 8, 2), ("B", 11), ("Y", 4, 4), ("W", 11), ("Y", 8, 2),
+        ("T", 10, 1), ("EY", 10, 1), ("T", 11, 1), ("EY", 11, 1), ("Y", 10, 2), ("SS", 4, 8)]
+TY_AFTER = {9: [0, 2]}
+EY_AFTER = {9: [0, 2]}
+CAST_AFTER = {5: [0], 6: [1], 7: [2], 8: [3], 10: [4], 11: [5]}
+CAST_LATE = {}
+SORT_ACT = {-1: U1[:2]}
 VEC_AFTER = 0
 
 
@@ -239,6 +240,20 @@ def tile_user_tower_for_scoring_h1_kernel(
                 in_=h_words[s % H_RING][:, : 4 * count * P],
             )
 
+        def interleave_half(s, h, copy):
+            rows = h_rows[s % H_RING][:].rearrange("p (t c i) -> p c t i", i=4, t=4)
+            words = h_words[s % H_RING][:].rearrange("p (c i t) -> p c t i", i=4, t=4)
+            copy(out=words[:, 64 * h : 64 * (h + 1)], in_=rows[:, 64 * h : 64 * (h + 1)])
+
+        def quantize_half(s, h):
+            first, count, fg = SLOTS[s]
+            cols = slice(256 * h, 256 * (h + 1))
+            nc.vector.quantize_mx(
+                out=h_codes[first // 4 * FG + fg][:, cols].bitcast(FP8X4),
+                scales=h_scales[first // 4 * FG + fg][:, cols],
+                in_=h_words[s % H_RING][:, 1024 * h : 1024 * (h + 1)],
+            )
+
         def output_passes(j, first=0, last=FG):
             c, i = divmod(j, 4)
             for fg in range(first, last):
@@ -388,7 +403,8 @@ def tile_user_tower_for_scoring_h1_kernel(
             store_codes(x, count)
 
         extra = {"P": permute_w1, "Q": quantize_users, "C": add_free_and_bias, "Y": planes, "O": sort_users,
-                 "S": add_product, "Z": output_passes, "T": transpose_output, "EY": evacuate_output, "B": weight_rounded,
+                 "S": add_product, "IH": lambda s, h: interleave_half(s, h, nc.vector.tensor_copy),
+                 "IA": lambda s, h: interleave_half(s, h, nc.scalar.copy), "HH": quantize_half, "Z": output_passes, "T": transpose_output, "EY": evacuate_output, "B": weight_rounded,
                  "SS": lambda x, n: store_scales(x, n, [nc.sync, nc.scalar] if x + n == TILES else [nc.sync]),
                  "EV": lambda j, n: evacuate_output(j, n, nc.vector.tensor_copy), "I": interleave_hidden, "H": quantize_hidden, "QC": quantize_chunk, "A": round_output, "W": weight_and_store,
                  "E": lambda pair, g: evacuate_users(pair, g, nc.vector.tensor_copy)}

@@ -24,39 +24,43 @@ TILES = M // P
 PAIRS = TILES // 2
 CHUNKS = M // 512
 BANKS = 8
-H_RING = 4
+H_RING = 3
 X_RING = 4
 
 SLOTS = [(4 * c, 4, fg) for c in range(CHUNKS) for fg in range(FG)]
 PAIRED = (5, 7, 9)
+FINE = False
+WARM = (0, 0)
 HEAD_EXTRA = []
-U1 = [(2, 0), (3, 0), (2, 1), (3, 1)]
-U2 = [(4, 0), (5, 0), (4, 1), (5, 1)]
+LOADS = [("b1",), ("u", 2), ("w1b",), ("s1",), ("w1c",), ("b2",), ("dw",), ("u", 3), ("uf", 0), ("u", 4), ("u", 5), ("w2",), ("s2",), ("uf", 1), ("uf", 2)]
+U1 = [(2, 0), (2, 1), (3, 0), (3, 1)]
+U2 = [(4, 0), (4, 1), (5, 0), (5, 1)]
 TU_AFTER = {0: U1[:2], 1: U1[2:], 4: U2}
 EU_ACT = TU_AFTER
 Z_AFTER = {s: [s - 4] for s in range(4, 12)}
 VEC = {s: [("I", s - 1), ("S", s - 5), ("H", s - 1), ("W", s - 5)] for s in range(5, 12)}
-VEC[0] = [("P", 1), ("P", 2), ("P", 3)]
-VEC[1] = [("I", 0), ("QC", 1, 0), ("H", 0), ("C", 0)]
-VEC[2] = [("I", 1), ("QC", 1, 1), ("H", 1), ("O", 4, 0), ("O", 5, 0), ("O", 4, 1)]
-VEC[3] = [("I", 2), ("O", 5, 1), ("H", 2)]
+VEC[0] = [("P", 1), ("P", 2)]
+VEC[1] = [("P", 3), ("I", 0), ("H", 0)]
+VEC[2] = [("Q", 2, 0), ("Q", 2, 1), ("I", 1), ("Q", 3, 0), ("Q", 3, 1), ("H", 1), ("O", 4, 0), ("O", 4, 1), ("C", 0)]
+VEC[3] = [("I", 2), ("H", 2)]
 VEC[4] = [("I", 3), ("H", 3), ("C", 1)]
-VEC[5] = VEC[5] + [("C", 2), ("QC", 2, 0)]
-VEC[6] = VEC[6] + [("QC", 2, 1), ("C", 3)]
+VEC[5] = VEC[5] + [("QC", 2, 0), ("C", 2)]
+VEC[6] = VEC[6] + [("QC", 2, 1)]
+VEC[7] = VEC[7] + [("C", 3)]
 VEC[8] = VEC[8] + [("C", 4)]
-VEC[10] = VEC[10] + [("C", 5)]
+VEC[9] = VEC[9] + [("C", 5)]
 VEC[11] = VEC[11] + [("Y", 0, 4), ("SS", 0, 4)]
 TAIL = [("IH", 11, 0), ("IA", 11, 1), ("A", 6), ("S", 7), ("HH", 11, 0), ("W", 7), ("HH", 11, 1), ("A", 7),
         ("Z", 8, 0, 3), ("Z", 9, 0, 3), ("Z", 8, 3), ("Z", 9, 3), ("Z", 10), ("Z", 11),
         ("T", 4, 2), ("T", 6, 2), ("S", 8), ("S", 9), ("W", 8), ("A", 8), ("W", 9), ("A", 9), ("EY", 4, 2), ("EY", 6, 2),
         ("T", 8, 2), ("S", 10), ("S", 11), ("W", 10), ("A", 10), ("EY", 8, 2), ("B", 11), ("Y", 4, 4), ("W", 11), ("Y", 8, 2),
         ("T", 10, 1), ("EY", 10, 1), ("T", 11, 1), ("EY", 11, 1), ("Y", 10, 2), ("SS", 4, 8)]
-TY_AFTER = {9: [0, 2]}
-EY_AFTER = {9: [0, 2]}
+TY_AFTER = {10: [0, 2]}
+EY_AFTER = {10: [0, 2]}
 CAST_AFTER = {5: [0], 6: [1], 7: [2], 8: [3], 10: [4], 11: [5]}
 CAST_LATE = {}
 SORT_ACT = {-1: U1[:2]}
-VEC_AFTER = 0
+VEC_AFTER = 1
 
 
 def tile_user_tower_for_scoring_h1_kernel(
@@ -73,10 +77,14 @@ def tile_user_tower_for_scoring_h1_kernel(
 
         banks = [ps.tile([P, 512], F32, name="bank%d" % n) for n in range(BANKS)]
         ident = sb.tile([P, P], F32, name="ident", align_bytes=64)
-        u_raw = tiles("u_raw", PAIRS * KG, [P, 2, 512], BF16)
+        u_head = tiles("u_head", 2 * KG, [P, 2, 512], BF16)
+        u_raw = [None, None] + tiles("u_raw", PAIRS - 2, [P, 2, K], BF16)
+        u_last = tiles("u_last", 2, [P, 512], BF16)
         u_sorted = tiles("u_sorted", 4, [P, 2, 2, P], F32)
         w1_first = tiles("w1_first", KG, [P, 1024], U8)
-        w1_raw = [None] + tiles("w1_raw", FG - 1, [P, KG, 1024], U8)
+        w1_second = sb.tile([P, KG, 1024], U8, name="w1_second", align_bytes=64)
+        w1_last = sb.tile([P, KG, 2048], U8, name="w1_last", align_bytes=64)
+        w1_raw = [None, w1_second[:], w1_last[:, :, :1024], w1_last[:, :, 1024:]]
         w1_perm = tiles("w1_perm", FG, [P, KG, 1024], U8, 256)
         s1_first = sb.tile([P, KG, 512], U8, name="s1_first", align_bytes=64)
         s1_rest = sb.tile([P, KG, F - 512], U8, name="s1_rest", align_bytes=64)
@@ -104,6 +112,22 @@ def tile_user_tower_for_scoring_h1_kernel(
         y_codes = sb.tile([P, M], U32, name="y_codes", align_bytes=64)
         y_scales = sb.tile([P, M], U8, name="y_scales", align_bytes=64)
 
+        warm_in = sb.tile([P, 1024], BF16, name="warm_in", align_bytes=64)
+        warm_codes = sb.tile([P, 256], U32, name="warm_codes", align_bytes=256)
+        warm_scales = sb.tile([P, 256], U8, name="warm_scales", align_bytes=256)
+
+        def warm_up(count):
+            for n in range(count):
+                nc.tensor.matmul_mx(
+                    out=banks[BANKS - 1][:, :256],
+                    lhsT=warm_codes[:, :64].bitcast(FP4X4),
+                    lhsT_scale=warm_scales[:, :P],
+                    rhs=warm_codes[:].bitcast(FP8X4),
+                    rhs_scale=warm_scales[:],
+                    start=True,
+                    stop=True,
+                )
+
         taken = []
         held = {}
         x_home = {}
@@ -116,14 +140,23 @@ def tile_user_tower_for_scoring_h1_kernel(
 
         def load_users(pair, g):
             src = users[pair * 256 : (pair + 1) * 256, g * 512 : (g + 1) * 512].rearrange("(i p) k -> p i k", p=P)
-            nc.sync.dma_start(out=u_raw[pair * KG + g][:], in_=src)
+            nc.sync.dma_start(out=u_head[pair * KG + g][:], in_=src)
+
+        def load_pair(pair):
+            src = users[pair * 256 : (pair + 1) * 256, :].rearrange("(i p) k -> p i k", p=P)
+            nc.sync.dma_start(out=u_raw[pair][:], in_=src)
+
+        def user_words(pair, g):
+            if pair < 2:
+                return u_head[pair * KG + g][:].bitcast(F32)
+            return u_raw[pair][:].bitcast(F32)[:, :, g * 256 : (g + 1) * 256]
 
         def load_w1_first(g):
             nc.sync.dma_start(out=w1_first[g][:].bitcast(I32), in_=w1_words[g, :, :1024].bitcast(I32))
 
-        def load_w1(fg):
-            src = w1_words[:, :, fg * 1024 : (fg + 1) * 1024].rearrange("g p n -> p g n")
-            nc.sync.dma_start(out=w1_raw[fg][:].bitcast(I32), in_=src.bitcast(I32))
+        def load_w1(tile, first, last):
+            src = w1_words[:, :, first * 1024 : last * 1024].rearrange("g p n -> p g n")
+            nc.sync.dma_start(out=tile[:].bitcast(I32), in_=src.bitcast(I32))
 
         def load_scale_rows(plane, rows):
             for q in range(4):
@@ -143,7 +176,7 @@ def tile_user_tower_for_scoring_h1_kernel(
         def permute_w1_codes(fg):
             nc.vector.tensor_copy(
                 out=w1_perm[fg][:].bitcast(U16).rearrange("p g (t m) -> p g t m", t=4),
-                in_=w1_raw[fg][:].bitcast(U16).rearrange("p g (m t) -> p g t m", t=4),
+                in_=w1_raw[fg].bitcast(U16).rearrange("p g (m t) -> p g t m", t=4),
             )
 
         def permute_w1_scales(fg):
@@ -157,17 +190,36 @@ def tile_user_tower_for_scoring_h1_kernel(
             sorted_home[(pair, g)] = u_sorted[len(sorted_home) % 4]
             copy(
                 out=sorted_home[(pair, g)][:],
-                in_=u_raw[pair * KG + g][:].bitcast(F32).rearrange("p i (q u) -> p i u q", u=2),
+                in_=user_words(pair, g).rearrange("p i (q u) -> p i u q", u=2),
             )
 
         def transpose_users(pair, g):
             bank = next_bank(("u", pair, g))
-            words = u_raw[pair * KG + g][:].bitcast(F32)
+            words = user_words(pair, g)
             for i in range(2):
                 for u in range(2):
                     col = (2 * i + u) * P
                     src = sorted_home[(pair, g)][:, i, u, :] if (pair, g) in sorted_home else words[:, i, u:256:2]
                     nc.tensor.transpose(bank[:, col : col + P], src, ident[:])
+
+        def load_tile(j, g):
+            nc.sync.dma_start(out=u_last[j % 2][:], in_=users[j * P : (j + 1) * P, g * 512 : (g + 1) * 512])
+
+        def turn_tile(j, g):
+            bank = next_bank(("ut", j))
+            words = u_last[j % 2][:].bitcast(F32)
+            for u in range(2):
+                nc.tensor.transpose(bank[:, u * P : (u + 1) * P], words[:, u:256:2], ident[:])
+            nc.scalar.copy(
+                out=x_t[g][:, j * 512 : (j + 1) * 512].bitcast(F32).rearrange("p (m u) -> p m u", u=2),
+                in_=bank[:, :256].rearrange("p (u m) -> p m u", u=2),
+            )
+
+        def quantize_tile(j, g):
+            cols = slice(j * P, (j + 1) * P)
+            nc.vector.quantize_mx(
+                out=x_codes[g][:, cols].bitcast(FP8X4), scales=x_scales[g][:, cols], in_=x_t[g][:, j * 512 : (j + 1) * 512]
+            )
 
         def evacuate_users(pair, g, copy=nc.scalar.copy):
             x_home[(pair, g)] = x_t[(pair // 2 * KG + g) % X_RING][:, pair % 2 * 1024 : (pair % 2 + 1) * 1024]
@@ -342,7 +394,11 @@ def tile_user_tower_for_scoring_h1_kernel(
             )
 
         make_identity(nc, ident[:])
+        if WARM[0]:
+            nc.vector.memset(warm_in[:].bitcast(I32), 0)
         nc.vector.memset(s1_first[:].bitcast(I32), 0)
+        if WARM[0]:
+            nc.vector.quantize_mx(out=warm_codes[:].bitcast(FP8X4), scales=warm_scales[:], in_=warm_in[:])
         nc.vector.memset(s1_rest[:].bitcast(I32), 0)
         nc.vector.memset(s2[:].bitcast(I32), 0)
 
@@ -351,31 +407,39 @@ def tile_user_tower_for_scoring_h1_kernel(
         load_w1_first(0)
         load_scale_rows(s1_first, w1_scales[:, :, :512])
         load_users(0, 1)
-        load_users(1, 1)
-        load_w1_first(1)
-        nc.sync.dma_start(out=b1_col[:], in_=b1.rearrange("(g p t) -> p g t", p=P, t=4))
-        nc.sync.dma_start(out=b2_col[:], in_=b2.rearrange("(p t) -> p t", t=4))
-        nc.sync.dma_start(out=dw_col[:], in_=dim_weight.rearrange("(p t) -> p t", t=4))
-        load_users(2, 0)
-        load_users(3, 0)
-        load_w1(1)
-        load_scale_rows(s1_rest, w1_scales[:, :, 512:])
-        load_w1(2)
-        load_w1(3)
-        load_users(2, 1)
-        load_users(3, 1)
-        for c in range(CHUNKS):
-            load_user_free(c)
-        nc.sync.dma_start(out=w2[:].bitcast(I32), in_=w2_words.rearrange("g p n -> p g n").bitcast(I32))
-        load_scale_rows(s2, w2_scales)
-        for g in range(KG):
-            for pair in (4, 5):
-                load_users(pair, g)
+        if FINE:
+            load_w1_first(1)
+            load_tile(2, 1)
+            load_tile(3, 1)
+        else:
+            load_users(1, 1)
+            load_w1_first(1)
+        loads = {
+            "b1": lambda: nc.sync.dma_start(out=b1_col[:], in_=b1.rearrange("(g p t) -> p g t", p=P, t=4)),
+            "b2": lambda: nc.sync.dma_start(out=b2_col[:], in_=b2.rearrange("(p t) -> p t", t=4)),
+            "dw": lambda: nc.sync.dma_start(out=dw_col[:], in_=dim_weight.rearrange("(p t) -> p t", t=4)),
+            "b2x": lambda: nc.sync.dma_start(out=vec_all[:, 0, :], in_=b2.partition_broadcast(P)),
+            "dwx": lambda: nc.sync.dma_start(out=vec_all[:, 1, :], in_=dim_weight.partition_broadcast(P)),
+            "w1b": lambda: load_w1(w1_second, 1, 2),
+            "w1c": lambda: load_w1(w1_last, 2, 4),
+            "s1": lambda: load_scale_rows(s1_rest, w1_scales[:, :, 512:]),
+            "u": load_pair,
+            "uf": load_user_free,
+            "w2": lambda: nc.sync.dma_start(out=w2[:].bitcast(I32), in_=w2_words.rearrange("g p n -> p g n").bitcast(I32)),
+            "s2": lambda: load_scale_rows(s2, w2_scales),
+        }
+        for step in LOADS:
+            loads[step[0]](*step[1:])
 
         for g in range(KG):
+            warm_up(WARM[g])
             for pair in range(2):
-                transpose_users(pair, g)
-                evacuate_users(pair, g)
+                if FINE and (pair, g) == (1, 1):
+                    turn_tile(2, 1)
+                    turn_tile(3, 1)
+                else:
+                    transpose_users(pair, g)
+                    evacuate_users(pair, g)
         permute_w1_first(0)
         quantize_users(0, 0)
         permute_w1_scales(0)
@@ -384,7 +448,11 @@ def tile_user_tower_for_scoring_h1_kernel(
             hidden_pass(0, t, 0)
         quantize_users(0, 1)
         permute_w1_first(1)
-        quantize_users(1, 1)
+        if FINE:
+            quantize_tile(2, 1)
+            quantize_tile(3, 1)
+        else:
+            quantize_users(1, 1)
         if VEC_AFTER < 0:
             transpose_vectors()
             evacuate_vectors()

@@ -14,53 +14,21 @@ U16 = mybir.dt.uint16
 U8 = mybir.dt.uint8
 FP8X4 = mybir.dt.float8_e4m3fn_x4
 FP4X4 = mybir.dt.float4_e2m1fn_x4
-ALU = mybir.AluOpType
 ACT = mybir.ActivationFunctionType
+ALU = mybir.AluOpType
 
 P = 128
 KG = K // 512
 FG = F // 512
+CHUNKS = M // 512
 TILES = M // P
 PAIRS = TILES // 2
-CHUNKS = M // 512
+SLOTS = CHUNKS * FG
 BANKS = 8
 H_RING = 3
 X_RING = 4
-
-SLOTS = [(4 * c, 4, fg) for c in range(CHUNKS) for fg in range(FG)]
-PAIRED = (5, 7, 9)
-FINE = False
-WARM = (0, 0)
-HEAD_EXTRA = []
-LOADS = [("b1",), ("u", 2), ("w1b",), ("s1",), ("w1c",), ("b2",), ("dw",), ("u", 3), ("uf", 0), ("u", 4), ("u", 5), ("w2",), ("s2",), ("uf", 1), ("uf", 2)]
-U1 = [(2, 0), (2, 1), (3, 0), (3, 1)]
-U2 = [(4, 0), (4, 1), (5, 0), (5, 1)]
-TU_AFTER = {0: U1[:2], 1: U1[2:], 4: U2}
-EU_ACT = TU_AFTER
-Z_AFTER = {s: [s - 4] for s in range(4, 12)}
-VEC = {s: [("I", s - 1), ("S", s - 5), ("H", s - 1), ("W", s - 5)] for s in range(5, 12)}
-VEC[0] = [("P", 1), ("P", 2)]
-VEC[1] = [("P", 3), ("I", 0), ("H", 0)]
-VEC[2] = [("Q", 2, 0), ("Q", 2, 1), ("I", 1), ("Q", 3, 0), ("Q", 3, 1), ("H", 1), ("O", 4, 0), ("O", 4, 1), ("C", 0)]
-VEC[3] = [("I", 2), ("H", 2)]
-VEC[4] = [("I", 3), ("H", 3), ("C", 1)]
-VEC[5] = VEC[5] + [("QC", 2, 0), ("C", 2)]
-VEC[6] = VEC[6] + [("QC", 2, 1)]
-VEC[7] = VEC[7] + [("C", 3)]
-VEC[8] = VEC[8] + [("C", 4)]
-VEC[9] = VEC[9] + [("C", 5)]
-VEC[11] = VEC[11] + [("Y", 0, 4), ("SS", 0, 4)]
-TAIL = [("IH", 11, 0), ("IA", 11, 1), ("A", 6), ("S", 7), ("HH", 11, 0), ("W", 7), ("HH", 11, 1), ("A", 7),
-        ("Z", 8, 0, 3), ("Z", 9, 0, 3), ("Z", 8, 3), ("Z", 9, 3), ("Z", 10), ("Z", 11),
-        ("T", 4, 2), ("T", 6, 2), ("S", 8), ("S", 9), ("W", 8), ("A", 8), ("W", 9), ("A", 9), ("EY", 4, 2), ("EY", 6, 2),
-        ("T", 8, 2), ("S", 10), ("S", 11), ("W", 10), ("A", 10), ("EY", 8, 2), ("B", 11), ("Y", 4, 4), ("W", 11), ("Y", 8, 2),
-        ("T", 10, 1), ("EY", 10, 1), ("T", 11, 1), ("EY", 11, 1), ("Y", 10, 2), ("SS", 4, 8)]
-TY_AFTER = {10: [0, 2]}
-EY_AFTER = {10: [0, 2]}
-CAST_AFTER = {5: [0], 6: [1], 7: [2], 8: [3], 10: [4], 11: [5]}
-CAST_LATE = {}
-SORT_ACT = {-1: U1[:2]}
-VEC_AFTER = 1
+OUT_LAG = 4
+PAIRED = (7, 9)
 
 
 def tile_user_tower_for_scoring_h1_kernel(
@@ -72,244 +40,170 @@ def tile_user_tower_for_scoring_h1_kernel(
         ps = ctx.enter_context(tc.psum_pool(name="ps", bufs=1))
         ctx.enter_context(tc.manual_schedule())
 
-        def tiles(name, count, shape, dtype, align=64):
-            return [sb.tile(shape, dtype, name="%s%d" % (name, n), align_bytes=align) for n in range(count)]
+        def tile(name, shape, dtype, align=64):
+            return sb.tile(shape, dtype, name=name, align_bytes=align)
 
-        banks = [ps.tile([P, 512], F32, name="bank%d" % n) for n in range(BANKS)]
-        ident = sb.tile([P, P], F32, name="ident", align_bytes=64)
+        def tiles(name, count, shape, dtype, align=64):
+            return [tile("%s%d" % (name, i), shape, dtype, align) for i in range(count)]
+
+        ident = tile("ident", [P, P], F32)
+        b1_col = tile("b1_col", [P, FG, 4], BF16)
+        b2_col = tile("b2_col", [P, 4], BF16)
+        dw_col = tile("dw_col", [P, 4], BF16)
         u_head = tiles("u_head", 2 * KG, [P, 2, 512], BF16)
-        u_raw = [None, None] + tiles("u_raw", PAIRS - 2, [P, 2, K], BF16)
-        u_last = tiles("u_last", 2, [P, 512], BF16)
-        u_sorted = tiles("u_sorted", 4, [P, 2, 2, P], F32)
+        u_rest = tiles("u_rest", PAIRS - 2, [P, 2, K], BF16)
         w1_first = tiles("w1_first", KG, [P, 1024], U8)
-        w1_second = sb.tile([P, KG, 1024], U8, name="w1_second", align_bytes=64)
-        w1_last = sb.tile([P, KG, 2048], U8, name="w1_last", align_bytes=64)
-        w1_raw = [None, w1_second[:], w1_last[:, :, :1024], w1_last[:, :, 1024:]]
-        w1_perm = tiles("w1_perm", FG, [P, KG, 1024], U8, 256)
-        s1_first = sb.tile([P, KG, 512], U8, name="s1_first", align_bytes=64)
-        s1_rest = sb.tile([P, KG, F - 512], U8, name="s1_rest", align_bytes=64)
-        s1_perm = tiles("s1_perm", FG, [P, KG, 512], U8, 256)
-        b1_col = sb.tile([P, FG, 4], BF16, name="b1_col", align_bytes=64)
-        w2 = sb.tile([P, FG, 1024], U8, name="w2", align_bytes=256)
-        s2 = sb.tile([P, FG, D], U8, name="s2", align_bytes=256)
-        b2_col = sb.tile([P, 4], BF16, name="b2_col", align_bytes=64)
-        dw_col = sb.tile([P, 4], BF16, name="dw_col", align_bytes=64)
-        vec_all = sb.tile([P, 2, D], BF16, name="vec_all", align_bytes=64)
-        b2_all = vec_all[:, 0:1, :]
-        dw_all = vec_all[:, 1, :]
-        uf = tiles("uf", CHUNKS, [P, 4, D], BF16)
-        x_t = tiles("x_t", X_RING, [P, 2048], BF16)
+        w1_second = tile("w1_second", [P, KG, 1024], U8)
+        w1_last = tile("w1_last", [P, KG, 2048], U8)
+        w1_dealt = tiles("w1_dealt", FG, [P, KG, 1024], U8, 256)
+        s1_first = tile("s1_first", [P, KG, 512], U8)
+        s1_rest = tile("s1_rest", [P, KG, 1536], U8)
+        s1_dealt = tiles("s1_dealt", FG, [P, KG, 512], U8, 256)
+        w2 = tile("w2", [P, FG, 1024], U8, 256)
+        s2 = tile("s2", [P, FG, D], U8, 256)
+        vectors = tile("vectors", [P, 2, D], BF16)
+        free = tiles("free", CHUNKS, [P, 4, D], BF16)
+        x_turned = tiles("x_turned", X_RING, [P, 2048], BF16)
         x_codes = tiles("x_codes", CHUNKS * KG, [P, 512], U32, 256)
         x_scales = tiles("x_scales", CHUNKS * KG, [P, 512], U8, 256)
         h_rows = tiles("h_rows", H_RING, [P, 2048], BF16)
         h_words = tiles("h_words", H_RING, [P, 2048], BF16)
-        h_codes = tiles("h_codes", CHUNKS * FG, [P, 512], U32, 256)
-        h_scales = tiles("h_scales", CHUNKS * FG, [P, 512], U8, 256)
+        h_codes = tiles("h_codes", SLOTS, [P, 512], U32, 256)
+        h_scales = tiles("h_scales", SLOTS, [P, 512], U8, 256)
         y_pair = tiles("y", PAIRS, [P, 2, D], F32)
         y = [y_pair[j // 2][:, j % 2, :] for j in range(TILES)]
-        y_bf = tiles("y_bf", TILES, [P, D], BF16)
-        y_t = sb.tile([P, TILES * 512], BF16, name="y_t", align_bytes=64)
-        y_codes = sb.tile([P, M], U32, name="y_codes", align_bytes=64)
-        y_scales = sb.tile([P, M], U8, name="y_scales", align_bytes=64)
+        y_round = tiles("y_round", TILES, [P, D], BF16)
+        y_turned = tile("y_turned", [P, TILES * D], BF16)
+        y_codes = tile("y_codes", [P, M], U32)
+        y_scales = tile("y_scales", [P, M], U8)
+        banks = [ps.tile([P, 512], F32, name="bank%d" % i) for i in range(BANKS)]
 
-        warm_in = sb.tile([P, 1024], BF16, name="warm_in", align_bytes=64)
-        warm_codes = sb.tile([P, 256], U32, name="warm_codes", align_bytes=256)
-        warm_scales = sb.tile([P, 256], U8, name="warm_scales", align_bytes=256)
-
-        def warm_up(count):
-            for n in range(count):
-                nc.tensor.matmul_mx(
-                    out=banks[BANKS - 1][:, :256],
-                    lhsT=warm_codes[:, :64].bitcast(FP4X4),
-                    lhsT_scale=warm_scales[:, :P],
-                    rhs=warm_codes[:].bitcast(FP8X4),
-                    rhs_scale=warm_scales[:],
-                    start=True,
-                    stop=True,
-                )
-
-        taken = []
         held = {}
-        x_home = {}
-        sorted_home = {}
 
-        def next_bank(key):
-            held[key] = banks[len(taken) % BANKS]
-            taken.append(key)
+        def take_bank(key):
+            held[key] = banks[len(held) % BANKS]
             return held[key]
 
-        def load_users(pair, g):
+        def load_head(pair, g):
             src = users[pair * 256 : (pair + 1) * 256, g * 512 : (g + 1) * 512].rearrange("(i p) k -> p i k", p=P)
             nc.sync.dma_start(out=u_head[pair * KG + g][:], in_=src)
 
         def load_pair(pair):
             src = users[pair * 256 : (pair + 1) * 256, :].rearrange("(i p) k -> p i k", p=P)
-            nc.sync.dma_start(out=u_raw[pair][:], in_=src)
-
-        def user_words(pair, g):
-            if pair < 2:
-                return u_head[pair * KG + g][:].bitcast(F32)
-            return u_raw[pair][:].bitcast(F32)[:, :, g * 256 : (g + 1) * 256]
+            nc.sync.dma_start(out=u_rest[pair - 2][:], in_=src)
 
         def load_w1_first(g):
             nc.sync.dma_start(out=w1_first[g][:].bitcast(I32), in_=w1_words[g, :, :1024].bitcast(I32))
 
-        def load_w1(tile, first, last):
+        def load_w1(dst, first, last):
             src = w1_words[:, :, first * 1024 : last * 1024].rearrange("g p n -> p g n")
-            nc.sync.dma_start(out=tile[:].bitcast(I32), in_=src.bitcast(I32))
+            nc.sync.dma_start(out=dst[:].bitcast(I32), in_=src.bitcast(I32))
 
-        def load_scale_rows(plane, rows):
+        def load_scale_rows(dst, src):
             for q in range(4):
-                src = rows[:, q:16:4, :].rearrange("g r n -> r g n")
-                nc.sync.dma_start(out=plane[q:P:32, :, :].bitcast(I32), in_=src.bitcast(I32))
+                rows = src[:, q:16:4, :].rearrange("g r n -> r g n")
+                nc.sync.dma_start(out=dst[q:P:32, :, :].bitcast(I32), in_=rows.bitcast(I32))
 
-        def load_user_free(c):
-            src = user_free[c * 512 : (c + 1) * 512, :].rearrange("(i p) d -> p i d", p=P)
-            nc.sync.dma_start(out=uf[c][:], in_=src)
+        def load_free(c):
+            nc.sync.dma_start(out=free[c][:], in_=user_free[c * 512 : (c + 1) * 512, :].rearrange("(i p) d -> p i d", p=P))
 
-        def permute_w1_first(g):
-            nc.vector.tensor_copy(
-                out=w1_perm[0][:, g, :].bitcast(U16).rearrange("p (t m) -> p t m", t=4),
-                in_=w1_first[g][:].bitcast(U16).rearrange("p (m t) -> p t m", t=4),
-            )
+        def user_words(pair, g):
+            if pair < 2:
+                return u_head[pair * KG + g][:].bitcast(F32)
+            return u_rest[pair - 2][:].bitcast(F32)[:, :, g * 256 : (g + 1) * 256]
 
-        def permute_w1_codes(fg):
-            nc.vector.tensor_copy(
-                out=w1_perm[fg][:].bitcast(U16).rearrange("p g (t m) -> p g t m", t=4),
-                in_=w1_raw[fg].bitcast(U16).rearrange("p g (m t) -> p g t m", t=4),
-            )
-
-        def permute_w1_scales(fg):
-            src = s1_first[:] if fg == 0 else s1_rest[:, :, (fg - 1) * 512 : fg * 512]
-            nc.vector.tensor_copy(
-                out=s1_perm[fg][:].rearrange("p g (t m) -> p g t m", t=4),
-                in_=src.rearrange("p g (m t) -> p g t m", t=4),
-            )
-
-        def sort_users(pair, g, copy=nc.vector.tensor_copy):
-            sorted_home[(pair, g)] = u_sorted[len(sorted_home) % 4]
-            copy(
-                out=sorted_home[(pair, g)][:],
-                in_=user_words(pair, g).rearrange("p i (q u) -> p i u q", u=2),
-            )
-
-        def transpose_users(pair, g):
-            bank = next_bank(("u", pair, g))
-            words = user_words(pair, g)
+        def turn_users(pair, g):
+            bank = take_bank(("u", pair, g))
             for i in range(2):
                 for u in range(2):
-                    col = (2 * i + u) * P
-                    src = sorted_home[(pair, g)][:, i, u, :] if (pair, g) in sorted_home else words[:, i, u:256:2]
-                    nc.tensor.transpose(bank[:, col : col + P], src, ident[:])
+                    at = (2 * i + u) * P
+                    nc.tensor.transpose(bank[:, at : at + P], user_words(pair, g)[:, i, u:256:2], ident[:])
 
-        def load_tile(j, g):
-            nc.sync.dma_start(out=u_last[j % 2][:], in_=users[j * P : (j + 1) * P, g * 512 : (g + 1) * 512])
+        def x_home(pair, g):
+            return x_turned[(pair // 2 * KG + g) % X_RING][:, pair % 2 * 1024 : (pair % 2 + 1) * 1024]
 
-        def turn_tile(j, g):
-            bank = next_bank(("ut", j))
-            words = u_last[j % 2][:].bitcast(F32)
-            for u in range(2):
-                nc.tensor.transpose(bank[:, u * P : (u + 1) * P], words[:, u:256:2], ident[:])
+        def empty_users(pair, g):
             nc.scalar.copy(
-                out=x_t[g][:, j * 512 : (j + 1) * 512].bitcast(F32).rearrange("p (m u) -> p m u", u=2),
-                in_=bank[:, :256].rearrange("p (u m) -> p m u", u=2),
-            )
-
-        def quantize_tile(j, g):
-            cols = slice(j * P, (j + 1) * P)
-            nc.vector.quantize_mx(
-                out=x_codes[g][:, cols].bitcast(FP8X4), scales=x_scales[g][:, cols], in_=x_t[g][:, j * 512 : (j + 1) * 512]
-            )
-
-        def evacuate_users(pair, g, copy=nc.scalar.copy):
-            x_home[(pair, g)] = x_t[(pair // 2 * KG + g) % X_RING][:, pair % 2 * 1024 : (pair % 2 + 1) * 1024]
-            copy(
-                out=x_home[(pair, g)].bitcast(F32).rearrange("p (i m u) -> p i m u", i=2, u=2),
+                out=x_home(pair, g).bitcast(F32).rearrange("p (i m u) -> p i m u", i=2, u=2),
                 in_=held[("u", pair, g)][:].rearrange("p (i u m) -> p i m u", i=2, u=2),
             )
 
-        def quantize_users(pair, g):
+        def quantize_pair(pair, g):
             c, half = divmod(pair, 2)
             cols = slice(half * 256, (half + 1) * 256)
             nc.vector.quantize_mx(
-                out=x_codes[c * KG + g][:, cols].bitcast(FP8X4),
-                scales=x_scales[c * KG + g][:, cols],
-                in_=x_home[(pair, g)],
+                out=x_codes[c * KG + g][:, cols].bitcast(FP8X4), scales=x_scales[c * KG + g][:, cols], in_=x_home(pair, g)
             )
 
         def quantize_chunk(c, g):
-            nc.vector.quantize_mx(
-                out=x_codes[c * KG + g][:].bitcast(FP8X4), scales=x_scales[c * KG + g][:], in_=x_t[(c * KG + g) % X_RING][:]
+            n = c * KG + g
+            nc.vector.quantize_mx(out=x_codes[n][:].bitcast(FP8X4), scales=x_scales[n][:], in_=x_turned[n % X_RING][:])
+
+        def deal_first_codes(g):
+            nc.vector.tensor_copy(
+                out=w1_dealt[0][:, g, :].bitcast(U16).rearrange("p (t m) -> p t m", t=4),
+                in_=w1_first[g][:].bitcast(U16).rearrange("p (m t) -> p t m", t=4),
             )
 
-        def slot_cols(s):
-            first, count, fg = SLOTS[s]
-            return slice(first % 4 * P, (first % 4 + count) * P)
+        def deal_scales(fg):
+            src = s1_first[:] if fg == 0 else s1_rest[:, :, (fg - 1) * 512 : fg * 512]
+            nc.vector.tensor_copy(
+                out=s1_dealt[fg][:].rearrange("p g (t m) -> p g t m", t=4), in_=src.rearrange("p g (m t) -> p g t m", t=4)
+            )
+
+        def deal_group(fg):
+            src = w1_second[:] if fg == 1 else w1_last[:, :, (fg - 2) * 1024 : (fg - 1) * 1024]
+            nc.vector.tensor_copy(
+                out=w1_dealt[fg][:].bitcast(U16).rearrange("p g (t m) -> p g t m", t=4),
+                in_=src.bitcast(U16).rearrange("p g (m t) -> p g t m", t=4),
+            )
+            deal_scales(fg)
 
         def hidden_pass(s, t, g):
-            first, count, fg = SLOTS[s]
-            bank = next_bank(("h", s, t)) if g == 0 else held[("h", s, t)]
+            c, fg = divmod(s, FG)
+            bank = take_bank(("h", s, t)) if g == 0 else held[("h", s, t)]
             nc.tensor.matmul_mx(
-                out=bank[:, : count * P],
-                lhsT=w1_perm[fg][:, g, t * 256 : (t + 1) * 256].bitcast(FP4X4),
-                lhsT_scale=s1_perm[fg][:, g, t * P : (t + 1) * P],
-                rhs=x_codes[first // 4 * KG + g][:, slot_cols(s)].bitcast(FP8X4),
-                rhs_scale=x_scales[first // 4 * KG + g][:, slot_cols(s)],
+                out=bank[:],
+                lhsT=w1_dealt[fg][:, g, t * 256 : (t + 1) * 256].bitcast(FP4X4),
+                lhsT_scale=s1_dealt[fg][:, g, t * P : (t + 1) * P],
+                rhs=x_codes[c * KG + g][:].bitcast(FP8X4),
+                rhs_scale=x_scales[c * KG + g][:],
                 start=(g == 0),
                 stop=(g == KG - 1),
             )
 
-        def evacuate_hidden(s, t):
-            first, count, fg = SLOTS[s]
-            n = count * P
-            rows = h_rows[s % H_RING][:, : 4 * n]
+        def empty_hidden(s, t):
+            rows = h_rows[s % H_RING][:]
             if s in PAIRED:
                 dst = rows.rearrange("p (u m e) -> p u m e", u=2, e=2)[:, t // 2, :, t % 2]
             else:
-                dst = rows[:, t * n : (t + 1) * n]
-            nc.scalar.activation(out=dst, in_=held[("h", s, t)][:, :n], func=ACT.Relu, bias=b1_col[:, fg, t : t + 1])
+                dst = rows[:, t * 512 : (t + 1) * 512]
+            nc.scalar.activation(out=dst, in_=held[("h", s, t)][:], func=ACT.Relu, bias=b1_col[:, s % FG, t : t + 1])
 
-        def interleave_hidden(s):
-            n = SLOTS[s][1] * P
-            rows = h_rows[s % H_RING][:, : 4 * n]
-            words = h_words[s % H_RING][:, : 4 * n]
+        def interleave_hidden(s, copy=nc.vector.tensor_copy, first=0, last=P):
+            rows, words = h_rows[s % H_RING][:], h_words[s % H_RING][:]
             if s in PAIRED:
-                nc.vector.tensor_copy(
+                copy(
                     out=words.bitcast(F32).rearrange("p (m u) -> p m u", u=2),
                     in_=rows.bitcast(F32).rearrange("p (u m) -> p m u", u=2),
                 )
             else:
-                nc.vector.tensor_copy(
-                    out=words.rearrange("p (c i t) -> p c t i", i=4, t=4),
-                    in_=rows.rearrange("p (t c i) -> p c t i", i=4, t=4),
+                copy(
+                    out=words.rearrange("p (c i t) -> p c t i", i=4, t=4)[:, first:last],
+                    in_=rows.rearrange("p (t c i) -> p c t i", i=4, t=4)[:, first:last],
                 )
 
-        def quantize_hidden(s):
-            first, count, fg = SLOTS[s]
+        def quantize_hidden(s, first=0, last=512):
             nc.vector.quantize_mx(
-                out=h_codes[first // 4 * FG + fg][:, slot_cols(s)].bitcast(FP8X4),
-                scales=h_scales[first // 4 * FG + fg][:, slot_cols(s)],
-                in_=h_words[s % H_RING][:, : 4 * count * P],
-            )
-
-        def interleave_half(s, h, copy):
-            rows = h_rows[s % H_RING][:].rearrange("p (t c i) -> p c t i", i=4, t=4)
-            words = h_words[s % H_RING][:].rearrange("p (c i t) -> p c t i", i=4, t=4)
-            copy(out=words[:, 64 * h : 64 * (h + 1)], in_=rows[:, 64 * h : 64 * (h + 1)])
-
-        def quantize_half(s, h):
-            first, count, fg = SLOTS[s]
-            cols = slice(256 * h, 256 * (h + 1))
-            nc.vector.quantize_mx(
-                out=h_codes[first // 4 * FG + fg][:, cols].bitcast(FP8X4),
-                scales=h_scales[first // 4 * FG + fg][:, cols],
-                in_=h_words[s % H_RING][:, 1024 * h : 1024 * (h + 1)],
+                out=h_codes[s][:, first:last].bitcast(FP8X4),
+                scales=h_scales[s][:, first:last],
+                in_=h_words[s % H_RING][:, 4 * first : 4 * last],
             )
 
         def output_passes(j, first=0, last=FG):
             c, i = divmod(j, 4)
             for fg in range(first, last):
-                bank = next_bank(("z", j)) if fg == 0 else held[("z", j)]
+                bank = take_bank(("z", j)) if fg == 0 else held[("z", j)]
                 nc.tensor.matmul_mx(
                     out=bank[:],
                     lhsT=h_codes[c * FG + fg][:, i * P : (i + 1) * P].bitcast(FP8X4),
@@ -320,57 +214,67 @@ def tile_user_tower_for_scoring_h1_kernel(
                     stop=(fg == FG - 1),
                 )
 
+        def spread_vectors():
+            bank = take_bank(("v",))
+            for v, col in enumerate((b2_col, dw_col)):
+                words = col[:].bitcast(F32)
+                for u in range(2):
+                    at = (2 * v + u) * P
+                    nc.tensor.transpose(bank[:, at : at + P], words[:, u : u + 1].to_broadcast([P, P]), ident[:])
+            nc.scalar.copy(
+                out=vectors[:].bitcast(F32).rearrange("m v (q u) -> m v q u", u=2),
+                in_=bank[:].rearrange("m (v u q) -> m v q u", v=2, u=2),
+            )
+
         def add_free_and_bias(pair):
             c, half = divmod(pair, 2)
             nc.vector.tensor_tensor(
-                out=y_pair[pair][:], in0=uf[c][:, 2 * half : 2 * half + 2, :], in1=b2_all.to_broadcast([P, 2, D]), op=ALU.add
+                out=y_pair[pair][:],
+                in0=free[c][:, 2 * half : 2 * half + 2, :],
+                in1=vectors[:, 0:1, :].to_broadcast([P, 2, D]),
+                op=ALU.add,
             )
 
         def add_product(j):
             nc.vector.tensor_tensor(out=y[j], in0=held[("z", j)][:], in1=y[j], op=ALU.add)
 
         def weight_and_store(j):
-            nc.vector.tensor_tensor(out=y[j], in0=y[j], in1=dw_all, op=ALU.mult)
+            nc.vector.tensor_tensor(out=y[j], in0=y[j], in1=vectors[:, 1, :], op=ALU.mult)
             nc.sync.dma_start(out=out_0[j * P : (j + 1) * P, :], in_=y[j])
 
-        def weight_rounded(j):
-            nc.vector.tensor_tensor(
-                out=y_bf[j][:].rearrange("p (u q e) -> p u q e", u=2, e=2),
-                in0=y[j].rearrange("p (q u e) -> p u q e", u=2, e=2),
-                in1=dw_all.rearrange("p (q u e) -> p u q e", u=2, e=2),
-                op=ALU.mult,
-            )
+        def by_words(ap):
+            return ap.rearrange("p (q u e) -> p u q e", u=2, e=2)
+
+        def sorted_round(j):
+            return y_round[j][:].rearrange("p (u q e) -> p u q e", u=2, e=2)
 
         def round_output(j):
-            nc.scalar.copy(
-                out=y_bf[j][:].rearrange("p (u q e) -> p u q e", u=2, e=2),
-                in_=y[j].rearrange("p (q u e) -> p u q e", u=2, e=2),
-            )
+            nc.scalar.copy(out=sorted_round(j), in_=by_words(y[j]))
 
-        def transpose_output(j, count):
-            bank = next_bank(("y", j))
-            for x in range(count):
-                words = y_bf[j + x][:].bitcast(F32)
+        def weight_rounded(j):
+            nc.vector.tensor_tensor(out=sorted_round(j), in0=by_words(y[j]), in1=by_words(vectors[:, 1, :]), op=ALU.mult)
+
+        def turn_output(j, count):
+            bank = take_bank(("y", j))
+            for i in range(count):
+                words = y_round[j + i][:].bitcast(F32)
                 for u in range(2):
-                    col = (2 * x + u) * P
-                    nc.tensor.transpose(bank[:, col : col + P], words[:, u * P : (u + 1) * P], ident[:])
+                    at = (2 * i + u) * P
+                    nc.tensor.transpose(bank[:, at : at + P], words[:, u * P : (u + 1) * P], ident[:])
 
-        def turned(j, count):
-            return y_t[:, j * 512 : (j + count) * 512]
-
-        def evacuate_output(j, count, copy=nc.scalar.copy):
-            copy(
-                out=turned(j, count).bitcast(F32).rearrange("p (x m u) -> p x m u", x=count, u=2),
-                in_=held[("y", j)][:, : count * 256].rearrange("p (x u m) -> p x m u", x=count, u=2),
+        def empty_output(j, count):
+            nc.scalar.copy(
+                out=y_turned[:, j * D : (j + count) * D].bitcast(F32).rearrange("p (i m u) -> p i m u", i=count, u=2),
+                in_=held[("y", j)][:, : count * 256].rearrange("p (i u m) -> p i m u", i=count, u=2),
             )
 
-        def quantize_output(j, count):
+        def quantize_and_store_codes(j, count):
             cols = slice(j * P, (j + count) * P)
-            nc.vector.quantize_mx(out=y_codes[:, cols].bitcast(FP8X4), scales=y_scales[:, cols], in_=turned(j, count))
-
-        def store_codes(j, count):
+            nc.vector.quantize_mx(
+                out=y_codes[:, cols].bitcast(FP8X4), scales=y_scales[:, cols], in_=y_turned[:, j * D : (j + count) * D]
+            )
             dst = out_1[0].rearrange("p m t -> p (m t)")[:, 4 * j * P : 4 * (j + count) * P]
-            nc.sync.dma_start(out=dst.bitcast(I32), in_=y_codes[:, j * P : (j + count) * P].bitcast(I32))
+            nc.sync.dma_start(out=dst.bitcast(I32), in_=y_codes[:, cols].bitcast(I32))
 
         def store_scales(j, count, queues):
             cols = slice(j * P, (j + count) * P)
@@ -379,131 +283,141 @@ def tile_user_tower_for_scoring_h1_kernel(
                     out=out_2[0][q:16:4, cols].bitcast(I32), in_=y_scales[q:P:32, cols].bitcast(I32)
                 )
 
-        def transpose_vectors():
-            bank = next_bank(("v",))
-            for v, col in enumerate((b2_col, dw_col)):
-                words = col[:].bitcast(F32)
-                for u in range(2):
-                    at = (2 * v + u) * P
-                    nc.tensor.transpose(bank[:, at : at + P], words[:, u : u + 1].to_broadcast([P, P]), ident[:])
-
-        def evacuate_vectors():
-            nc.scalar.copy(
-                out=vec_all[:].bitcast(F32).rearrange("m v (q u) -> m v q u", u=2),
-                in_=held[("v",)][:].rearrange("m (v u q) -> m v q u", v=2, u=2),
-            )
-
         make_identity(nc, ident[:])
-        if WARM[0]:
-            nc.vector.memset(warm_in[:].bitcast(I32), 0)
-        nc.vector.memset(s1_first[:].bitcast(I32), 0)
-        if WARM[0]:
-            nc.vector.quantize_mx(out=warm_codes[:].bitcast(FP8X4), scales=warm_scales[:], in_=warm_in[:])
-        nc.vector.memset(s1_rest[:].bitcast(I32), 0)
-        nc.vector.memset(s2[:].bitcast(I32), 0)
-
-        load_users(0, 0)
-        load_users(1, 0)
-        load_w1_first(0)
-        load_scale_rows(s1_first, w1_scales[:, :, :512])
-        load_users(0, 1)
-        if FINE:
-            load_w1_first(1)
-            load_tile(2, 1)
-            load_tile(3, 1)
-        else:
-            load_users(1, 1)
-            load_w1_first(1)
-        loads = {
-            "b1": lambda: nc.sync.dma_start(out=b1_col[:], in_=b1.rearrange("(g p t) -> p g t", p=P, t=4)),
-            "b2": lambda: nc.sync.dma_start(out=b2_col[:], in_=b2.rearrange("(p t) -> p t", t=4)),
-            "dw": lambda: nc.sync.dma_start(out=dw_col[:], in_=dim_weight.rearrange("(p t) -> p t", t=4)),
-            "b2x": lambda: nc.sync.dma_start(out=vec_all[:, 0, :], in_=b2.partition_broadcast(P)),
-            "dwx": lambda: nc.sync.dma_start(out=vec_all[:, 1, :], in_=dim_weight.partition_broadcast(P)),
-            "w1b": lambda: load_w1(w1_second, 1, 2),
-            "w1c": lambda: load_w1(w1_last, 2, 4),
-            "s1": lambda: load_scale_rows(s1_rest, w1_scales[:, :, 512:]),
-            "u": load_pair,
-            "uf": load_user_free,
-            "w2": lambda: nc.sync.dma_start(out=w2[:].bitcast(I32), in_=w2_words.rearrange("g p n -> p g n").bitcast(I32)),
-            "s2": lambda: load_scale_rows(s2, w2_scales),
-        }
-        for step in LOADS:
-            loads[step[0]](*step[1:])
+        for scales in (s1_first, s1_rest, s2):
+            nc.vector.memset(scales[:].bitcast(I32), 0)
 
         for g in range(KG):
-            warm_up(WARM[g])
+            load_head(0, g)
+            load_head(1, g)
+            load_w1_first(g)
+            if g == 0:
+                load_scale_rows(s1_first, w1_scales[:, :, :512])
+        nc.sync.dma_start(out=b1_col[:], in_=b1.rearrange("(g p t) -> p g t", p=P, t=4))
+        load_pair(2)
+        load_w1(w1_second, 1, 2)
+        load_scale_rows(s1_rest, w1_scales[:, :, 512:])
+        load_w1(w1_last, 2, 4)
+        nc.sync.dma_start(out=b2_col[:], in_=b2.rearrange("(p t) -> p t", t=4))
+        nc.sync.dma_start(out=dw_col[:], in_=dim_weight.rearrange("(p t) -> p t", t=4))
+        load_pair(3)
+        load_free(0)
+        load_pair(4)
+        load_pair(5)
+        nc.sync.dma_start(out=w2[:].bitcast(I32), in_=w2_words.rearrange("g p n -> p g n").bitcast(I32))
+        load_scale_rows(s2, w2_scales)
+        load_free(1)
+        load_free(2)
+
+        for g in range(KG):
             for pair in range(2):
-                if FINE and (pair, g) == (1, 1):
-                    turn_tile(2, 1)
-                    turn_tile(3, 1)
-                else:
-                    transpose_users(pair, g)
-                    evacuate_users(pair, g)
-        permute_w1_first(0)
-        quantize_users(0, 0)
-        permute_w1_scales(0)
-        quantize_users(1, 0)
+                turn_users(pair, g)
+                empty_users(pair, g)
+        deal_first_codes(0)
+        quantize_pair(0, 0)
+        deal_scales(0)
+        quantize_pair(1, 0)
         for t in range(4):
             hidden_pass(0, t, 0)
-        quantize_users(0, 1)
-        permute_w1_first(1)
-        if FINE:
-            quantize_tile(2, 1)
-            quantize_tile(3, 1)
-        else:
-            quantize_users(1, 1)
-        if VEC_AFTER < 0:
-            transpose_vectors()
-            evacuate_vectors()
-        for unit in SORT_ACT.get(-1, []):
-            sort_users(*unit, nc.scalar.copy)
-        for unit in HEAD_EXTRA:
-            transpose_users(*unit)
-            evacuate_users(*unit)
+        quantize_pair(0, 1)
+        deal_first_codes(1)
+        quantize_pair(1, 1)
 
-        def permute_w1(fg):
-            permute_w1_codes(fg)
-            permute_w1_scales(fg)
+        for s in range(SLOTS):
+            done = s - 1 - OUT_LAG
+            if s == 0:
+                deal_group(1)
+                deal_group(2)
+            if s == 1:
+                deal_group(3)
+            if s == 2:
+                for g in range(KG):
+                    quantize_pair(2, g)
+            if s >= 1:
+                interleave_hidden(s - 1)
+            if s == 2:
+                for g in range(KG):
+                    quantize_pair(3, g)
+            if done >= 0:
+                add_product(done)
+            if s >= 1:
+                quantize_hidden(s - 1)
+            if done >= 0:
+                weight_and_store(done)
+            if s in (2, 3):
+                add_free_and_bias(s - 2)
+            if s == FG + 1:
+                for g in range(KG):
+                    quantize_chunk(2, g)
+            if 6 <= s < 10:
+                add_free_and_bias(s - 4)
+            if s == SLOTS - 1:
+                quantize_and_store_codes(0, 4)
+                store_scales(0, 4, [nc.sync])
 
-        def planes(x, count):
-            quantize_output(x, count)
-            store_codes(x, count)
-
-        extra = {"P": permute_w1, "Q": quantize_users, "C": add_free_and_bias, "Y": planes, "O": sort_users,
-                 "S": add_product, "IH": lambda s, h: interleave_half(s, h, nc.vector.tensor_copy),
-                 "IA": lambda s, h: interleave_half(s, h, nc.scalar.copy), "HH": quantize_half, "Z": output_passes, "T": transpose_output, "EY": evacuate_output, "B": weight_rounded,
-                 "SS": lambda x, n: store_scales(x, n, [nc.sync, nc.scalar] if x + n == TILES else [nc.sync]),
-                 "EV": lambda j, n: evacuate_output(j, n, nc.vector.tensor_copy), "I": interleave_hidden, "H": quantize_hidden, "QC": quantize_chunk, "A": round_output, "W": weight_and_store,
-                 "E": lambda pair, g: evacuate_users(pair, g, nc.vector.tensor_copy)}
-
-        def extras(steps):
-            for step in steps:
-                extra[step[0]](*step[1:])
-
-        for s in range(len(SLOTS)):
-            extras(VEC.get(s, []))
             for t in range(4):
                 for g in range(KG):
                     if s > 0 or g > 0:
                         hidden_pass(s, t, g)
-                evacuate_hidden(s, t)
-            for x in CAST_AFTER.get(s, []):
-                round_output(x)
-            for unit in TU_AFTER.get(s, []):
-                transpose_users(*unit)
-            if s == VEC_AFTER:
-                transpose_vectors()
-                evacuate_vectors()
-            for x in TY_AFTER.get(s, []):
-                transpose_output(x, 2)
-            for unit in EU_ACT.get(s, []):
-                evacuate_users(*unit)
-            for x in EY_AFTER.get(s, []):
-                evacuate_output(x, 2)
-            for x in CAST_LATE.get(s, []):
-                round_output(x)
-            for j in Z_AFTER.get(s, []):
-                output_passes(j)
+                empty_hidden(s, t)
 
-        extras(TAIL)
+            if 0 <= done < 4:
+                round_output(done)
+            if done > 4:
+                round_output(done - 1)
+            turned = {0: [2], 1: [3], FG: [4, 5]}.get(s, [])
+            for pair in turned:
+                for g in range(KG):
+                    turn_users(pair, g)
+            if s == 1:
+                spread_vectors()
+            if s == SLOTS - 2:
+                for j in (0, 2):
+                    turn_output(j, 2)
+                for j in (0, 2):
+                    empty_output(j, 2)
+            for pair in turned:
+                for g in range(KG):
+                    empty_users(pair, g)
+            if s >= OUT_LAG:
+                output_passes(s - OUT_LAG)
+
+        last = SLOTS - 1
+        interleave_hidden(last, nc.vector.tensor_copy, 0, 64)
+        interleave_hidden(last, nc.scalar.copy, 64, P)
+        round_output(6)
+        add_product(7)
+        quantize_hidden(last, 0, 256)
+        weight_and_store(7)
+        quantize_hidden(last, 256, 512)
+        round_output(7)
+        for j in (8, 9):
+            output_passes(j, 0, FG - 1)
+        for j in (8, 9):
+            output_passes(j, FG - 1)
+        for j in (10, 11):
+            output_passes(j)
+        for j in (4, 6):
+            turn_output(j, 2)
+        for j in (8, 9):
+            add_product(j)
+        for j in (8, 9):
+            weight_and_store(j)
+            round_output(j)
+        for j in (4, 6):
+            empty_output(j, 2)
+        turn_output(8, 2)
+        for j in (10, 11):
+            add_product(j)
+        weight_and_store(10)
+        round_output(10)
+        empty_output(8, 2)
+        weight_rounded(11)
+        quantize_and_store_codes(4, 4)
+        weight_and_store(11)
+        quantize_and_store_codes(8, 2)
+        for j in (10, 11):
+            turn_output(j, 1)
+            empty_output(j, 1)
+        quantize_and_store_codes(10, 2)
+        store_scales(4, 8, [nc.sync, nc.scalar])

@@ -29,6 +29,8 @@ H_RING = 3
 X_RING = 4
 OUT_LAG = 4
 PAIRED = (7, 9)
+ADD_SLOT = {0: 2, 2: 5, 3: 7, 4: 8, 5: 9}
+SORTED = 2
 
 
 def tile_user_tower_for_scoring_h1_kernel(
@@ -52,6 +54,7 @@ def tile_user_tower_for_scoring_h1_kernel(
         dw_col = tile("dw_col", [P, 4], BF16)
         u_head = tiles("u_head", 2 * KG, [P, 2, 512], BF16)
         u_rest = tiles("u_rest", PAIRS - 2, [P, 2, K], BF16)
+        u_sorted = tiles("u_sorted", KG, [P, 2, 2, P], F32)
         w1_first = tiles("w1_first", KG, [P, 1024], U8)
         w1_second = tile("w1_second", [P, KG, 1024], U8)
         w1_last = tile("w1_last", [P, KG, 2048], U8)
@@ -112,12 +115,17 @@ def tile_user_tower_for_scoring_h1_kernel(
                 return u_head[pair * KG + g][:].bitcast(F32)
             return u_rest[pair - 2][:].bitcast(F32)[:, :, g * 256 : (g + 1) * 256]
 
+        def sort_users(pair):
+            for g in range(KG):
+                nc.scalar.copy(out=u_sorted[g][:], in_=user_words(pair, g).rearrange("p i (q u) -> p i u q", u=2))
+
         def turn_users(pair, g):
             bank = take_bank(("u", pair, g))
             for i in range(2):
                 for u in range(2):
+                    src = u_sorted[g][:, i, u, :] if pair == SORTED else user_words(pair, g)[:, i, u:256:2]
                     at = (2 * i + u) * P
-                    nc.tensor.transpose(bank[:, at : at + P], user_words(pair, g)[:, i, u:256:2], ident[:])
+                    nc.tensor.transpose(bank[:, at : at + P], src, ident[:])
 
         def x_home(pair, g):
             return x_turned[(pair // 2 * KG + g) % X_RING][:, pair % 2 * 1024 : (pair % 2 + 1) * 1024]
@@ -151,13 +159,12 @@ def tile_user_tower_for_scoring_h1_kernel(
                 out=s1_dealt[fg][:].rearrange("p g (t m) -> p g t m", t=4), in_=src.rearrange("p g (m t) -> p g t m", t=4)
             )
 
-        def deal_group(fg):
+        def deal_codes(fg):
             src = w1_second[:] if fg == 1 else w1_last[:, :, (fg - 2) * 1024 : (fg - 1) * 1024]
             nc.vector.tensor_copy(
                 out=w1_dealt[fg][:].bitcast(U16).rearrange("p g (t m) -> p g t m", t=4),
                 in_=src.bitcast(U16).rearrange("p g (m t) -> p g t m", t=4),
             )
-            deal_scales(fg)
 
         def hidden_pass(s, t, g):
             c, fg = divmod(s, FG)
@@ -226,12 +233,12 @@ def tile_user_tower_for_scoring_h1_kernel(
                 in_=bank[:].rearrange("m (v u q) -> m v q u", v=2, u=2),
             )
 
-        def add_free_and_bias(pair):
-            c, half = divmod(pair, 2)
+        def add_free_and_bias(j, count):
+            c, i = divmod(j, 4)
             nc.vector.tensor_tensor(
-                out=y_pair[pair][:],
-                in0=free[c][:, 2 * half : 2 * half + 2, :],
-                in1=vectors[:, 0:1, :].to_broadcast([P, 2, D]),
+                out=y_pair[j // 2][:, j % 2 : j % 2 + count, :],
+                in0=free[c][:, i : i + count, :],
+                in1=vectors[:, 0:1, :].to_broadcast([P, count, D]),
                 op=ALU.add,
             )
 
@@ -322,35 +329,39 @@ def tile_user_tower_for_scoring_h1_kernel(
         quantize_pair(0, 1)
         deal_first_codes(1)
         quantize_pair(1, 1)
+        sort_users(SORTED)
 
         for s in range(SLOTS):
             done = s - 1 - OUT_LAG
             if s == 0:
-                deal_group(1)
-                deal_group(2)
+                for fg in (1, 2):
+                    deal_codes(fg)
+                    deal_scales(fg)
             if s == 1:
-                deal_group(3)
+                deal_codes(3)
             if s == 2:
                 for g in range(KG):
                     quantize_pair(2, g)
             if s >= 1:
                 interleave_hidden(s - 1)
+            if s == 1:
+                deal_scales(3)
             if s == 2:
                 for g in range(KG):
                     quantize_pair(3, g)
+            if s in (3, 4):
+                add_free_and_bias(s - 1, 1)
             if done >= 0:
                 add_product(done)
             if s >= 1:
                 quantize_hidden(s - 1)
             if done >= 0:
                 weight_and_store(done)
-            if s in (2, 3):
-                add_free_and_bias(s - 2)
-            if s == FG + 1:
-                for g in range(KG):
-                    quantize_chunk(2, g)
-            if 6 <= s < 10:
-                add_free_and_bias(s - 4)
+            if s in (FG + 1, FG + 2):
+                quantize_chunk(2, s - FG - 1)
+            for pair in ADD_SLOT:
+                if ADD_SLOT[pair] == s:
+                    add_free_and_bias(2 * pair, 2)
             if s == SLOTS - 1:
                 quantize_and_store_codes(0, 4)
                 store_scales(0, 4, [nc.sync])

@@ -28,8 +28,7 @@ BANKS = 8
 H_RING = 3
 X_RING = 4
 OUT_LAG = 4
-PAIRED = (7, 9)
-ADD_SLOT = {0: 2, 2: 5, 3: 7, 4: 8, 5: 9}
+PAIRED = (5, 6, 9)
 SORTED = 2
 
 
@@ -311,9 +310,9 @@ def tile_user_tower_for_scoring_h1_kernel(
         load_free(0)
         load_pair(4)
         load_pair(5)
+        load_free(1)
         nc.sync.dma_start(out=w2[:].bitcast(I32), in_=w2_words.rearrange("g p n -> p g n").bitcast(I32))
         load_scale_rows(s2, w2_scales)
-        load_free(1)
         load_free(2)
 
         for g in range(KG):
@@ -331,8 +330,13 @@ def tile_user_tower_for_scoring_h1_kernel(
         quantize_pair(1, 1)
         sort_users(SORTED)
 
+        def products_behind(s):
+            if s <= OUT_LAG:
+                return []
+            return [0, 1] if s == OUT_LAG + 1 else [s - OUT_LAG]
+
         for s in range(SLOTS):
-            done = s - 1 - OUT_LAG
+            done = products_behind(s - 1)
             if s == 0:
                 for fg in (1, 2):
                     deal_codes(fg)
@@ -351,17 +355,24 @@ def tile_user_tower_for_scoring_h1_kernel(
                     quantize_pair(3, g)
             if s in (3, 4):
                 add_free_and_bias(s - 1, 1)
-            if done >= 0:
-                add_product(done)
+            if s == 5:
+                add_free_and_bias(6, 1)
+            for j in done[:1]:
+                add_product(j)
             if s >= 1:
                 quantize_hidden(s - 1)
-            if done >= 0:
-                weight_and_store(done)
-            if s in (FG + 1, FG + 2):
-                quantize_chunk(2, s - FG - 1)
-            for pair in ADD_SLOT:
-                if ADD_SLOT[pair] == s:
-                    add_free_and_bias(2 * pair, 2)
+            for j in done[1:]:
+                add_product(j)
+            for j in done:
+                weight_and_store(j)
+            if s in (2, 4):
+                add_free_and_bias(2 * s - 4, 2)
+            if s == 5:
+                add_free_and_bias(7, 1)
+                for g in range(KG):
+                    quantize_chunk(2, g)
+            if s in (8, 9):
+                add_free_and_bias(2 * s - 8, 2)
             if s == SLOTS - 1:
                 quantize_and_store_codes(0, 4)
                 store_scales(0, 4, [nc.sync])
@@ -372,11 +383,12 @@ def tile_user_tower_for_scoring_h1_kernel(
                         hidden_pass(s, t, g)
                 empty_hidden(s, t)
 
-            if 0 <= done < 4:
-                round_output(done)
-            if done > 4:
-                round_output(done - 1)
-            turned = {0: [2], 1: [3], FG: [4, 5]}.get(s, [])
+            if s in (7, 8):
+                for j in (2 * s - 14, 2 * s - 13):
+                    round_output(j)
+            if s in (10, 11):
+                round_output(s - 6)
+            turned = {0: [2], 1: [3], 3: [4], 4: [5]}.get(s, [])
             for pair in turned:
                 for g in range(KG):
                     turn_users(pair, g)
@@ -390,8 +402,8 @@ def tile_user_tower_for_scoring_h1_kernel(
             for pair in turned:
                 for g in range(KG):
                     empty_users(pair, g)
-            if s >= OUT_LAG:
-                output_passes(s - OUT_LAG)
+            for j in products_behind(s):
+                output_passes(j)
 
         last = SLOTS - 1
         interleave_hidden(last, nc.vector.tensor_copy, 0, 64)

@@ -29,7 +29,6 @@ H_RING = 3
 X_RING = 4
 OUT_LAG = 4
 PAIRED = (5, 6, 9)
-SORTED = 2
 
 
 def tile_user_tower_for_scoring_h1_kernel(
@@ -53,7 +52,6 @@ def tile_user_tower_for_scoring_h1_kernel(
         dw_col = tile("dw_col", [P, 4], BF16)
         u_head = tiles("u_head", 2 * KG, [P, 2, 512], BF16)
         u_rest = tiles("u_rest", PAIRS - 2, [P, 2, K], BF16)
-        u_sorted = tiles("u_sorted", KG, [P, 2, 2, P], F32)
         w1_first = tiles("w1_first", KG, [P, 1024], U8)
         w1_second = tile("w1_second", [P, KG, 1024], U8)
         w1_last = tile("w1_last", [P, KG, 2048], U8)
@@ -114,17 +112,12 @@ def tile_user_tower_for_scoring_h1_kernel(
                 return u_head[pair * KG + g][:].bitcast(F32)
             return u_rest[pair - 2][:].bitcast(F32)[:, :, g * 256 : (g + 1) * 256]
 
-        def sort_users(pair):
-            for g in range(KG):
-                nc.scalar.copy(out=u_sorted[g][:], in_=user_words(pair, g).rearrange("p i (q u) -> p i u q", u=2))
-
         def turn_users(pair, g):
             bank = take_bank(("u", pair, g))
             for i in range(2):
                 for u in range(2):
-                    src = u_sorted[g][:, i, u, :] if pair == SORTED else user_words(pair, g)[:, i, u:256:2]
                     at = (2 * i + u) * P
-                    nc.tensor.transpose(bank[:, at : at + P], src, ident[:])
+                    nc.tensor.transpose(bank[:, at : at + P], user_words(pair, g)[:, i, u:256:2], ident[:])
 
         def x_home(pair, g):
             return x_turned[(pair // 2 * KG + g) % X_RING][:, pair % 2 * 1024 : (pair % 2 + 1) * 1024]
@@ -299,11 +292,11 @@ def tile_user_tower_for_scoring_h1_kernel(
             load_w1_first(g)
             if g == 0:
                 load_scale_rows(s1_first, w1_scales[:, :, :512])
-        nc.sync.dma_start(out=b1_col[:], in_=b1.rearrange("(g p t) -> p g t", p=P, t=4))
-        load_pair(2)
         load_w1(w1_second, 1, 2)
+        nc.sync.dma_start(out=b1_col[:], in_=b1.rearrange("(g p t) -> p g t", p=P, t=4))
         load_scale_rows(s1_rest, w1_scales[:, :, 512:])
         load_w1(w1_last, 2, 4)
+        load_pair(2)
         nc.sync.dma_start(out=b2_col[:], in_=b2.rearrange("(p t) -> p t", t=4))
         nc.sync.dma_start(out=dw_col[:], in_=dim_weight.rearrange("(p t) -> p t", t=4))
         load_pair(3)
@@ -328,7 +321,6 @@ def tile_user_tower_for_scoring_h1_kernel(
         quantize_pair(0, 1)
         deal_first_codes(1)
         quantize_pair(1, 1)
-        sort_users(SORTED)
 
         def products_behind(s):
             if s <= OUT_LAG:
@@ -338,23 +330,20 @@ def tile_user_tower_for_scoring_h1_kernel(
         for s in range(SLOTS):
             done = products_behind(s - 1)
             if s == 0:
-                for fg in (1, 2):
-                    deal_codes(fg)
-                    deal_scales(fg)
-            if s == 1:
+                deal_codes(1)
+                deal_scales(1)
+                deal_scales(2)
+                deal_codes(2)
                 deal_codes(3)
-            if s == 2:
-                for g in range(KG):
-                    quantize_pair(2, g)
             if s >= 1:
                 interleave_hidden(s - 1)
             if s == 1:
                 deal_scales(3)
-            if s == 2:
+            if s in (2, 3):
                 for g in range(KG):
-                    quantize_pair(3, g)
-            if s in (3, 4):
-                add_free_and_bias(s - 1, 1)
+                    quantize_pair(s, g)
+            if s == 4:
+                add_free_and_bias(3, 1)
             if s == 5:
                 add_free_and_bias(6, 1)
             for j in done[:1]:
@@ -367,6 +356,8 @@ def tile_user_tower_for_scoring_h1_kernel(
                 weight_and_store(j)
             if s in (2, 4):
                 add_free_and_bias(2 * s - 4, 2)
+            if s == 3:
+                add_free_and_bias(2, 1)
             if s == 5:
                 add_free_and_bias(7, 1)
                 for g in range(KG):
@@ -388,7 +379,7 @@ def tile_user_tower_for_scoring_h1_kernel(
                     round_output(j)
             if s in (10, 11):
                 round_output(s - 6)
-            turned = {0: [2], 1: [3], 3: [4], 4: [5]}.get(s, [])
+            turned = [s + 1] if 1 <= s <= OUT_LAG else []
             for pair in turned:
                 for g in range(KG):
                     turn_users(pair, g)

@@ -48,8 +48,6 @@ def tile_user_tower_for_scoring_h1_kernel(
 
         ident = tile("ident", [P, P], F32)
         b1_col = tile("b1_col", [P, FG, 4], BF16)
-        b2_col = tile("b2_col", [P, 4], BF16)
-        dw_col = tile("dw_col", [P, 4], BF16)
         u_head = tiles("u_head", 2 * KG, [P, 2, 512], BF16)
         u_rest = tiles("u_rest", PAIRS - 2, [P, 2, K], BF16)
         w1_first = tiles("w1_first", KG, [P, 1024], U8)
@@ -213,18 +211,6 @@ def tile_user_tower_for_scoring_h1_kernel(
                     stop=(fg == FG - 1),
                 )
 
-        def spread_vectors():
-            bank = take_bank(("v",))
-            for v, col in enumerate((b2_col, dw_col)):
-                words = col[:].bitcast(F32)
-                for u in range(2):
-                    at = (2 * v + u) * P
-                    nc.tensor.transpose(bank[:, at : at + P], words[:, u : u + 1].to_broadcast([P, P]), ident[:])
-            nc.scalar.copy(
-                out=vectors[:].bitcast(F32).rearrange("m v (q u) -> m v q u", u=2),
-                in_=bank[:].rearrange("m (v u q) -> m v q u", v=2, u=2),
-            )
-
         def add_free_and_bias(j, count):
             c, i = divmod(j, 4)
             nc.vector.tensor_tensor(
@@ -288,24 +274,24 @@ def tile_user_tower_for_scoring_h1_kernel(
 
         for g in range(KG):
             load_head(0, g)
+            if g == 1:
+                load_scale_rows(s1_first, w1_scales[:, :, :512])
             load_head(1, g)
             load_w1_first(g)
-            if g == 0:
-                load_scale_rows(s1_first, w1_scales[:, :, :512])
         load_w1(w1_second, 1, 2)
         nc.sync.dma_start(out=b1_col[:], in_=b1.rearrange("(g p t) -> p g t", p=P, t=4))
         load_scale_rows(s1_rest, w1_scales[:, :, 512:])
         load_w1(w1_last, 2, 4)
         load_pair(2)
-        nc.sync.dma_start(out=b2_col[:], in_=b2.rearrange("(p t) -> p t", t=4))
-        nc.sync.dma_start(out=dw_col[:], in_=dim_weight.rearrange("(p t) -> p t", t=4))
         load_pair(3)
+        nc.sync.dma_start(out=vectors[:, 0, :], in_=b2.partition_broadcast(P))
         load_free(0)
         load_pair(4)
         load_pair(5)
         load_free(1)
         nc.sync.dma_start(out=w2[:].bitcast(I32), in_=w2_words.rearrange("g p n -> p g n").bitcast(I32))
         load_scale_rows(s2, w2_scales)
+        nc.sync.dma_start(out=vectors[:, 1, :], in_=dim_weight.partition_broadcast(P))
         load_free(2)
 
         for g in range(KG):
@@ -383,8 +369,6 @@ def tile_user_tower_for_scoring_h1_kernel(
             for pair in turned:
                 for g in range(KG):
                     turn_users(pair, g)
-            if s == 1:
-                spread_vectors()
             if s == SLOTS - 2:
                 for j in (0, 2):
                     turn_output(j, 2)

@@ -47,6 +47,7 @@ def tile_user_tower_for_scoring_h1_kernel(
             return [tile("%s%d" % (name, i), shape, dtype, align) for i in range(count)]
 
         ident = tile("ident", [P, P], F32)
+        b1_rows = tile("b1_rows", [P, 512], BF16)
         b1_col = tile("b1_col", [P, FG, 4], BF16)
         u_head = tiles("u_head", 2 * KG, [P, 2, 512], BF16)
         u_rest = tiles("u_rest", PAIRS - 2, [P, 2, K], BF16)
@@ -154,6 +155,14 @@ def tile_user_tower_for_scoring_h1_kernel(
             nc.vector.tensor_copy(
                 out=w1_dealt[fg][:].bitcast(U16).rearrange("p g (t m) -> p g t m", t=4),
                 in_=src.bitcast(U16).rearrange("p g (m t) -> p g t m", t=4),
+            )
+
+        def turn_bias():
+            bank = take_bank(("b",))
+            for u in range(2):
+                nc.tensor.transpose(bank[:, u * P : (u + 1) * P], b1_rows[:].bitcast(F32)[:, u:256:2], ident[:])
+            nc.scalar.copy(
+                out=b1_col[:].bitcast(F32), in_=bank[:, :256].rearrange("p (u r) -> p r u", u=2)[:, :FG, :]
             )
 
         def hidden_pass(s, t, g):
@@ -268,18 +277,22 @@ def tile_user_tower_for_scoring_h1_kernel(
                     out=out_2[0][q:16:4, cols].bitcast(I32), in_=y_scales[q:P:32, cols].bitcast(I32)
                 )
 
-        make_identity(nc, ident[:])
-        for scales in (s1_first, s1_rest, s2):
+        nc.vector.memset(b1_rows[:], 0.0)
+        nc.vector.memset(s1_first[:].bitcast(I32), 0)
+        nc.vector.memset(ident[:], 0.0)
+        make_identity(nc, ident[:], nomemset=True)
+        for scales in (s1_rest, s2):
             nc.vector.memset(scales[:].bitcast(I32), 0)
 
         for g in range(KG):
             load_head(0, g)
+            if g == 0:
+                nc.sync.dma_start(out=b1_rows[:FG, :], in_=b1.rearrange("(g n) -> g n", g=FG))
             if g == 1:
                 load_scale_rows(s1_first, w1_scales[:, :, :512])
             load_head(1, g)
             load_w1_first(g)
         load_w1(w1_second, 1, 2)
-        nc.sync.dma_start(out=b1_col[:], in_=b1.rearrange("(g p t) -> p g t", p=P, t=4))
         load_scale_rows(s1_rest, w1_scales[:, :, 512:])
         load_w1(w1_last, 2, 4)
         load_pair(2)
@@ -298,6 +311,8 @@ def tile_user_tower_for_scoring_h1_kernel(
             for pair in range(2):
                 turn_users(pair, g)
                 empty_users(pair, g)
+                if (pair, g) == (1, 0):
+                    turn_bias()
         deal_first_codes(0)
         quantize_pair(0, 0)
         deal_scales(0)

@@ -150,9 +150,9 @@ def tile_user_tower_for_scoring_h1_kernel(
                 out=s1_dealt[fg][:].rearrange("p g (t m) -> p g t m", t=4), in_=src.rearrange("p g (m t) -> p g t m", t=4)
             )
 
-        def deal_codes(fg):
+        def deal_codes(fg, copy=nc.vector.tensor_copy):
             src = w1_second[:] if fg == 1 else w1_last[:, :, (fg - 2) * 1024 : (fg - 1) * 1024]
-            nc.vector.tensor_copy(
+            copy(
                 out=w1_dealt[fg][:].bitcast(U16).rearrange("p g (t m) -> p g t m", t=4),
                 in_=src.bitcast(U16).rearrange("p g (m t) -> p g t m", t=4),
             )
@@ -242,11 +242,8 @@ def tile_user_tower_for_scoring_h1_kernel(
         def sorted_round(j):
             return y_round[j][:].rearrange("p (u q e) -> p u q e", u=2, e=2)
 
-        def round_output(j):
-            nc.scalar.copy(out=sorted_round(j), in_=by_words(y[j]))
-
-        def weight_rounded(j):
-            nc.vector.tensor_tensor(out=sorted_round(j), in0=by_words(y[j]), in1=by_words(vectors[:, 1, :]), op=ALU.mult)
+        def round_output(j, copy=nc.scalar.copy):
+            copy(out=sorted_round(j), in_=by_words(y[j]))
 
         def turn_output(j, count):
             bank = take_bank(("y", j))
@@ -331,15 +328,19 @@ def tile_user_tower_for_scoring_h1_kernel(
         for s in range(SLOTS):
             done = products_behind(s - 1)
             if s == 0:
-                deal_codes(1)
+                deal_codes(1, nc.scalar.copy)
                 deal_scales(1)
                 deal_scales(2)
                 deal_codes(2)
                 deal_codes(3)
-            if s >= 1:
-                interleave_hidden(s - 1)
-            if s == 1:
                 deal_scales(3)
+            if s == 1:
+                for half in range(2):
+                    interleave_hidden(0, nc.vector.tensor_copy, 64 * half, 64 * half + 64)
+                quantize_hidden(0, 0, 256)
+                quantize_hidden(0, 256, 512)
+            if s >= 2:
+                interleave_hidden(s - 1)
             if s in (2, 3):
                 for g in range(KG):
                     quantize_pair(s, g)
@@ -349,7 +350,7 @@ def tile_user_tower_for_scoring_h1_kernel(
                 add_free_and_bias(6, 1)
             for j in done[:1]:
                 add_product(j)
-            if s >= 1:
+            if s >= 2:
                 quantize_hidden(s - 1)
             for j in done[1:]:
                 add_product(j)
@@ -423,14 +424,14 @@ def tile_user_tower_for_scoring_h1_kernel(
         for j in (10, 11):
             add_product(j)
         weight_and_store(10)
-        round_output(10)
         empty_output(8, 2)
-        weight_rounded(11)
-        quantize_and_store_codes(4, 4)
         weight_and_store(11)
-        quantize_and_store_codes(8, 2)
+        for j in (10, 11):
+            round_output(j, nc.vector.tensor_copy)
+        quantize_and_store_codes(4, 4)
         for j in (10, 11):
             turn_output(j, 1)
             empty_output(j, 1)
+        quantize_and_store_codes(8, 2)
         quantize_and_store_codes(10, 2)
         store_scales(4, 8, [nc.sync, nc.scalar])

@@ -25,6 +25,7 @@ TILES = M // P
 PAIRS = TILES // 2
 SLOTS = CHUNKS * FG
 BANKS = 8
+ROW = 520
 H_RING = 3
 X_RING = 4
 OUT_LAG = 4
@@ -65,7 +66,7 @@ def tile_user_tower_for_scoring_h1_kernel(
         x_turned = tiles("x_turned", X_RING, [P, 2048], BF16)
         x_codes = tiles("x_codes", CHUNKS * KG, [P, 512], U32, 256)
         x_scales = tiles("x_scales", CHUNKS * KG, [P, 512], U8, 256)
-        h_rows = tiles("h_rows", H_RING, [P, 2048], BF16)
+        h_rows = tiles("h_rows", H_RING, [P, 4, ROW], BF16)
         h_words = tiles("h_words", H_RING, [P, 2048], BF16)
         h_codes = tiles("h_codes", SLOTS, [P, 512], U32, 256)
         h_scales = tiles("h_scales", SLOTS, [P, 512], U8, 256)
@@ -178,25 +179,27 @@ def tile_user_tower_for_scoring_h1_kernel(
                 stop=(g == KG - 1),
             )
 
+        def paired_rows(s):
+            return h_rows[s % H_RING][:].rearrange("p t m -> p (t m)")[:, :2048]
+
         def empty_hidden(s, t):
-            rows = h_rows[s % H_RING][:]
             if s in PAIRED:
-                dst = rows.rearrange("p (u m e) -> p u m e", u=2, e=2)[:, t // 2, :, t % 2]
+                dst = paired_rows(s).rearrange("p (u m e) -> p u m e", u=2, e=2)[:, t // 2, :, t % 2]
             else:
-                dst = rows[:, t * 512 : (t + 1) * 512]
+                dst = h_rows[s % H_RING][:, t, :512]
             nc.scalar.activation(out=dst, in_=held[("h", s, t)][:], func=ACT.Relu, bias=b1_col[:, s % FG, t : t + 1])
 
-        def interleave_hidden(s, copy=nc.vector.tensor_copy, first=0, last=P):
-            rows, words = h_rows[s % H_RING][:], h_words[s % H_RING][:]
+        def interleave_hidden(s, copy=nc.vector.tensor_copy, first=0, last=512):
+            words = h_words[s % H_RING][:]
             if s in PAIRED:
                 copy(
                     out=words.bitcast(F32).rearrange("p (m u) -> p m u", u=2),
-                    in_=rows.bitcast(F32).rearrange("p (u m) -> p m u", u=2),
+                    in_=paired_rows(s).bitcast(F32).rearrange("p (u m) -> p m u", u=2),
                 )
             else:
                 copy(
-                    out=words.rearrange("p (c i t) -> p c t i", i=4, t=4)[:, first:last],
-                    in_=rows.rearrange("p (t c i) -> p c t i", i=4, t=4)[:, first:last],
+                    out=words.rearrange("p (c i t) -> p c t i", i=2, t=4)[:, first // 2 : last // 2],
+                    in_=h_rows[s % H_RING][:, :, first:last].rearrange("p t (c i) -> p c t i", i=2),
                 )
 
         def quantize_hidden(s, first=0, last=512):
@@ -336,7 +339,7 @@ def tile_user_tower_for_scoring_h1_kernel(
                 deal_scales(3)
             if s == 1:
                 for half in range(2):
-                    interleave_hidden(0, nc.vector.tensor_copy, 64 * half, 64 * half + 64)
+                    interleave_hidden(0, nc.vector.tensor_copy, 256 * half, 256 * half + 256)
                 quantize_hidden(0, 0, 256)
                 quantize_hidden(0, 256, 512)
             if s >= 2:
@@ -397,8 +400,8 @@ def tile_user_tower_for_scoring_h1_kernel(
                 output_passes(j)
 
         last = SLOTS - 1
-        interleave_hidden(last, nc.vector.tensor_copy, 0, 64)
-        interleave_hidden(last, nc.scalar.copy, 64, P)
+        interleave_hidden(last, nc.vector.tensor_copy, 0, 256)
+        interleave_hidden(last, nc.scalar.copy, 256, 512)
         round_output(6)
         add_product(7)
         quantize_hidden(last, 0, 256)

@@ -24,12 +24,11 @@ CHUNKS = M // 512
 TILES = M // P
 PAIRS = TILES // 2
 SLOTS = CHUNKS * FG
-BANKS = 8
+RING = 7
 ROW = 520
 H_RING = 3
 X_RING = 4
-OUT_LAG = 4
-PAIRED = (5, 6, 9)
+SHARE = {0: 0, 2: 128, 3: 256, 4: 384, 5: 448}
 
 
 def tile_user_tower_for_scoring_h1_kernel(
@@ -50,6 +49,7 @@ def tile_user_tower_for_scoring_h1_kernel(
         ident = tile("ident", [P, P], F32)
         b1_rows = tile("b1_rows", [P, 512], BF16)
         b1_col = tile("b1_col", [P, FG, 4], BF16)
+        vector_cols = tiles("vector_col", 2, [P, 4], BF16)
         u_head = tiles("u_head", 2 * KG, [P, 2, 512], BF16)
         u_rest = tiles("u_rest", PAIRS - 2, [P, 2, K], BF16)
         w1_first = tiles("w1_first", KG, [P, 1024], U8)
@@ -59,29 +59,29 @@ def tile_user_tower_for_scoring_h1_kernel(
         s1_first = tile("s1_first", [P, KG, 512], U8)
         s1_rest = tile("s1_rest", [P, KG, 1536], U8)
         s1_dealt = tiles("s1_dealt", FG, [P, KG, 512], U8, 256)
+        u_sorted = tiles("u_sorted", 2, [P, 2 * K], BF16)
         w2 = tile("w2", [P, FG, 1024], U8, 256)
         s2 = tile("s2", [P, FG, D], U8, 256)
-        vectors = tile("vectors", [P, 2, D], BF16)
         free = tiles("free", CHUNKS, [P, 4, D], BF16)
         x_turned = tiles("x_turned", X_RING, [P, 2048], BF16)
         x_codes = tiles("x_codes", CHUNKS * KG, [P, 512], U32, 256)
         x_scales = tiles("x_scales", CHUNKS * KG, [P, 512], U8, 256)
         h_rows = tiles("h_rows", H_RING, [P, 4, ROW], BF16)
-        h_words = tiles("h_words", H_RING, [P, 2048], BF16)
+        h_words = tile("h_words", [P, 2048], BF16)
         h_codes = tiles("h_codes", SLOTS, [P, 512], U32, 256)
         h_scales = tiles("h_scales", SLOTS, [P, 512], U8, 256)
-        y_pair = tiles("y", PAIRS, [P, 2, D], F32)
-        y = [y_pair[j // 2][:, j % 2, :] for j in range(TILES)]
+        y = tiles("y", TILES, [P, D], F32)
         y_round = tiles("y_round", TILES, [P, D], BF16)
         y_turned = tile("y_turned", [P, TILES * D], BF16)
         y_codes = tile("y_codes", [P, M], U32)
         y_scales = tile("y_scales", [P, M], U8)
-        banks = [ps.tile([P, 512], F32, name="bank%d" % i) for i in range(BANKS)]
+        banks = [ps.tile([P, 512], F32, name="bank%d" % i) for i in range(RING)]
+        vectors = ps.tile([P, 2, 256], F32, name="vectors")
 
         held = {}
 
         def take_bank(key):
-            held[key] = banks[len(held) % BANKS]
+            held[key] = banks[len(held) % RING]
             return held[key]
 
         def load_head(pair, g):
@@ -107,23 +107,38 @@ def tile_user_tower_for_scoring_h1_kernel(
         def load_free(c):
             nc.sync.dma_start(out=free[c][:], in_=user_free[c * 512 : (c + 1) * 512, :].rearrange("(i p) d -> p i d", p=P))
 
+        def spread_vectors():
+            for v in range(2):
+                for u in range(2):
+                    column = vector_cols[v][:].bitcast(F32)[:, u : u + 1].to_broadcast([P, P])
+                    nc.tensor.transpose(vectors[:, v, u:256:2], column, ident[:])
+
         def user_words(pair, g):
-            if pair < 2:
-                return u_head[pair * KG + g][:].bitcast(F32)
-            return u_rest[pair - 2][:].bitcast(F32)[:, :, g * 256 : (g + 1) * 256]
+            return u_head[pair * KG + g][:].bitcast(F32)
+
+        def sort_users(pair):
+            nc.vector.tensor_copy(
+                out=u_sorted[pair % 2][:].bitcast(F32).rearrange("p (r u q) -> p r u q", u=2, q=P),
+                in_=u_rest[pair - 2][:].bitcast(F32).rearrange("p i (g q u) -> p (i g) u q", u=2, q=P),
+            )
 
         def turn_users(pair, g):
             bank = take_bank(("u", pair, g))
             for i in range(2):
                 for u in range(2):
                     at = (2 * i + u) * P
-                    nc.tensor.transpose(bank[:, at : at + P], user_words(pair, g)[:, i, u:256:2], ident[:])
+                    if pair < 2:
+                        words = user_words(pair, g)[:, i, u:256:2]
+                    else:
+                        first = ((i * KG + g) * 2 + u) * P
+                        words = u_sorted[pair % 2][:].bitcast(F32)[:, first : first + P]
+                    nc.tensor.transpose(bank[:, at : at + P], words, ident[:])
 
         def x_home(pair, g):
             return x_turned[(pair // 2 * KG + g) % X_RING][:, pair % 2 * 1024 : (pair % 2 + 1) * 1024]
 
-        def empty_users(pair, g):
-            nc.scalar.copy(
+        def empty_users(pair, g, copy=nc.scalar.copy):
+            copy(
                 out=x_home(pair, g).bitcast(F32).rearrange("p (i m u) -> p i m u", i=2, u=2),
                 in_=held[("u", pair, g)][:].rearrange("p (i u m) -> p i m u", i=2, u=2),
             )
@@ -162,51 +177,50 @@ def tile_user_tower_for_scoring_h1_kernel(
             bank = take_bank(("b",))
             for u in range(2):
                 nc.tensor.transpose(bank[:, u * P : (u + 1) * P], b1_rows[:].bitcast(F32)[:, u:256:2], ident[:])
-            nc.scalar.copy(
-                out=b1_col[:].bitcast(F32), in_=bank[:, :256].rearrange("p (u r) -> p r u", u=2)[:, :FG, :]
-            )
+            nc.scalar.copy(out=b1_col[:].bitcast(F32), in_=bank[:, :256].rearrange("p (u r) -> p r u", u=2)[:, :FG, :])
 
-        def hidden_pass(s, t, g):
+        def hidden_pass(s, t, g, first=0, last=512):
             c, fg = divmod(s, FG)
-            bank = take_bank(("h", s, t)) if g == 0 else held[("h", s, t)]
+            bank = take_bank(("h", s, t, first)) if g == 0 else held[("h", s, t, first)]
             nc.tensor.matmul_mx(
-                out=bank[:],
+                out=bank[:, : last - first],
                 lhsT=w1_dealt[fg][:, g, t * 256 : (t + 1) * 256].bitcast(FP4X4),
                 lhsT_scale=s1_dealt[fg][:, g, t * P : (t + 1) * P],
-                rhs=x_codes[c * KG + g][:].bitcast(FP8X4),
-                rhs_scale=x_scales[c * KG + g][:],
+                rhs=x_codes[c * KG + g][:, first:last].bitcast(FP8X4),
+                rhs_scale=x_scales[c * KG + g][:, first:last],
                 start=(g == 0),
                 stop=(g == KG - 1),
             )
 
-        def paired_rows(s):
-            return h_rows[s % H_RING][:].rearrange("p t m -> p (t m)")[:, :2048]
+        def empty_hidden(s, t, first=0, last=512):
+            nc.scalar.activation(
+                out=h_rows[s % H_RING][:, t, first:last],
+                in_=held[("h", s, t, first)][:, : last - first],
+                func=ACT.Relu,
+                bias=b1_col[:, s % FG, t : t + 1],
+            )
 
-        def empty_hidden(s, t):
-            if s in PAIRED:
-                dst = paired_rows(s).rearrange("p (u m e) -> p u m e", u=2, e=2)[:, t // 2, :, t % 2]
-            else:
-                dst = h_rows[s % H_RING][:, t, :512]
-            nc.scalar.activation(out=dst, in_=held[("h", s, t)][:], func=ACT.Relu, bias=b1_col[:, s % FG, t : t + 1])
+        def interleave_hidden(s, copy, first, last):
+            copy(
+                out=h_words[:].rearrange("p (c i t) -> p c t i", i=2, t=4)[:, first // 2 : last // 2],
+                in_=h_rows[s % H_RING][:, :, first:last].rearrange("p t (c i) -> p c t i", i=2),
+            )
 
-        def interleave_hidden(s, copy=nc.vector.tensor_copy, first=0, last=512):
-            words = h_words[s % H_RING][:]
-            if s in PAIRED:
-                copy(
-                    out=words.bitcast(F32).rearrange("p (m u) -> p m u", u=2),
-                    in_=paired_rows(s).bitcast(F32).rearrange("p (u m) -> p m u", u=2),
-                )
-            else:
-                copy(
-                    out=words.rearrange("p (c i t) -> p c t i", i=2, t=4)[:, first // 2 : last // 2],
-                    in_=h_rows[s % H_RING][:, :, first:last].rearrange("p t (c i) -> p c t i", i=2),
-                )
+        def interleave_on_gpsimd(s, count):
+            nc.gpsimd.tensor_scalar(
+                out=h_words[:, : 4 * count].rearrange("p (m t) -> p m t", t=4),
+                in0=h_rows[s % H_RING][:, :, :count].rearrange("p t m -> p m t"),
+                scalar1=1.0,
+                scalar2=0.0,
+                op0=ALU.mult,
+                op1=ALU.add,
+            )
 
         def quantize_hidden(s, first=0, last=512):
             nc.vector.quantize_mx(
                 out=h_codes[s][:, first:last].bitcast(FP8X4),
                 scales=h_scales[s][:, first:last],
-                in_=h_words[s % H_RING][:, 4 * first : 4 * last],
+                in_=h_words[:, 4 * first : 4 * last],
             )
 
         def output_passes(j, first=0, last=FG):
@@ -223,30 +237,47 @@ def tile_user_tower_for_scoring_h1_kernel(
                     stop=(fg == FG - 1),
                 )
 
-        def add_free_and_bias(j, count):
+        def add_free_and_bias(j):
             c, i = divmod(j, 4)
-            nc.vector.tensor_tensor(
-                out=y_pair[j // 2][:, j % 2 : j % 2 + count, :],
-                in0=free[c][:, i : i + count, :],
-                in1=vectors[:, 0:1, :].to_broadcast([P, count, D]),
-                op=ALU.add,
-            )
+            nc.vector.tensor_tensor(out=y[j][:], in0=vectors[:, 0, :].bitcast(BF16), in1=free[c][:, i, :], op=ALU.add)
 
         def add_product(j):
-            nc.vector.tensor_tensor(out=y[j], in0=held[("z", j)][:], in1=y[j], op=ALU.add)
+            nc.vector.tensor_tensor(out=y[j][:], in0=held[("z", j)][:], in1=y[j][:], op=ALU.add)
+
+        def add_product_to_free(j):
+            c, i = divmod(j, 4)
+            nc.vector.tensor_tensor(out=y[j][:], in0=held[("z", j)][:], in1=free[c][:, i, :], op=ALU.add)
+
+        def add_bias(j):
+            nc.vector.tensor_tensor(out=y[j][:], in0=vectors[:, 0, :].bitcast(BF16), in1=y[j][:], op=ALU.add)
 
         def weight_and_store(j):
-            nc.vector.tensor_tensor(out=y[j], in0=y[j], in1=vectors[:, 1, :], op=ALU.mult)
-            nc.sync.dma_start(out=out_0[j * P : (j + 1) * P, :], in_=y[j])
-
-        def by_words(ap):
-            return ap.rearrange("p (q u e) -> p u q e", u=2, e=2)
-
-        def sorted_round(j):
-            return y_round[j][:].rearrange("p (u q e) -> p u q e", u=2, e=2)
+            nc.vector.tensor_tensor(out=y[j][:], in0=vectors[:, 1, :].bitcast(BF16), in1=y[j][:], op=ALU.mult)
+            nc.sync.dma_start(out=out_0[j * P : (j + 1) * P, :], in_=y[j][:])
 
         def round_output(j, copy=nc.scalar.copy):
-            copy(out=sorted_round(j), in_=by_words(y[j]))
+            copy(
+                out=y_round[j][:].rearrange("p (u q e) -> p u q e", u=2, e=2),
+                in_=y[j][:].rearrange("p (q u e) -> p u q e", u=2, e=2),
+            )
+
+        def weight_and_round(j):
+            nc.vector.tensor_tensor(
+                out=y_round[j][:].rearrange("p (u q e) -> p u q e", u=2, e=2),
+                in0=vectors[:, 1, :].bitcast(BF16).rearrange("p (q u e) -> p u q e", u=2, e=2),
+                in1=y[j][:].rearrange("p (q u e) -> p u q e", u=2, e=2),
+                op=ALU.mult,
+            )
+
+        def round_on_gpsimd(j):
+            nc.gpsimd.tensor_scalar(
+                out=y_round[j][:].rearrange("p (u q e) -> p u q e", u=2, e=2),
+                in0=y[j][:].rearrange("p (q u e) -> p u q e", u=2, e=2),
+                scalar1=1.0,
+                scalar2=0.0,
+                op0=ALU.mult,
+                op1=ALU.add,
+            )
 
         def turn_output(j, count):
             bank = take_bank(("y", j))
@@ -284,6 +315,8 @@ def tile_user_tower_for_scoring_h1_kernel(
         for scales in (s1_rest, s2):
             nc.vector.memset(scales[:].bitcast(I32), 0)
 
+        for v, vector in enumerate((b2, dim_weight)):
+            nc.scalar.dma_start(out=vector_cols[v][:], in_=vector.rearrange("(p e) -> p e", e=4))
         for g in range(KG):
             load_head(0, g)
             if g == 0:
@@ -294,17 +327,15 @@ def tile_user_tower_for_scoring_h1_kernel(
             load_w1_first(g)
         load_w1(w1_second, 1, 2)
         load_scale_rows(s1_rest, w1_scales[:, :, 512:])
-        load_w1(w1_last, 2, 4)
         load_pair(2)
         load_pair(3)
-        nc.sync.dma_start(out=vectors[:, 0, :], in_=b2.partition_broadcast(P))
+        load_w1(w1_last, 2, 4)
         load_free(0)
         load_pair(4)
         load_pair(5)
         load_free(1)
         nc.sync.dma_start(out=w2[:].bitcast(I32), in_=w2_words.rearrange("g p n -> p g n").bitcast(I32))
         load_scale_rows(s2, w2_scales)
-        nc.sync.dma_start(out=vectors[:, 1, :], in_=dim_weight.partition_broadcast(P))
         load_free(2)
 
         for g in range(KG):
@@ -313,6 +344,8 @@ def tile_user_tower_for_scoring_h1_kernel(
                 empty_users(pair, g)
                 if (pair, g) == (1, 0):
                     turn_bias()
+                if (pair, g) == (0, 1):
+                    spread_vectors()
         deal_first_codes(0)
         quantize_pair(0, 0)
         deal_scales(0)
@@ -324,54 +357,53 @@ def tile_user_tower_for_scoring_h1_kernel(
         quantize_pair(1, 1)
 
         def products_behind(s):
-            if s <= OUT_LAG:
-                return []
-            return [0, 1] if s == OUT_LAG + 1 else [s - OUT_LAG]
+            return {5: [0], 6: [1], 7: [2], 8: [3], 9: [4], 10: [5, 6], 11: [7]}.get(s, [])
+
+        A, B, W, C, Z, E = add_product_to_free, add_bias, weight_and_store, add_free_and_bias, add_product, lambda pair: empty_users(pair, 1, nc.vector.tensor_copy)
+        window = {2: [(C, 0), (E, 3)], 4: [(C, 1), (C, 2)], 5: [(C, 3), (C, 4), (C, 5)], 6: [(Z, 0), (E, 5), (C, 6), (W, 0)], 7: [(Z, 1), (C, 7), (W, 1)], 8: [(Z, 2), (C, 8), (W, 2)], 9: [(Z, 3), (C, 9), (W, 3)], 10: [(Z, 4), (C, 10), (C, 11), (W, 4)], 11: [(Z, 5), (Z, 6), (W, 5), (W, 6)]}
 
         for s in range(SLOTS):
-            done = products_behind(s - 1)
             if s == 0:
                 deal_codes(1, nc.scalar.copy)
                 deal_scales(1)
                 deal_scales(2)
-                deal_codes(2)
-                deal_codes(3)
                 deal_scales(3)
-            if s == 1:
-                for half in range(2):
-                    interleave_hidden(0, nc.vector.tensor_copy, 256 * half, 256 * half + 256)
-                quantize_hidden(0, 0, 256)
-                quantize_hidden(0, 256, 512)
-            if s >= 2:
-                interleave_hidden(s - 1)
-            if s in (2, 3):
-                for g in range(KG):
-                    quantize_pair(s, g)
-            if s == 4:
-                add_free_and_bias(3, 1)
-            if s == 5:
-                add_free_and_bias(6, 1)
-            for j in done[:1]:
-                add_product(j)
-            if s >= 2:
-                quantize_hidden(s - 1)
-            for j in done[1:]:
-                add_product(j)
-            for j in done:
-                weight_and_store(j)
-            if s in (2, 4):
-                add_free_and_bias(2 * s - 4, 2)
-            if s == 3:
-                add_free_and_bias(2, 1)
-            if s == 5:
-                add_free_and_bias(7, 1)
-                for g in range(KG):
-                    quantize_chunk(2, g)
-            if s in (8, 9):
-                add_free_and_bias(2 * s - 8, 2)
-            if s == SLOTS - 1:
-                quantize_and_store_codes(0, 4)
-                store_scales(0, 4, [nc.sync])
+                for pair in (2, 3):
+                    sort_users(pair)
+                deal_codes(2)
+            if s >= 1:
+                work = window.get(s, [])
+                share = SHARE[len(work)]
+                if share:
+                    interleave_on_gpsimd(s - 1, share)
+                for step, j in work:
+                    step(j)
+                interleave_hidden(s - 1, nc.vector.tensor_copy, share, 512)
+                between = s == 1
+                if s == 1:
+                    deal_codes(3)
+                for pair in {}.get(s, []):
+                    for g in range(KG):
+                        quantize_pair(pair, g)
+                    between = True
+                for pair in {3: [5]}.get(s, []):
+                    sort_users(pair)
+                    between = True
+                for c, g in {2: [(1, 0), (1, 1)], 6: [(2, 0), (2, 1)]}.get(s, []):
+                    quantize_chunk(c, g)
+                    between = True
+                if s == SLOTS - 1:
+                    quantize_and_store_codes(0, 4)
+                    store_scales(0, 4, [nc.sync])
+                    between = True
+                if between and not share:
+                    quantize_hidden(s - 1)
+                else:
+                    cut = share if share in (128, 384) else 256
+                    quantize_hidden(s - 1, 0, cut)
+                    quantize_hidden(s - 1, cut, 512)
+                for step, j in {2: [(sort_users, 4)]}.get(s, []):
+                    step(j)
 
             for t in range(4):
                 for g in range(KG):
@@ -379,25 +411,23 @@ def tile_user_tower_for_scoring_h1_kernel(
                         hidden_pass(s, t, g)
                 empty_hidden(s, t)
 
-            if s in (7, 8):
-                for j in (2 * s - 14, 2 * s - 13):
-                    round_output(j)
-            if s in (10, 11):
-                round_output(s - 6)
-            turned = [s + 1] if 1 <= s <= OUT_LAG else []
-            for pair in turned:
-                for g in range(KG):
-                    turn_users(pair, g)
+            for j in {7: [0], 8: [1], 9: [2], 10: [3, 4], 11: [5]}.get(s, []):
+                round_output(j)
             if s == SLOTS - 2:
+                for j in products_behind(s):
+                    output_passes(j)
                 for j in (0, 2):
                     turn_output(j, 2)
-                for j in (0, 2):
                     empty_output(j, 2)
-            for pair in turned:
-                for g in range(KG):
-                    empty_users(pair, g)
-            for j in products_behind(s):
-                output_passes(j)
+            turned = {1: [2, 3], 5: [4, 5]}.get(s, [])
+            for g in range(KG):
+                for pair in turned:
+                    turn_users(pair, g)
+                    if g == 0 or pair not in (3, 5):
+                        empty_users(pair, g)
+            if s != SLOTS - 2:
+                for j in products_behind(s):
+                    output_passes(j)
 
         last = SLOTS - 1
         interleave_hidden(last, nc.vector.tensor_copy, 0, 256)

@@ -28,7 +28,7 @@ RING = 7
 ROW = 520
 H_RING = 3
 X_RING = 4
-SHARE = {0: 0, 2: 128, 3: 256, 4: 384, 5: 448}
+SHARE = {0: 0, 1: 0, 2: 128, 3: 256, 4: 384, 5: 512}
 
 
 def tile_user_tower_for_scoring_h1_kernel(
@@ -67,7 +67,8 @@ def tile_user_tower_for_scoring_h1_kernel(
         x_codes = tiles("x_codes", CHUNKS * KG, [P, 512], U32, 256)
         x_scales = tiles("x_scales", CHUNKS * KG, [P, 512], U8, 256)
         h_rows = tiles("h_rows", H_RING, [P, 4, ROW], BF16)
-        h_words = tile("h_words", [P, 2048], BF16)
+        h_front = tile("h_front", [P, 2048], BF16)
+        h_back = tiles("h_back", 2, [P, 1536], BF16)
         h_codes = tiles("h_codes", SLOTS, [P, 512], U32, 256)
         h_scales = tiles("h_scales", SLOTS, [P, 512], U8, 256)
         y = tiles("y", TILES, [P, D], F32)
@@ -192,23 +193,31 @@ def tile_user_tower_for_scoring_h1_kernel(
                 stop=(g == KG - 1),
             )
 
+        def rows_of(s, first):
+            return h_rows[(s + (s == SLOTS - 1 and first > 0)) % H_RING]
+
         def empty_hidden(s, t, first=0, last=512):
             nc.scalar.activation(
-                out=h_rows[s % H_RING][:, t, first:last],
+                out=rows_of(s, first)[:, t, first:last],
                 in_=held[("h", s, t, first)][:, : last - first],
                 func=ACT.Relu,
                 bias=b1_col[:, s % FG, t : t + 1],
             )
 
-        def interleave_hidden(s, copy, first, last):
+        def h_words(s, cut, first, last):
+            if first < cut:
+                return h_front[:, 4 * first : 4 * last]
+            return h_back[s % 2][:, 4 * (first - cut) : 4 * (last - cut)]
+
+        def interleave_hidden(s, copy, cut, first, last):
             copy(
-                out=h_words[:].rearrange("p (c i t) -> p c t i", i=2, t=4)[:, first // 2 : last // 2],
-                in_=h_rows[s % H_RING][:, :, first:last].rearrange("p t (c i) -> p c t i", i=2),
+                out=h_words(s, cut, first, last).rearrange("p (c i t) -> p c t i", i=2, t=4),
+                in_=rows_of(s, first)[:, :, first:last].rearrange("p t (c i) -> p c t i", i=2),
             )
 
         def interleave_on_gpsimd(s, count):
             nc.gpsimd.tensor_scalar(
-                out=h_words[:, : 4 * count].rearrange("p (m t) -> p m t", t=4),
+                out=h_front[:, : 4 * count].rearrange("p (m t) -> p m t", t=4),
                 in0=h_rows[s % H_RING][:, :, :count].rearrange("p t m -> p m t"),
                 scalar1=1.0,
                 scalar2=0.0,
@@ -216,11 +225,11 @@ def tile_user_tower_for_scoring_h1_kernel(
                 op1=ALU.add,
             )
 
-        def quantize_hidden(s, first=0, last=512):
+        def quantize_hidden(s, cut, first, last):
             nc.vector.quantize_mx(
                 out=h_codes[s][:, first:last].bitcast(FP8X4),
                 scales=h_scales[s][:, first:last],
-                in_=h_words[:, 4 * first : 4 * last],
+                in_=h_words(s, cut, first, last),
             )
 
         def output_passes(j, first=0, last=FG):
@@ -251,9 +260,10 @@ def tile_user_tower_for_scoring_h1_kernel(
         def add_bias(j):
             nc.vector.tensor_tensor(out=y[j][:], in0=vectors[:, 0, :].bitcast(BF16), in1=y[j][:], op=ALU.add)
 
-        def weight_and_store(j):
-            nc.vector.tensor_tensor(out=y[j][:], in0=vectors[:, 1, :].bitcast(BF16), in1=y[j][:], op=ALU.mult)
-            nc.sync.dma_start(out=out_0[j * P : (j + 1) * P, :], in_=y[j][:])
+        def weight_and_store(j, into=None):
+            into = j if into is None else into
+            nc.vector.tensor_tensor(out=y[into][:], in0=vectors[:, 1, :].bitcast(BF16), in1=y[j][:], op=ALU.mult)
+            nc.sync.dma_start(out=out_0[j * P : (j + 1) * P, :], in_=y[into][:])
 
         def round_output(j, copy=nc.scalar.copy):
             copy(
@@ -356,11 +366,26 @@ def tile_user_tower_for_scoring_h1_kernel(
         deal_first_codes(1)
         quantize_pair(1, 1)
 
-        def products_behind(s):
-            return {5: [0], 6: [1], 7: [2], 8: [3], 9: [4], 10: [5, 6], 11: [7]}.get(s, [])
+        products = {5: [0], 6: [1], 7: [2], 8: [3], 9: [4], 10: [5, 6], 11: [7]}
+        W, C, Z = weight_and_store, add_free_and_bias, add_product
 
-        A, B, W, C, Z, E = add_product_to_free, add_bias, weight_and_store, add_free_and_bias, add_product, lambda pair: empty_users(pair, 1, nc.vector.tensor_copy)
-        window = {2: [(C, 0), (E, 3)], 4: [(C, 1), (C, 2)], 5: [(C, 3), (C, 4), (C, 5)], 6: [(Z, 0), (E, 5), (C, 6), (W, 0)], 7: [(Z, 1), (C, 7), (W, 1)], 8: [(Z, 2), (C, 8), (W, 2)], 9: [(Z, 3), (C, 9), (W, 3)], 10: [(Z, 4), (C, 10), (C, 11), (W, 4)], 11: [(Z, 5), (Z, 6), (W, 5), (W, 6)]}
+        def E(pair):
+            empty_users(pair, 1, nc.vector.tensor_copy)
+
+        def X(n):
+            quantize_chunk(n // KG, n % KG)
+
+        def Y(j):
+            quantize_and_store_codes(j, 4)
+            store_scales(j, 4, [nc.sync])
+
+        window = {2: [(E, 3), (C, 0), (C, 1)], 5: [(C, 2), (C, 3), (C, 4), (C, 5)], 6: [(Z, 0), (C, 6), (W, 0)], 7: [(Z, 1), (C, 7), (W, 1)], 8: [(Z, 2), (C, 8), (W, 2)], 9: [(Z, 3), (C, 9), (W, 3)], 10: [(Z, 4), (C, 10), (C, 11), (W, 4)], 11: [(Z, 5), (Z, 6), (W, 5), (W, 6)]}
+        between = {1: [(deal_codes, 3)], 3: [(sort_users, 5)], 6: [(X, 4), (X, 5)]}
+        after = {2: [(sort_users, 4)]}
+        by_scalar = {7: 80, 8: 80, 9: 80, 10: 64}
+
+        def cut_of(h):
+            return SHARE[len(window.get(h + 1, []))] or 256
 
         for s in range(SLOTS):
             if s == 0:
@@ -372,97 +397,80 @@ def tile_user_tower_for_scoring_h1_kernel(
                     sort_users(pair)
                 deal_codes(2)
             if s >= 1:
-                work = window.get(s, [])
-                share = SHARE[len(work)]
+                h = s - 1
+                share, cut, end = SHARE[len(window.get(s, []))], cut_of(h), 512 - by_scalar.get(h, 0)
                 if share:
-                    interleave_on_gpsimd(s - 1, share)
-                for step, j in work:
+                    interleave_on_gpsimd(h, share)
+                for step, j in window.get(s, []):
                     step(j)
-                interleave_hidden(s - 1, nc.vector.tensor_copy, share, 512)
-                between = s == 1
-                if s == 1:
-                    deal_codes(3)
-                for pair in {}.get(s, []):
+                for step, j in {2: [(X, 2), (X, 3)]}.get(s, []):
+                    step(j)
+                if not share:
+                    interleave_hidden(h, nc.vector.tensor_copy, cut, 0, cut)
+                if cut < end:
+                    interleave_hidden(h, nc.vector.tensor_copy, cut, cut, end)
+                for step, j in between.get(s, []):
+                    step(j)
+                quantize_hidden(h, cut, 0, cut)
+                if cut < 512:
+                    quantize_hidden(h, cut, cut, 512)
+                for step, j in after.get(s, []):
+                    step(j)
+
+            for first, last in ((0, 256), (256, 512)) if s == SLOTS - 1 else ((0, 512),):
+                for t in range(4):
                     for g in range(KG):
-                        quantize_pair(pair, g)
-                    between = True
-                for pair in {3: [5]}.get(s, []):
-                    sort_users(pair)
-                    between = True
-                for c, g in {2: [(1, 0), (1, 1)], 6: [(2, 0), (2, 1)]}.get(s, []):
-                    quantize_chunk(c, g)
-                    between = True
-                if s == SLOTS - 1:
-                    quantize_and_store_codes(0, 4)
-                    store_scales(0, 4, [nc.sync])
-                    between = True
-                if between and not share:
-                    quantize_hidden(s - 1)
-                else:
-                    cut = share if share in (128, 384) else 256
-                    quantize_hidden(s - 1, 0, cut)
-                    quantize_hidden(s - 1, cut, 512)
-                for step, j in {2: [(sort_users, 4)]}.get(s, []):
-                    step(j)
+                        if s > 0 or g > 0:
+                            hidden_pass(s, t, g, first, last)
+                    empty_hidden(s, t, first, last)
 
-            for t in range(4):
-                for g in range(KG):
-                    if s > 0 or g > 0:
-                        hidden_pass(s, t, g)
-                empty_hidden(s, t)
-
-            for j in {7: [0], 8: [1], 9: [2], 10: [3, 4], 11: [5]}.get(s, []):
+            for j in {7: [0], 8: [1], 9: [2], 10: [3, 4]}.get(s, []):
                 round_output(j)
+            if s in by_scalar:
+                interleave_hidden(s, nc.scalar.copy, cut_of(s), 512 - by_scalar[s], 512)
+            for pair, g in {1: [(2, 0), (3, 0), (2, 1), (3, 1)], 5: [(4, 0), (5, 0), (4, 1), (5, 1)]}.get(s, []):
+                turn_users(pair, g)
+                if g == 0 or pair not in (3,):
+                    empty_users(pair, g)
+            for j in products.get(s, []):
+                output_passes(j)
             if s == SLOTS - 2:
-                for j in products_behind(s):
-                    output_passes(j)
                 for j in (0, 2):
                     turn_output(j, 2)
                     empty_output(j, 2)
-            turned = {1: [2, 3], 5: [4, 5]}.get(s, [])
-            for g in range(KG):
-                for pair in turned:
-                    turn_users(pair, g)
-                    if g == 0 or pair not in (3, 5):
-                        empty_users(pair, g)
-            if s != SLOTS - 2:
-                for j in products_behind(s):
-                    output_passes(j)
 
         last = SLOTS - 1
-        interleave_hidden(last, nc.vector.tensor_copy, 0, 256)
-        interleave_hidden(last, nc.scalar.copy, 256, 512)
+        interleave_hidden(last, nc.vector.tensor_copy, 256, 0, 256)
+        Y(0)
+        quantize_hidden(last, 256, 0, 256)
+        round_output(5)
+        interleave_hidden(last, nc.scalar.copy, 256, 256, 512)
         round_output(6)
+        for j in (8, 9):
+            output_passes(j)
         add_product(7)
-        quantize_hidden(last, 0, 256)
         weight_and_store(7)
-        quantize_hidden(last, 256, 512)
+        add_product(8)
+        quantize_hidden(last, 256, 256, 512)
         round_output(7)
-        for j in (8, 9):
-            output_passes(j, 0, FG - 1)
-        for j in (8, 9):
-            output_passes(j, FG - 1)
         for j in (10, 11):
             output_passes(j)
-        for j in (4, 6):
+        weight_and_store(8)
+        round_output(8)
+        add_product(9)
+        add_product(10)
+        weight_and_store(9)
+        round_on_gpsimd(9)
+        for j in (4, 6, 8):
             turn_output(j, 2)
-        for j in (8, 9):
-            add_product(j)
-        for j in (8, 9):
-            weight_and_store(j)
-            round_output(j)
-        for j in (4, 6):
             empty_output(j, 2)
-        turn_output(8, 2)
-        for j in (10, 11):
-            add_product(j)
+        add_product(11)
         weight_and_store(10)
-        empty_output(8, 2)
-        weight_and_store(11)
-        for j in (10, 11):
-            round_output(j, nc.vector.tensor_copy)
+        weight_and_round(11)
+        round_on_gpsimd(10)
+        weight_and_store(11, 0)
         quantize_and_store_codes(4, 4)
-        for j in (10, 11):
+        for j in (11, 10):
             turn_output(j, 1)
             empty_output(j, 1)
         quantize_and_store_codes(8, 2)

@@ -193,12 +193,9 @@ def tile_user_tower_for_scoring_h1_kernel(
                 stop=(g == KG - 1),
             )
 
-        def rows_of(s, first):
-            return h_rows[(s + (s == SLOTS - 1 and first > 0)) % H_RING]
-
         def empty_hidden(s, t, first=0, last=512):
             nc.scalar.activation(
-                out=rows_of(s, first)[:, t, first:last],
+                out=h_rows[s % H_RING][:, t, first:last],
                 in_=held[("h", s, t, first)][:, : last - first],
                 func=ACT.Relu,
                 bias=b1_col[:, s % FG, t : t + 1],
@@ -212,7 +209,7 @@ def tile_user_tower_for_scoring_h1_kernel(
         def interleave_hidden(s, copy, cut, first, last):
             copy(
                 out=h_words(s, cut, first, last).rearrange("p (c i t) -> p c t i", i=2, t=4),
-                in_=rows_of(s, first)[:, :, first:last].rearrange("p t (c i) -> p c t i", i=2),
+                in_=h_rows[s % H_RING][:, :, first:last].rearrange("p t (c i) -> p c t i", i=2),
             )
 
         def interleave_on_gpsimd(s, count):
@@ -380,7 +377,7 @@ def tile_user_tower_for_scoring_h1_kernel(
             store_scales(j, 4, [nc.sync])
 
         window = {2: [(E, 3), (C, 0), (C, 1)], 5: [(C, 2), (C, 3), (C, 4), (C, 5)], 6: [(Z, 0), (C, 6), (W, 0)], 7: [(Z, 1), (C, 7), (W, 1)], 8: [(Z, 2), (C, 8), (W, 2)], 9: [(Z, 3), (C, 9), (W, 3)], 10: [(Z, 4), (C, 10), (C, 11), (W, 4)], 11: [(Z, 5), (Z, 6), (W, 5), (W, 6)]}
-        between = {1: [(deal_codes, 3)], 3: [(sort_users, 5)], 6: [(X, 4), (X, 5)]}
+        between = {1: [(deal_codes, 3)], 3: [(sort_users, 5)], 6: [(X, 4), (X, 5)], 11: [(Y, 0)]}
         after = {2: [(sort_users, 4)]}
         by_scalar = {7: 80, 8: 80, 9: 80, 10: 64}
 
@@ -417,14 +414,13 @@ def tile_user_tower_for_scoring_h1_kernel(
                 for step, j in after.get(s, []):
                     step(j)
 
-            for first, last in ((0, 256), (256, 512)) if s == SLOTS - 1 else ((0, 512),):
-                for t in range(4):
-                    for g in range(KG):
-                        if s > 0 or g > 0:
-                            hidden_pass(s, t, g, first, last)
-                    empty_hidden(s, t, first, last)
+            for t in range(4):
+                for g in range(KG):
+                    if s > 0 or g > 0:
+                        hidden_pass(s, t, g)
+                empty_hidden(s, t)
 
-            for j in {7: [0], 8: [1], 9: [2], 10: [3, 4]}.get(s, []):
+            for j in {7: [0], 8: [1], 9: [2], 10: [3, 4], 11: [5]}.get(s, []):
                 round_output(j)
             if s in by_scalar:
                 interleave_hidden(s, nc.scalar.copy, cut_of(s), 512 - by_scalar[s], 512)
@@ -441,36 +437,38 @@ def tile_user_tower_for_scoring_h1_kernel(
 
         last = SLOTS - 1
         interleave_hidden(last, nc.vector.tensor_copy, 256, 0, 256)
-        Y(0)
-        quantize_hidden(last, 256, 0, 256)
-        round_output(5)
         interleave_hidden(last, nc.scalar.copy, 256, 256, 512)
         round_output(6)
-        for j in (8, 9):
-            output_passes(j)
         add_product(7)
+        quantize_hidden(last, 256, 0, 256)
         weight_and_store(7)
-        add_product(8)
         quantize_hidden(last, 256, 256, 512)
         round_output(7)
+        for j in (8, 9):
+            output_passes(j, 0, FG - 1)
+        for j in (8, 9):
+            output_passes(j, FG - 1)
         for j in (10, 11):
             output_passes(j)
-        weight_and_store(8)
-        round_output(8)
-        add_product(9)
-        add_product(10)
-        weight_and_store(9)
-        round_on_gpsimd(9)
-        for j in (4, 6, 8):
+        for j in (4, 6):
             turn_output(j, 2)
+        for j in (8, 9):
+            add_product(j)
+        for j in (8, 9):
+            weight_and_store(j)
+            round_output(j)
+        for j in (4, 6):
             empty_output(j, 2)
-        add_product(11)
+        turn_output(8, 2)
+        for j in (10, 11):
+            add_product(j)
         weight_and_store(10)
-        weight_and_round(11)
-        round_on_gpsimd(10)
-        weight_and_store(11, 0)
+        empty_output(8, 2)
+        weight_and_store(11)
+        for j in (10, 11):
+            round_output(j, nc.vector.tensor_copy)
         quantize_and_store_codes(4, 4)
-        for j in (11, 10):
+        for j in (10, 11):
             turn_output(j, 1)
             empty_output(j, 1)
         quantize_and_store_codes(8, 2)

@@ -73,6 +73,7 @@ def tile_user_tower_for_scoring_h1_kernel(
         h_scales = tiles("h_scales", SLOTS, [P, 512], U8, 256)
         y = tiles("y", TILES, [P, D], F32)
         y_round = tiles("y_round", TILES, [P, D], BF16)
+        weight_row = tile("weight_row", [P, D], BF16)
         y_turned = tile("y_turned", [P, TILES * D], BF16)
         y_codes = tile("y_codes", [P, M], U32)
         y_scales = tile("y_scales", [P, M], U8)
@@ -262,6 +263,10 @@ def tile_user_tower_for_scoring_h1_kernel(
             nc.vector.tensor_tensor(out=y[into][:], in0=vectors[:, 1, :].bitcast(BF16), in1=y[j][:], op=ALU.mult)
             nc.sync.dma_start(out=out_0[j * P : (j + 1) * P, :], in_=y[into][:])
 
+        def weight_on_gpsimd(j):
+            nc.gpsimd.tensor_tensor(out=y[j][:], in0=y[j][:], in1=weight_row[:], op=ALU.mult)
+            nc.sync.dma_start(out=out_0[j * P : (j + 1) * P, :], in_=y[j][:])
+
         def round_output(j, copy=nc.scalar.copy):
             copy(
                 out=y_round[j][:].rearrange("p (u q e) -> p u q e", u=2, e=2),
@@ -353,6 +358,7 @@ def tile_user_tower_for_scoring_h1_kernel(
                     turn_bias()
                 if (pair, g) == (0, 1):
                     spread_vectors()
+                    nc.scalar.copy(out=weight_row[:], in_=vectors[:, 1, :].bitcast(BF16))
         deal_first_codes(0)
         quantize_pair(0, 0)
         deal_scales(0)
@@ -379,10 +385,11 @@ def tile_user_tower_for_scoring_h1_kernel(
         window = {2: [(E, 3), (C, 0), (C, 1)], 5: [(C, 2), (C, 3), (C, 4), (C, 5)], 6: [(Z, 0), (C, 6), (W, 0)], 7: [(Z, 1), (C, 7), (W, 1)], 8: [(Z, 2), (C, 8), (W, 2)], 9: [(Z, 3), (C, 9), (W, 3)], 10: [(Z, 4), (C, 10), (C, 11), (W, 4)], 11: [(Z, 5), (Z, 6), (W, 5), (W, 6)]}
         between = {1: [(deal_codes, 3)], 3: [(sort_users, 5)], 6: [(X, 4), (X, 5)], 11: [(Y, 0)]}
         after = {2: [(sort_users, 4)]}
-        by_scalar = {7: 80, 8: 80, 9: 80, 10: 64}
+        share_of = {2: 256, 5: 384, 6: 256, 7: 256, 8: 256, 9: 256, 10: 384, 11: 384}
+        by_scalar = {}
 
         def cut_of(h):
-            return SHARE[len(window.get(h + 1, []))] or 256
+            return share_of.get(h + 1) or 256
 
         for s in range(SLOTS):
             if s == 0:
@@ -395,7 +402,7 @@ def tile_user_tower_for_scoring_h1_kernel(
                 deal_codes(2)
             if s >= 1:
                 h = s - 1
-                share, cut, end = SHARE[len(window.get(s, []))], cut_of(h), 512 - by_scalar.get(h, 0)
+                share, cut, end = share_of.get(s, 0), cut_of(h), 512 - by_scalar.get(h, 0)
                 if share:
                     interleave_on_gpsimd(h, share)
                 for step, j in window.get(s, []):
@@ -437,7 +444,10 @@ def tile_user_tower_for_scoring_h1_kernel(
 
         last = SLOTS - 1
         interleave_hidden(last, nc.vector.tensor_copy, 256, 0, 256)
-        interleave_hidden(last, nc.scalar.copy, 256, 256, 512)
+        nc.scalar.copy(
+            out=h_words(last, 256, 256, 512).rearrange("p (m t) -> p m t", t=4),
+            in_=h_rows[last % H_RING][:, :, 256:512].rearrange("p t m -> p m t"),
+        )
         round_output(6)
         add_product(7)
         quantize_hidden(last, 256, 0, 256)
@@ -446,24 +456,26 @@ def tile_user_tower_for_scoring_h1_kernel(
         round_output(7)
         for j in (8, 9):
             output_passes(j, 0, FG - 1)
+        output_passes(10, 0, 1)
         for j in (8, 9):
             output_passes(j, FG - 1)
-        for j in (10, 11):
-            output_passes(j)
+        output_passes(10, 1)
+        output_passes(11)
         for j in (4, 6):
             turn_output(j, 2)
-        for j in (8, 9):
-            add_product(j)
-        for j in (8, 9):
-            weight_and_store(j)
-            round_output(j)
+        add_product(8)
+        weight_on_gpsimd(8)
+        add_product(9)
+        add_product(10)
+        weight_and_store(9)
+        round_output(8)
+        round_on_gpsimd(9)
         for j in (4, 6):
             empty_output(j, 2)
         turn_output(8, 2)
-        for j in (10, 11):
-            add_product(j)
-        weight_and_store(10)
         empty_output(8, 2)
+        add_product(11)
+        weight_and_store(10)
         weight_and_store(11)
         for j in (10, 11):
             round_output(j, nc.vector.tensor_copy)

@@ -194,9 +194,12 @@ def tile_user_tower_for_scoring_h1_kernel(
                 stop=(g == KG - 1),
             )
 
+        def rows_of(s, first):
+            return h_rows[(s + (s == SLOTS - 1 and first > 0)) % H_RING]
+
         def empty_hidden(s, t, first=0, last=512):
             nc.scalar.activation(
-                out=h_rows[s % H_RING][:, t, first:last],
+                out=rows_of(s, first)[:, t, first:last],
                 in_=held[("h", s, t, first)][:, : last - first],
                 func=ACT.Relu,
                 bias=b1_col[:, s % FG, t : t + 1],
@@ -210,7 +213,7 @@ def tile_user_tower_for_scoring_h1_kernel(
         def interleave_hidden(s, copy, cut, first, last):
             copy(
                 out=h_words(s, cut, first, last).rearrange("p (c i t) -> p c t i", i=2, t=4),
-                in_=h_rows[s % H_RING][:, :, first:last].rearrange("p t (c i) -> p c t i", i=2),
+                in_=rows_of(s, first)[:, :, first:last].rearrange("p t (c i) -> p c t i", i=2),
             )
 
         def interleave_on_gpsimd(s, count):
@@ -382,10 +385,10 @@ def tile_user_tower_for_scoring_h1_kernel(
             quantize_and_store_codes(j, 4)
             store_scales(j, 4, [nc.sync])
 
-        window = {2: [(E, 3), (C, 0), (C, 1)], 5: [(C, 2), (C, 3), (C, 4), (C, 5)], 6: [(Z, 0), (C, 6), (W, 0)], 7: [(Z, 1), (C, 7), (W, 1)], 8: [(Z, 2), (C, 8), (W, 2)], 9: [(Z, 3), (C, 9), (W, 3)], 10: [(Z, 4), (C, 10), (C, 11), (W, 4)], 11: [(Z, 5), (Z, 6), (W, 5), (W, 6)]}
+        window = {2: [(E, 2), (E, 3), (C, 0), (C, 1)], 5: [(C, 2), (C, 3), (C, 4), (C, 5)], 6: [(Z, 0), (C, 6), (W, 0)], 7: [(Z, 1), (C, 7), (W, 1)], 8: [(Z, 2), (C, 8), (W, 2)], 9: [(Z, 3), (C, 9), (W, 3)], 10: [(Z, 4), (C, 10), (C, 11), (W, 4)], 11: [(Z, 5), (Z, 6), (W, 5), (W, 6)]}
         between = {1: [(deal_codes, 3)], 3: [(sort_users, 5)], 6: [(X, 4), (X, 5)], 11: [(Y, 0)]}
         after = {2: [(sort_users, 4)]}
-        share_of = {2: 256, 5: 384, 6: 256, 7: 256, 8: 256, 9: 256, 10: 384, 11: 384}
+        share_of = {2: 384, 5: 384, 6: 256, 7: 256, 8: 256, 9: 256, 10: 384, 11: 384}
         by_scalar = {}
 
         def cut_of(h):
@@ -427,13 +430,13 @@ def tile_user_tower_for_scoring_h1_kernel(
                         hidden_pass(s, t, g)
                 empty_hidden(s, t)
 
-            for j in {7: [0], 8: [1], 9: [2], 10: [3, 4], 11: [5]}.get(s, []):
+            for j in {7: [0], 8: [1], 9: [2], 10: [3, 4]}.get(s, []):
                 round_output(j)
             if s in by_scalar:
                 interleave_hidden(s, nc.scalar.copy, cut_of(s), 512 - by_scalar[s], 512)
             for pair, g in {1: [(2, 0), (3, 0), (2, 1), (3, 1)], 5: [(4, 0), (5, 0), (4, 1), (5, 1)]}.get(s, []):
                 turn_users(pair, g)
-                if g == 0 or pair not in (3,):
+                if g == 0 or pair not in (2, 3):
                     empty_users(pair, g)
             for j in products.get(s, []):
                 output_passes(j)
@@ -448,6 +451,7 @@ def tile_user_tower_for_scoring_h1_kernel(
             out=h_words(last, 256, 256, 512).rearrange("p (m t) -> p m t", t=4),
             in_=h_rows[last % H_RING][:, :, 256:512].rearrange("p t m -> p m t"),
         )
+        round_output(5)
         round_output(6)
         add_product(7)
         quantize_hidden(last, 256, 0, 256)
@@ -468,10 +472,10 @@ def tile_user_tower_for_scoring_h1_kernel(
         add_product(9)
         add_product(10)
         weight_and_store(9)
-        round_output(8)
-        round_on_gpsimd(9)
-        for j in (4, 6):
-            empty_output(j, 2)
+        round_output(9)
+        round_on_gpsimd(8)
+        empty_output(4, 2)
+        empty_output(6, 2)
         turn_output(8, 2)
         empty_output(8, 2)
         add_product(11)

@@ -46,6 +46,9 @@ def tile_user_tower_for_scoring_h1_kernel(
         def tiles(name, count, shape, dtype, align=64):
             return [tile("%s%d" % (name, i), shape, dtype, align) for i in range(count)]
 
+        def shifted(name, count, width, dtype, skip):
+            return [t[:, skip:] for t in tiles(name, count, [P, skip + width], dtype, 256)]
+
         ident = tile("ident", [P, P], F32)
         b1_rows = tile("b1_rows", [P, 512], BF16)
         b1_col = tile("b1_col", [P, FG, 4], BF16)
@@ -55,22 +58,22 @@ def tile_user_tower_for_scoring_h1_kernel(
         w1_first = tiles("w1_first", KG, [P, 1024], U8)
         w1_second = tile("w1_second", [P, KG, 1024], U8)
         w1_last = tile("w1_last", [P, KG, 2048], U8)
-        w1_dealt = tiles("w1_dealt", FG, [P, KG, 1024], U8, 256)
+        w1_dealt = [t.rearrange("p (g n) -> p g n", g=KG) for t in shifted("w1_dealt", FG, KG * 1024, U8, 128)]
         s1_first = tile("s1_first", [P, KG, 512], U8)
         s1_rest = tile("s1_rest", [P, KG, 1536], U8)
-        s1_dealt = tiles("s1_dealt", FG, [P, KG, 512], U8, 256)
+        s1_dealt = [t.rearrange("p (g n) -> p g n", g=KG) for t in shifted("s1_dealt", FG, KG * 512, U8, 192)]
         u_sorted = tiles("u_sorted", 2, [P, 2 * K], BF16)
         w2 = tile("w2", [P, FG, 1024], U8, 256)
-        s2 = tile("s2", [P, FG, D], U8, 256)
+        s2 = shifted("s2", 1, FG * D, U8, 64)[0].rearrange("p (f n) -> p f n", f=FG)
         free = tiles("free", CHUNKS, [P, 4, D], BF16)
         x_turned = tiles("x_turned", X_RING, [P, 2048], BF16)
         x_codes = tiles("x_codes", CHUNKS * KG, [P, 512], U32, 256)
-        x_scales = tiles("x_scales", CHUNKS * KG, [P, 512], U8, 256)
+        x_scales = shifted("x_scales", CHUNKS * KG, 512, U8, 64)
         h_rows = tiles("h_rows", H_RING, [P, 4, ROW], BF16)
         h_front = tile("h_front", [P, 2048], BF16)
         h_back = tiles("h_back", 2, [P, 1536], BF16)
-        h_codes = tiles("h_codes", SLOTS, [P, 512], U32, 256)
-        h_scales = tiles("h_scales", SLOTS, [P, 512], U8, 256)
+        h_codes = shifted("h_codes", SLOTS, 512, U32, 32)
+        h_scales = shifted("h_scales", SLOTS, 512, U8, 192)
         y = tiles("y", TILES, [P, D], F32)
         y_round = tiles("y_round", TILES, [P, D], BF16)
         weight_row = tile("weight_row", [P, D], BF16)

@@ -271,7 +271,6 @@ def tile_user_tower_for_scoring_h1_kernel(
 
         def weight_on_gpsimd(j):
             nc.gpsimd.tensor_tensor(out=y[j][:], in0=y[j][:], in1=weight_row[:], op=ALU.mult)
-            nc.sync.dma_start(out=out_0[j * P : (j + 1) * P, :], in_=y[j][:])
 
         def round_output(j, copy=nc.scalar.copy):
             copy(
@@ -475,12 +474,14 @@ def tile_user_tower_for_scoring_h1_kernel(
         add_product(9)
         add_product(10)
         weight_and_store(9)
+        nc.sync.dma_start(out=out_0[8 * P : 9 * P, :], in_=y[8][:])
         round_output(9)
         round_on_gpsimd(8)
         empty_output(4, 2)
         empty_output(6, 2)
-        turn_output(8, 2)
-        empty_output(8, 2)
+        for j in (9, 8):
+            turn_output(j, 1)
+            empty_output(j, 1)
         add_product(11)
         weight_and_store(10)
         weight_and_store(11)

@@ -58,21 +58,21 @@ def tile_user_tower_for_scoring_h1_kernel(
         w1_first = tiles("w1_first", KG, [P, 1024], U8)
         w1_second = tile("w1_second", [P, KG, 1024], U8)
         w1_last = tile("w1_last", [P, KG, 2048], U8)
-        w1_dealt = [t.rearrange("p (g n) -> p g n", g=KG) for t in shifted("w1_dealt", FG, KG * 1024, U8, 128)]
+        w1_dealt = [t.rearrange("p (g n) -> p g n", g=KG) for t in shifted("w1_dealt", FG, KG * 1024, U8, 64)]
         s1_first = tile("s1_first", [P, KG, 512], U8)
         s1_rest = tile("s1_rest", [P, KG, 1536], U8)
         s1_dealt = [t.rearrange("p (g n) -> p g n", g=KG) for t in shifted("s1_dealt", FG, KG * 512, U8, 192)]
         u_sorted = tiles("u_sorted", 2, [P, 2 * K], BF16)
         w2 = tile("w2", [P, FG, 1024], U8, 256)
-        s2 = shifted("s2", 1, FG * D, U8, 64)[0].rearrange("p (f n) -> p f n", f=FG)
+        s2 = shifted("s2", 1, FG * D, U8, 128)[0].rearrange("p (f n) -> p f n", f=FG)
         free = tiles("free", CHUNKS, [P, 4, D], BF16)
         x_turned = tiles("x_turned", X_RING, [P, 2048], BF16)
         x_codes = tiles("x_codes", CHUNKS * KG, [P, 512], U32, 256)
-        x_scales = shifted("x_scales", CHUNKS * KG, 512, U8, 64)
+        x_scales = shifted("x_scales", CHUNKS * KG, 512, U8, 128)
         h_rows = tiles("h_rows", H_RING, [P, 4, ROW], BF16)
         h_front = tile("h_front", [P, 2048], BF16)
         h_back = tiles("h_back", 2, [P, 1536], BF16)
-        h_codes = shifted("h_codes", SLOTS, 512, U32, 32)
+        h_codes = shifted("h_codes", SLOTS, 512, U32, 16)
         h_scales = shifted("h_scales", SLOTS, 512, U8, 192)
         y = tiles("y", TILES, [P, D], F32)
         y_round = tiles("y_round", TILES, [P, D], BF16)

from contextlib import ExitStack

import concourse.mybir as mybir
from concourse.masks import make_identity

M, K, F, D = 1536, 1024, 2048, 512
FLOPS = 2 * M * (K * F + F * D)

F32 = mybir.dt.float32
BF16 = mybir.dt.bfloat16
I32 = mybir.dt.int32
U32 = mybir.dt.uint32
U16 = mybir.dt.uint16
U8 = mybir.dt.uint8
FP8X4 = mybir.dt.float8_e4m3fn_x4
FP4X4 = mybir.dt.float4_e2m1fn_x4
ACT = mybir.ActivationFunctionType
ALU = mybir.AluOpType

P = 128
KG = K // 512
FG = F // 512
CHUNKS = M // 512
TILES = M // P
PAIRS = TILES // 2
SLOTS = CHUNKS * FG
RING = 7
ROW = 520
H_RING = 3
X_RING = 4
SHARE = {0: 0, 1: 0, 2: 128, 3: 256, 4: 384, 5: 512}


def tile_user_tower_for_scoring_h1_kernel(
    tc, users, w1_words, w1_scales, b1, w2_words, w2_scales, b2, user_free, dim_weight, out_0, out_1, out_2
):
    nc = tc.nc
    with ExitStack() as ctx:
        sb = ctx.enter_context(tc.tile_pool(name="sb", bufs=1))
        ps = ctx.enter_context(tc.psum_pool(name="ps", bufs=1))
        ctx.enter_context(tc.manual_schedule())

        def tile(name, shape, dtype, align=64):
            return sb.tile(shape, dtype, name=name, align_bytes=align)

        def tiles(name, count, shape, dtype, align=64):
            return [tile("%s%d" % (name, i), shape, dtype, align) for i in range(count)]

        def shifted(name, count, width, dtype, skip):
            return [t[:, skip:] for t in tiles(name, count, [P, skip + width], dtype, 256)]

        ident = tile("ident", [P, P], F32)
        b1_rows = tile("b1_rows", [P, 512], BF16)
        b1_col = tile("b1_col", [P, FG, 4], BF16)
        vector_cols = tiles("vector_col", 2, [P, 4], BF16)
        u_head = tiles("u_head", 2 * KG, [P, 2, 512], BF16)
        u_rest = tiles("u_rest", PAIRS - 2, [P, 2, K], BF16)
        w1_first = tiles("w1_first", KG, [P, 1024], U8)
        w1_second = tile("w1_second", [P, KG, 1024], U8)
        w1_last = tile("w1_last", [P, KG, 2048], U8)
        w1_dealt = [t.rearrange("p (g n) -> p g n", g=KG) for t in shifted("w1_dealt", FG, KG * 1024, U8, 64)]
        s1_first = tile("s1_first", [P, KG, 512], U8)
        s1_rest = tile("s1_rest", [P, KG, 1536], U8)
        s1_dealt = [t.rearrange("p (g n) -> p g n", g=KG) for t in shifted("s1_dealt", FG, KG * 512, U8, 192)]
        u_sorted = tiles("u_sorted", 2, [P, 2 * K], BF16)
        w2 = tile("w2", [P, FG, 1024], U8, 256)
        s2 = shifted("s2", 1, FG * D, U8, 128)[0].rearrange("p (f n) -> p f n", f=FG)
        free = tiles("free", CHUNKS, [P, 4, D], BF16)
        x_turned = tiles("x_turned", X_RING, [P, 2048], BF16)
        x_codes = tiles("x_codes", CHUNKS * KG, [P, 512], U32, 256)
        x_scales = shifted("x_scales", CHUNKS * KG, 512, U8, 128)
        h_rows = tiles("h_rows", H_RING, [P, 4, ROW], BF16)
        h_front = tile("h_front", [P, 2048], BF16)
        h_back = tiles("h_back", 2, [P, 1536], BF16)
        h_codes = shifted("h_codes", SLOTS, 512, U32, 16)
        h_scales = shifted("h_scales", SLOTS, 512, U8, 192)
        y = tiles("y", TILES, [P, D], F32)
        y_round = tiles("y_round", TILES, [P, D], BF16)
        weight_row = tile("weight_row", [P, D], BF16)
        y_turned = tile("y_turned", [P, TILES * D], BF16)
        y_codes = tile("y_codes", [P, M], U32)
        y_scales = tile("y_scales", [P, M], U8)
        banks = [ps.tile([P, 512], F32, name="bank%d" % i) for i in range(RING)]
        vectors = ps.tile([P, 2, 256], F32, name="vectors")

        held = {}

        def take_bank(key):
            held[key] = banks[len(held) % RING]
            return held[key]

        def load_head(pair, g):
            src = users[pair * 256 : (pair + 1) * 256, g * 512 : (g + 1) * 512].rearrange("(i p) k -> p i k", p=P)
            nc.sync.dma_start(out=u_head[pair * KG + g][:], in_=src)

        def load_pair(pair):
            src = users[pair * 256 : (pair + 1) * 256, :].rearrange("(i p) k -> p i k", p=P)
            nc.sync.dma_start(out=u_rest[pair - 2][:], in_=src)

        def load_w1_first(g):
            nc.sync.dma_start(out=w1_first[g][:].bitcast(I32), in_=w1_words[g, :, :1024].bitcast(I32))

        def load_w1(dst, first, last):
            src = w1_words[:, :, first * 1024 : last * 1024].rearrange("g p n -> p g n")
            nc.sync.dma_start(out=dst[:].bitcast(I32), in_=src.bitcast(I32))

        def load_scale_rows(dst, src):
            for q in range(4):
                rows = src[:, q:16:4, :].rearrange("g r n -> r g n")
                nc.sync.dma_start(out=dst[q:P:32, :, :].bitcast(I32), in_=rows.bitcast(I32))

        def load_free(c):
            nc.sync.dma_start(out=free[c][:], in_=user_free[c * 512 : (c + 1) * 512, :].rearrange("(i p) d -> p i d", p=P))

        def spread_vectors():
            for v in range(2):
                for u in range(2):
                    column = vector_cols[v][:].bitcast(F32)[:, u : u + 1].to_broadcast([P, P])
                    nc.tensor.transpose(vectors[:, v, u:256:2], column, ident[:])

        def user_words(pair, g):
            return u_head[pair * KG + g][:].bitcast(F32)

        def sort_users(pair):
            nc.vector.tensor_copy(
                out=u_sorted[pair % 2][:].bitcast(F32).rearrange("p (r u q) -> p r u q", u=2, q=P),
                in_=u_rest[pair - 2][:].bitcast(F32).rearrange("p i (g q u) -> p (i g) u q", u=2, q=P),
            )

        def turn_users(pair, g):
            bank = take_bank(("u", pair, g))
            for i in range(2):
                for u in range(2):
                    at = (2 * i + u) * P
                    if pair < 2:
                        words = user_words(pair, g)[:, i, u:256:2]
                    else:
                        first = ((i * KG + g) * 2 + u) * P
                        words = u_sorted[pair % 2][:].bitcast(F32)[:, first : first + P]
                    nc.tensor.transpose(bank[:, at : at + P], words, ident[:])

        def x_home(pair, g):
            return x_turned[(pair // 2 * KG + g) % X_RING][:, pair % 2 * 1024 : (pair % 2 + 1) * 1024]

        def empty_users(pair, g, copy=nc.scalar.copy):
            copy(
                out=x_home(pair, g).bitcast(F32).rearrange("p (i m u) -> p i m u", i=2, u=2),
                in_=held[("u", pair, g)][:].rearrange("p (i u m) -> p i m u", i=2, u=2),
            )

        def quantize_pair(pair, g):
            c, half = divmod(pair, 2)
            cols = slice(half * 256, (half + 1) * 256)
            nc.vector.quantize_mx(
                out=x_codes[c * KG + g][:, cols].bitcast(FP8X4), scales=x_scales[c * KG + g][:, cols], in_=x_home(pair, g)
            )

        def quantize_chunk(c, g):
            n = c * KG + g
            nc.vector.quantize_mx(out=x_codes[n][:].bitcast(FP8X4), scales=x_scales[n][:], in_=x_turned[n % X_RING][:])

        def deal_first_codes(g):
            nc.vector.tensor_copy(
                out=w1_dealt[0][:, g, :].bitcast(U16).rearrange("p (t m) -> p t m", t=4),
                in_=w1_first[g][:].bitcast(U16).rearrange("p (m t) -> p t m", t=4),
            )

        def deal_scales(fg):
            src = s1_first[:] if fg == 0 else s1_rest[:, :, (fg - 1) * 512 : fg * 512]
            nc.vector.tensor_copy(
                out=s1_dealt[fg][:].rearrange("p g (t m) -> p g t m", t=4), in_=src.rearrange("p g (m t) -> p g t m", t=4)
            )

        def deal_codes(fg, copy=nc.vector.tensor_copy):
            src = w1_second[:] if fg == 1 else w1_last[:, :, (fg - 2) * 1024 : (fg - 1) * 1024]
            copy(
                out=w1_dealt[fg][:].bitcast(U16).rearrange("p g (t m) -> p g t m", t=4),
                in_=src.bitcast(U16).rearrange("p g (m t) -> p g t m", t=4),
            )

        def turn_bias():
            bank = take_bank(("b",))
            for u in range(2):
                nc.tensor.transpose(bank[:, u * P : (u + 1) * P], b1_rows[:].bitcast(F32)[:, u:256:2], ident[:])
            nc.scalar.copy(out=b1_col[:].bitcast(F32), in_=bank[:, :256].rearrange("p (u r) -> p r u", u=2)[:, :FG, :])

        def hidden_pass(s, t, g, first=0, last=512):
            c, fg = divmod(s, FG)
            bank = take_bank(("h", s, t, first)) if g == 0 else held[("h", s, t, first)]
            nc.tensor.matmul_mx(
                out=bank[:, : last - first],
                lhsT=w1_dealt[fg][:, g, t * 256 : (t + 1) * 256].bitcast(FP4X4),
                lhsT_scale=s1_dealt[fg][:, g, t * P : (t + 1) * P],
                rhs=x_codes[c * KG + g][:, first:last].bitcast(FP8X4),
                rhs_scale=x_scales[c * KG + g][:, first:last],
                start=(g == 0),
                stop=(g == KG - 1),
            )

        def rows_of(s, first):
            return h_rows[(s + (s == SLOTS - 1 and first > 0)) % H_RING]

        def empty_hidden(s, t, first=0, last=512):
            nc.scalar.activation(
                out=rows_of(s, first)[:, t, first:last],
                in_=held[("h", s, t, first)][:, : last - first],
                func=ACT.Relu,
                bias=b1_col[:, s % FG, t : t + 1],
            )

        def h_words(s, cut, first, last):
            if first < cut:
                return h_front[:, 4 * first : 4 * last]
            return h_back[s % 2][:, 4 * (first - cut) : 4 * (last - cut)]

        def interleave_hidden(s, copy, cut, first, last):
            copy(
                out=h_words(s, cut, first, last).rearrange("p (c i t) -> p c t i", i=2, t=4),
                in_=rows_of(s, first)[:, :, first:last].rearrange("p t (c i) -> p c t i", i=2),
            )

        def interleave_on_gpsimd(s, count):
            nc.gpsimd.tensor_scalar(
                out=h_front[:, : 4 * count].rearrange("p (m t) -> p m t", t=4),
                in0=h_rows[s % H_RING][:, :, :count].rearrange("p t m -> p m t"),
                scalar1=1.0,
                scalar2=0.0,
                op0=ALU.mult,
                op1=ALU.add,
            )

        def quantize_hidden(s, cut, first, last):
            nc.vector.quantize_mx(
                out=h_codes[s][:, first:last].bitcast(FP8X4),
                scales=h_scales[s][:, first:last],
                in_=h_words(s, cut, first, last),
            )

        def output_passes(j, first=0, last=FG):
            c, i = divmod(j, 4)
            for fg in range(first, last):
                bank = take_bank(("z", j)) if fg == 0 else held[("z", j)]
                nc.tensor.matmul_mx(
                    out=bank[:],
                    lhsT=h_codes[c * FG + fg][:, i * P : (i + 1) * P].bitcast(FP8X4),
                    lhsT_scale=h_scales[c * FG + fg][:, i * P : (i + 1) * P],
                    rhs=w2[:, fg, :].bitcast(FP4X4),
                    rhs_scale=s2[:, fg, :],
                    start=(fg == 0),
                    stop=(fg == FG - 1),
                )

        def add_free_and_bias(j):
            c, i = divmod(j, 4)
            nc.vector.tensor_tensor(out=y[j][:], in0=vectors[:, 0, :].bitcast(BF16), in1=free[c][:, i, :], op=ALU.add)

        def add_product(j):
            nc.vector.tensor_tensor(out=y[j][:], in0=held[("z", j)][:], in1=y[j][:], op=ALU.add)

        def add_product_to_free(j):
            c, i = divmod(j, 4)
            nc.vector.tensor_tensor(out=y[j][:], in0=held[("z", j)][:], in1=free[c][:, i, :], op=ALU.add)

        def add_bias(j):
            nc.vector.tensor_tensor(out=y[j][:], in0=vectors[:, 0, :].bitcast(BF16), in1=y[j][:], op=ALU.add)

        def weight_and_store(j, into=None):
            into = j if into is None else into
            nc.vector.tensor_tensor(out=y[into][:], in0=vectors[:, 1, :].bitcast(BF16), in1=y[j][:], op=ALU.mult)
            nc.sync.dma_start(out=out_0[j * P : (j + 1) * P, :], in_=y[into][:])

        def weight_on_gpsimd(j):
            nc.gpsimd.tensor_tensor(out=y[j][:], in0=y[j][:], in1=weight_row[:], op=ALU.mult)

        def round_output(j, copy=nc.scalar.copy):
            copy(
                out=y_round[j][:].rearrange("p (u q e) -> p u q e", u=2, e=2),
                in_=y[j][:].rearrange("p (q u e) -> p u q e", u=2, e=2),
            )

        def weight_and_round(j):
            nc.vector.tensor_tensor(
                out=y_round[j][:].rearrange("p (u q e) -> p u q e", u=2, e=2),
                in0=vectors[:, 1, :].bitcast(BF16).rearrange("p (q u e) -> p u q e", u=2, e=2),
                in1=y[j][:].rearrange("p (q u e) -> p u q e", u=2, e=2),
                op=ALU.mult,
            )

        def round_on_gpsimd(j):
            nc.gpsimd.tensor_scalar(
                out=y_round[j][:].rearrange("p (u q e) -> p u q e", u=2, e=2),
                in0=y[j][:].rearrange("p (q u e) -> p u q e", u=2, e=2),
                scalar1=1.0,
                scalar2=0.0,
                op0=ALU.mult,
                op1=ALU.add,
            )

        def turn_output(j, count):
            bank = take_bank(("y", j))
            for i in range(count):
                words = y_round[j + i][:].bitcast(F32)
                for u in range(2):
                    at = (2 * i + u) * P
                    nc.tensor.transpose(bank[:, at : at + P], words[:, u * P : (u + 1) * P], ident[:])

        def empty_output(j, count):
            nc.scalar.copy(
                out=y_turned[:, j * D : (j + count) * D].bitcast(F32).rearrange("p (i m u) -> p i m u", i=count, u=2),
                in_=held[("y", j)][:, : count * 256].rearrange("p (i u m) -> p i m u", i=count, u=2),
            )

        def quantize_and_store_codes(j, count):
            cols = slice(j * P, (j + count) * P)
            nc.vector.quantize_mx(
                out=y_codes[:, cols].bitcast(FP8X4), scales=y_scales[:, cols], in_=y_turned[:, j * D : (j + count) * D]
            )
            dst = out_1[0].rearrange("p m t -> p (m t)")[:, 4 * j * P : 4 * (j + count) * P]
            nc.sync.dma_start(out=dst.bitcast(I32), in_=y_codes[:, cols].bitcast(I32))

        def store_scales(j, count, queues):
            cols = slice(j * P, (j + count) * P)
            for q in range(4):
                queues[q % len(queues)].dma_start(
                    out=out_2[0][q:16:4, cols].bitcast(I32), in_=y_scales[q:P:32, cols].bitcast(I32)
                )

        nc.vector.memset(b1_rows[:], 0.0)
        nc.vector.memset(s1_first[:].bitcast(I32), 0)
        nc.vector.memset(ident[:], 0.0)
        make_identity(nc, ident[:], nomemset=True)
        for scales in (s1_rest, s2):
            nc.vector.memset(scales[:].bitcast(I32), 0)

        for v, vector in enumerate((b2, dim_weight)):
            nc.scalar.dma_start(out=vector_cols[v][:], in_=vector.rearrange("(p e) -> p e", e=4))
        for g in range(KG):
            load_head(0, g)
            if g == 0:
                nc.sync.dma_start(out=b1_rows[:FG, :], in_=b1.rearrange("(g n) -> g n", g=FG))
            if g == 1:
                load_scale_rows(s1_first, w1_scales[:, :, :512])
            load_head(1, g)
            load_w1_first(g)
        load_w1(w1_second, 1, 2)
        load_scale_rows(s1_rest, w1_scales[:, :, 512:])
        load_pair(2)
        load_pair(3)
        load_w1(w1_last, 2, 4)
        load_free(0)
        load_pair(4)
        load_pair(5)
        load_free(1)
        nc.sync.dma_start(out=w2[:].bitcast(I32), in_=w2_words.rearrange("g p n -> p g n").bitcast(I32))
        load_scale_rows(s2, w2_scales)
        load_free(2)

        for g in range(KG):
            for pair in range(2):
                turn_users(pair, g)
                empty_users(pair, g)
                if (pair, g) == (1, 0):
                    turn_bias()
                if (pair, g) == (0, 1):
                    spread_vectors()
                    nc.scalar.copy(out=weight_row[:], in_=vectors[:, 1, :].bitcast(BF16))
        deal_first_codes(0)
        quantize_pair(0, 0)
        deal_scales(0)
        quantize_pair(1, 0)
        for t in range(4):
            hidden_pass(0, t, 0)
        quantize_pair(0, 1)
        deal_first_codes(1)
        quantize_pair(1, 1)

        products = {5: [0], 6: [1], 7: [2], 8: [3], 9: [4], 10: [5, 6], 11: [7]}
        W, C, Z = weight_and_store, add_free_and_bias, add_product

        def E(pair):
            empty_users(pair, 1, nc.vector.tensor_copy)

        def X(n):
            quantize_chunk(n // KG, n % KG)

        def Y(j):
            quantize_and_store_codes(j, 4)
            store_scales(j, 4, [nc.sync])

        window = {2: [(E, 2), (E, 3), (C, 0), (C, 1)], 5: [(C, 2), (C, 3), (C, 4), (C, 5)], 6: [(Z, 0), (C, 6), (W, 0)], 7: [(Z, 1), (C, 7), (W, 1)], 8: [(Z, 2), (C, 8), (W, 2)], 9: [(Z, 3), (C, 9), (W, 3)], 10: [(Z, 4), (C, 10), (C, 11), (W, 4)], 11: [(Z, 5), (Z, 6), (W, 5), (W, 6)]}
        between = {1: [(deal_codes, 3)], 3: [(sort_users, 5)], 6: [(X, 4), (X, 5)], 11: [(Y, 0)]}
        after = {2: [(sort_users, 4)]}
        share_of = {2: 384, 5: 384, 6: 256, 7: 256, 8: 256, 9: 256, 10: 384, 11: 384}
        by_scalar = {}

        def cut_of(h):
            return share_of.get(h + 1) or 256

        for s in range(SLOTS):
            if s == 0:
                deal_codes(1, nc.scalar.copy)
                deal_scales(1)
                deal_scales(2)
                deal_scales(3)
                for pair in (2, 3):
                    sort_users(pair)
                deal_codes(2)
            if s >= 1:
                h = s - 1
                share, cut, end = share_of.get(s, 0), cut_of(h), 512 - by_scalar.get(h, 0)
                if share:
                    interleave_on_gpsimd(h, share)
                for step, j in window.get(s, []):
                    step(j)
                for step, j in {2: [(X, 2), (X, 3)]}.get(s, []):
                    step(j)
                if not share:
                    interleave_hidden(h, nc.vector.tensor_copy, cut, 0, cut)
                if cut < end:
                    interleave_hidden(h, nc.vector.tensor_copy, cut, cut, end)
                for step, j in between.get(s, []):
                    step(j)
                quantize_hidden(h, cut, 0, cut)
                if cut < 512:
                    quantize_hidden(h, cut, cut, 512)
                for step, j in after.get(s, []):
                    step(j)

            for t in range(4):
                for g in range(KG):
                    if s > 0 or g > 0:
                        hidden_pass(s, t, g)
                empty_hidden(s, t)

            for j in {7: [0], 8: [1], 9: [2], 10: [3, 4]}.get(s, []):
                round_output(j)
            if s in by_scalar:
                interleave_hidden(s, nc.scalar.copy, cut_of(s), 512 - by_scalar[s], 512)
            for pair, g in {1: [(2, 0), (3, 0), (2, 1), (3, 1)], 5: [(4, 0), (5, 0), (4, 1), (5, 1)]}.get(s, []):
                turn_users(pair, g)
                if g == 0 or pair not in (2, 3):
                    empty_users(pair, g)
            for j in products.get(s, []):
                output_passes(j)
            if s == SLOTS - 2:
                for j in (0, 2):
                    turn_output(j, 2)
                    empty_output(j, 2)

        last = SLOTS - 1
        interleave_hidden(last, nc.vector.tensor_copy, 256, 0, 256)
        nc.scalar.copy(
            out=h_words(last, 256, 256, 512).rearrange("p (m t) -> p m t", t=4),
            in_=h_rows[last % H_RING][:, :, 256:512].rearrange("p t m -> p m t"),
        )
        round_output(5)
        round_output(6)
        add_product(7)
        quantize_hidden(last, 256, 0, 256)
        weight_and_store(7)
        quantize_hidden(last, 256, 256, 512)
        round_output(7)
        for j in (8, 9):
            output_passes(j, 0, FG - 1)
        output_passes(10, 0, 1)
        for j in (8, 9):
            output_passes(j, FG - 1)
        output_passes(10, 1)
        output_passes(11)
        for j in (4, 6):
            turn_output(j, 2)
        add_product(8)
        weight_on_gpsimd(8)
        add_product(9)
        add_product(10)
        weight_and_store(9)
        nc.sync.dma_start(out=out_0[8 * P : 9 * P, :], in_=y[8][:])
        round_output(9)
        round_on_gpsimd(8)
        empty_output(4, 2)
        empty_output(6, 2)
        for j in (9, 8):
            turn_output(j, 1)
            empty_output(j, 1)
        add_product(11)
        weight_and_store(10)
        weight_and_store(11)
        for j in (10, 11):
            round_output(j, nc.vector.tensor_copy)
        quantize_and_store_codes(4, 4)
        for j in (10, 11):
            turn_output(j, 1)
            empty_output(j, 1)
        quantize_and_store_codes(8, 2)
        quantize_and_store_codes(10, 2)
        store_scales(4, 8, [nc.sync, nc.scalar])
